import numpy as np
import ml_dtypes


def mxq(x, axis, fmt="e4m3"):
    dtype, down = {"e4m3": (ml_dtypes.float8_e4m3fn, 7), "e5m2": (ml_dtypes.float8_e5m2, 14)}[fmt]
    v = np.moveaxis(np.asarray(x, np.float32).astype(ml_dtypes.bfloat16).astype(np.float64), axis, -1)
    blocks = v.reshape(v.shape[:-1] + (-1, 32))
    amax = np.abs(blocks).max(-1, keepdims=True)
    byte = np.maximum(np.where(amax > 0, np.frexp(amax)[1] - 1 + 127, 0) - down, 1)
    scale = np.exp2(byte - 127.0)
    codes = (blocks / scale).astype(np.float32).astype(dtype).astype(np.float64)
    return np.moveaxis((codes * scale).reshape(v.shape), -1, axis)


WIDE = False


def mx_kscale(k):
    if not WIDE:
        return np.ones(k)
    levels = np.array([10, -10, 5, -5, 0])
    if k % 512:
        return np.exp2(np.random.permutation(np.resize(levels, k // 32))).repeat(32)
    a = np.empty((k // 512, 16))
    for p in range(k // 512):
        a[p, :8] = np.random.permutation(np.resize(levels, 8))
        for g in range(8):
            far = levels[np.abs(levels - a[p, g]) >= 10]
            a[p, g + 8] = far[np.random.randint(len(far))]
    return np.exp2(a.ravel()).repeat(32)


def f64(x):
    return np.asarray(x).astype(np.float64)


def striped(idx):
    return np.tile(idx.reshape(-1, 16).T, (8, 1)).astype(np.uint16)


def unstriped(offs):
    return offs[:16].T.reshape(-1).astype(np.int64)


E2M1 = np.array([0.0, 0.5, 1.0, 1.5, 2.0, 3.0, 4.0, 6.0, -0.0, -0.5, -1.0, -1.5, -2.0, -3.0, -4.0, -6.0])


def pack_weight(w, fmt):
    k, n = w.shape
    w = f64(np.asarray(w, np.float32).astype(ml_dtypes.bfloat16)).reshape(k // 32, 32, n)
    amax = np.abs(w).max(1)
    if fmt == "e4m3":
        byte = np.frexp(amax)[1] - 1 + 127 - 7
    else:
        mant, ex = np.frexp(amax / 6.0)
        byte = np.where(mant > 0.5, ex, ex - 1) + 127
    byte = np.clip(np.where(amax > 0, byte, 1), 1, 254)
    scaled = (w * np.exp2(127.0 - byte)[:, None, :]).reshape(k, n).astype(np.float32)
    by_word = np.ascontiguousarray(scaled.reshape(k // 512, 128, 4, n).transpose(0, 1, 3, 2))
    if fmt == "e4m3":
        words = by_word.astype(ml_dtypes.float8_e4m3fn).view(np.uint8)
    else:
        c = by_word.astype(ml_dtypes.float4_e2m1fn).view(np.uint8) & 0xF
        words = (c[..., 0::2] | (c[..., 1::2] << 4)).reshape(k // 512, 128, 2 * n)
    return np.ascontiguousarray(words), np.ascontiguousarray(byte.astype(np.uint8).reshape(k // 512, 16, n))


def unpack_weight(words, scales, fmt):
    g, _, n = scales.shape
    words = np.ascontiguousarray(words).reshape(g, 128, n, -1)
    if fmt == "e4m3":
        vals = words.view(ml_dtypes.float8_e4m3fn).astype(np.float64)
    else:
        nib = np.empty((g, 128, n, 4), np.uint8)
        nib[..., 0::2] = words & 0xF
        nib[..., 1::2] = words >> 4
        vals = E2M1[nib]
    vals = vals * np.repeat(np.exp2(scales.astype(np.float64) - 127.0), 8, axis=1)[..., None]
    return vals.transpose(0, 1, 3, 2).reshape(g * 512, n)


def gelu(v):
    return 0.5 * v * (1.0 + np.tanh(np.sqrt(2.0 / np.pi) * (v + 0.044715 * v**3)))


K, T, S, H, N = 1024, 4096, 1024, 512, 1536

def setup_inputs():
    n = np.random.standard_normal
    s = mx_kscale(K)[:, None]
    u = mx_kscale(H)[:, None]
    tab_words, tab_scales = pack_weight(n((K, T)) * s, "e4m3")
    w2_words, w2_scales = pack_weight(n((K, H)) * 0.7 / np.sqrt(K) / s, "e4m3")
    w3_words, w3_scales = pack_weight(n((K, H)) * 0.7 / np.sqrt(K) / s, "e2m1")
    return {
        "tab_words": tab_words, "tab_scales": tab_scales,
        "offs": striped(np.random.permutation(T)[:S]),
        "offs2": striped(np.random.permutation(T)[:S]),
        "offs3": striped(np.random.permutation(T)[:S]),
        "w1": (n((K, H)) * 0.7 / np.sqrt(K) / s).astype(np.float32),
        "w2_words": w2_words, "w2_scales": w2_scales,
        "w3_words": w3_words, "w3_scales": w3_scales,
        "bh": (0.3 * n(H)).astype(np.float32),
        "gain": (np.exp(0.3 * n(H)) * u[:, 0]).astype(np.float32),
        "wo": (2.0 * n((H, N)) / np.sqrt(H) / u).astype(np.float32),
        "bo": (0.5 * n(N)).astype(np.float32),
    }

def reference(tab_words, tab_scales, offs, offs2, offs3, w1, w2_words, w2_scales, w3_words, w3_scales, bh, gain, wo, bo):
    x1 = unpack_weight(tab_words, tab_scales, "e4m3")[:, unstriped(offs)]
    x2 = unpack_weight(tab_words, tab_scales, "e4m3")[:, unstriped(offs2)]
    x3 = unpack_weight(tab_words, tab_scales, "e4m3")[:, unstriped(offs3)]
    w2 = unpack_weight(w2_words, w2_scales, "e4m3")
    w3 = unpack_weight(w3_words, w3_scales, "e2m1")
    a = mxq(f64(w1), 0, "e4m3").T @ x1 + w2.T @ x2 + w3.T @ x3
    h = np.tanh(a + f64(bh)[:, None]) * f64(gain)[:, None]
    y = mxq(f64(wo), 0, "e4m3").T @ mxq(h, 0, "e4m3")
    return y + f64(bo)[:, None]

@@ -1,0 +1,296 @@
+from contextlib import ExitStack
+
+import concourse.mybir as mybir
+from concourse.masks import make_identity
+
+K, T, S, H, N = 1024, 4096, 1024, 512, 1536
+FLOPS = 2 * S * (3 * K * H + H * N)
+
+F32 = mybir.dt.float32
+BF16 = mybir.dt.bfloat16
+I32 = mybir.dt.int32
+U32 = mybir.dt.uint32
+U16 = mybir.dt.uint16
+U8 = mybir.dt.uint8
+FP8X4 = mybir.dt.float8_e4m3fn_x4
+FP4X4 = mybir.dt.float4_e2m1fn_x4
+ACT = mybir.ActivationFunctionType
+ALU = mybir.AluOpType
+
+P = 128
+PASSES = 2
+HALF = 512
+SUB = 256
+CHUNK = 512
+OUT_TILES = N // P
+
+
+def tile_list_trigram_next_logits_kernel(
+    tc, tab_words, tab_scales, offs, offs2, offs3, w1, w2_words, w2_scales, w3_words, w3_scales, bh, gain, wo, bo, out
+):
+    nc = tc.nc
+    with ExitStack() as ctx:
+        keep = ctx.enter_context(tc.tile_pool(name="keep", bufs=1))
+        ring = ctx.enter_context(tc.tile_pool(name="ring", bufs=6))
+        psum = ctx.enter_context(tc.psum_pool(name="psum", bufs=1))
+
+        def held(name, shape, dtype, tag=None):
+            return keep.tile(shape, dtype, name=name, tag=tag or name, align_bytes=64)
+
+        def bank(b, name):
+            return psum.tile([P, HALF], F32, name=name, tag="bank%d" % b)
+
+        lists = [held("list%d" % u, [P, S // 16], U16) for u in range(3)]
+        table_scales = held("table_scales", [P, T // 4], I32)
+        ident = held("ident", [P, P], F32)
+        consts = held("consts", [P, 20], F32)
+        w1_bf = [held("w1_bf%d" % a, [P, 4 * H], BF16) for a in range(PASSES)]
+        w1_codes = held("w1_codes", [P, PASSES, H], U32)
+        w1_sc = held("w1_sc", [P, PASSES, H], U8)
+        w2_codes = held("w2_codes", [P, PASSES, H], I32)
+        w3_codes = held("w3_codes", [P, PASSES, H // 2], I32)
+        w2_sc_raw = held("w2_sc_raw", [P, PASSES, H // 4], I32)
+        w3_sc_raw = held("w3_sc_raw", [P, PASSES, H // 4], I32)
+        wo_bf = {}
+        wo_codes = [held("wo_codes%d" % c, [P, CHUNK], U32) for c in range(3)]
+        wo_sc = [held("wo_sc%d" % c, [P, CHUNK], U8) for c in range(3)]
+        x_words = {(0, u, a): held("x%d_%d" % (u, a), [P, HALF], U32)[:] for u in range(3) for a in range(PASSES)}
+        x_sc = {(0, u): held("xs0_%d" % u, [P, HALF], U8)[:] for u in range(3)}
+        x3_sc_low = [held("xs_low%d" % s, [P, HALF // 4], I32) for s in range(2)]
+        th = [[held("th%d_%d" % (s, v), [P, 4, SUB], F32) for v in range(2)] for s in range(2)]
+        h_bf = [held("h_bf%d" % s, [P, 2, 4 * SUB], BF16) for s in range(2)]
+        h_codes = [held("h_codes%d" % s, [P, HALF], U32) for s in range(2)]
+        h_sc = [held("h_sc%d" % s, [P, HALF], U8) for s in range(2)]
+
+        table = [held("table%d" % a, [P, T], I32) for a in range(PASSES)]
+        rows = held("rows", [P, P], F32)
+        warm = held("warm", [P, 1], F32)
+        w1_raw = [held("w1_raw%d" % a, [P, 4, H], F32) for a in range(PASSES)]
+        w2_raw = held("w2_raw", [P, PASSES, H], I32)
+        w3_raw = held("w3_raw", [P, PASSES, H // 2], I32)
+        wo_raw = [held("wo_raw%d" % c, [P, 4, CHUNK], F32) for c in range(3)]
+
+        nc.vector.memset(table_scales[:], 0)
+        nc.vector.memset(w2_sc_raw[:], 0)
+        nc.vector.memset(w3_sc_raw[:], 0)
+        nc.vector.memset(rows[0:96, :], 0.0)
+        nc.vector.memset(rows[96:108, :], 0.0)
+        for s in range(2):
+            nc.vector.memset(x3_sc_low[s][:], 0)
+        make_identity(nc, ident[:])
+        nc.scalar.activation(warm[:], ident[:, 0:1], ACT.Tanh)
+
+        def load_scales(dst, src, quadrants):
+            for q in quadrants:
+                nc.sync.dma_start(
+                    dst[32 * q : 32 * q + 4, :, :], src[:, 4 * q : 4 * q + 4, :].bitcast(I32).rearrange("a r c -> r a c")
+                )
+
+        def load_table(a):
+            nc.sync.dma_start(table[a][:], tab_words[a].rearrange("p t i -> p (t i)").bitcast(I32))
+
+        def load_w1(a):
+            nc.sync.dma_start(w1_raw[a][:], w1[a * 512 : (a + 1) * 512, :].rearrange("(p j) c -> p j c", j=4))
+
+        def load_wo(c):
+            src = wo[:, c * CHUNK : (c + 1) * CHUNK].rearrange("(g t q) n -> t g q n", t=4, q=8)
+            for t in range(4):
+                nc.sync.dma_start(wo_raw[c][:, t, :], src[t])
+
+        for tile, src in zip(lists, (offs, offs2, offs3)):
+            nc.sync.dma_start(tile[:], src)
+        for a in range(PASSES):
+            for q in range(4):
+                first = 32 * q + 4 * a
+                nc.sync.dma_start(table_scales[first : first + 4, :], tab_scales[a, 4 * q : 4 * q + 4, :].bitcast(I32))
+        nc.sync.dma_start(w2_raw[:], w2_words.rearrange("a p c i -> p a (c i)").bitcast(I32))
+        nc.sync.dma_start(w3_raw[:], w3_words.rearrange("a p b -> p a b").bitcast(I32))
+        load_table(0)
+        nc.sync.dma_start(rows[108:120, :], bo.rearrange("(i p) -> i p", p=P))
+        nc.sync.dma_start(rows[120:124, :].rearrange("t (g q) -> t g q", q=8), bh.rearrange("(g t q) -> t g q", t=4, q=8))
+        nc.sync.dma_start(rows[124:128, :].rearrange("t (g q) -> t g q", q=8), gain.rearrange("(g t q) -> t g q", t=4, q=8))
+        load_scales(w2_sc_raw, w2_scales, range(3))
+        load_w1(0)
+        load_scales(w2_sc_raw, w2_scales, range(3, 4))
+        load_scales(w3_sc_raw, w3_scales, range(4))
+        load_table(1)
+        load_w1(1)
+        for c in range(3):
+            load_wo(c)
+
+        turned = bank(7, "turned")
+        nc.tensor.transpose(turned[:, 0:P], rows[:], ident[:])
+        nc.scalar.copy(consts[:], turned[:, 108:128])
+
+        def offsets(u, s):
+            return lists[u][:, s * (HALF // 16) : (s + 1) * (HALF // 16)]
+
+        def gather_scales(s, u):
+            nc.vector.tensor_copy(x_sc[s, u], table_scales[:].bitcast(U8).indirect(offsets(u, s)))
+            if u == 2:
+                nc.gpsimd.dma_start(x3_sc_low[s][0:124, :], x_sc[s, u][4:128, :].bitcast(I32))
+
+        def gather_words(s, u, a):
+            nc.vector.tensor_copy(x_words[s, u, a], table[a][:].bitcast(U32).indirect(offsets(u, s)))
+
+        def cast_w1(a):
+            src = w1_raw[a][:].rearrange("p j (g t q) -> p t g j q", t=4, q=8)
+            dst = w1_bf[a][:].rearrange("p (t g q j) -> p t g j q", t=4, q=8, j=4)
+            for t in range(4):
+                nc.scalar.copy(dst[:, t], src[:, t])
+
+        def quantize_w1(a, pieces):
+            width = H // pieces
+            for first in range(0, H, width):
+                cols = slice(first, first + width)
+                nc.vector.quantize_mx(
+                    out=w1_codes[:, a, cols].bitcast(FP8X4),
+                    scales=w1_sc[:, a, cols],
+                    in_=w1_bf[a][:, 4 * first : 4 * (first + width)],
+                )
+
+        def reorder(dst, src, run):
+            for a in range(PASSES):
+                nc.vector.tensor_copy(
+                    dst[:, a, :].rearrange("p (t g q) -> p t g q", t=4, q=run),
+                    src[:, a, :].rearrange("p (g t q) -> p t g q", t=4, q=run),
+                )
+
+        def first_product(s, acc, u, a, start, stop):
+            for t in range(4):
+                if u == 0:
+                    lhs = w1_codes[:, a, t * P : (t + 1) * P].bitcast(FP8X4)
+                    lhs_sc = w1_sc[:, a, t * P : (t + 1) * P]
+                elif u == 1:
+                    lhs = w2_codes[:, a, t * P : (t + 1) * P].bitcast(FP8X4)
+                    lhs_sc = w2_sc[:, a, t * 32 : (t + 1) * 32].bitcast(U8)
+                else:
+                    lhs = w3_codes[:, a, t * 64 : (t + 1) * 64].bitcast(U8).bitcast(FP4X4)
+                    lhs_sc = w3_sc[:, a, t * 32 : (t + 1) * 32].bitcast(U8)
+                if a == 0:
+                    rhs_sc = x_sc[s, u]
+                elif u == 2:
+                    rhs_sc = x3_sc_low[s][:].bitcast(U8)
+                else:
+                    rhs_sc = x_sc[s, u][4:128, :]
+                nc.tensor.matmul_mx(
+                    out=acc[t][:],
+                    lhsT=lhs,
+                    lhsT_scale=lhs_sc,
+                    rhs=x_words[s, u, a].bitcast(FP8X4),
+                    rhs_scale=rhs_sc,
+                    start=start,
+                    stop=stop,
+                )
+
+        def hidden(s, acc):
+            for v in range(2):
+                for t in range(4):
+                    nc.scalar.activation(
+                        th[s][v][:, t, :], acc[t][:, v * SUB : (v + 1) * SUB], ACT.Tanh, bias=consts[:, 12 + t : 13 + t]
+                    )
+            for v in range(2):
+                nc.vector.tensor_tensor(
+                    h_bf[s][:, v, :].rearrange("p (n t) -> p n t", t=4),
+                    th[s][v][:].rearrange("p t n -> p n t"),
+                    consts[:, 16:20].unsqueeze(1).to_broadcast([P, SUB, 4]),
+                    ALU.mult,
+                )
+            for v in range(2):
+                cols = slice(v * SUB, (v + 1) * SUB)
+                nc.vector.quantize_mx(out=h_codes[s][:, cols].bitcast(FP8X4), scales=h_sc[s][:, cols], in_=h_bf[s][:, v, :])
+
+        def cast_wo(c, tag):
+            wo_bf[c] = held("wo_bf%d" % c, [P, 4 * CHUNK], BF16, tag)
+            dst = wo_bf[c][:].rearrange("p (m i t) -> p m t i", i=4, t=4)
+            src = wo_raw[c][:].rearrange("p t (m i) -> p m t i", i=4)
+            for first in range(0, CHUNK // 4, 32):
+                nc.scalar.copy(dst[:, first : first + 32], src[:, first : first + 32])
+
+        def quantize_wo(c):
+            nc.vector.quantize_mx(out=wo_codes[c][:].bitcast(FP8X4), scales=wo_sc[c][:], in_=wo_bf[c][:])
+
+        def logits(tokens, tiles, banks, on_vector):
+            s, first = divmod(tokens.start, HALF)
+            width = tokens.stop - tokens.start
+            cols_h = slice(first, first + width)
+            per_bank = HALF // width
+            staged = ring.tile([P, len(tiles), width], F32, name="staged")
+            for e, i in enumerate(tiles):
+                if e % per_bank == 0:
+                    y = bank(banks[e // per_bank], "y")
+                part = y[:, (e % per_bank) * width : (e % per_bank + 1) * width]
+                c, cols = i // 4, slice((i % 4) * P, (i % 4 + 1) * P)
+                nc.tensor.matmul_mx(
+                    out=part,
+                    lhsT=wo_codes[c][:, cols].bitcast(FP8X4),
+                    lhsT_scale=wo_sc[c][:, cols],
+                    rhs=h_codes[s][:, cols_h].bitcast(FP8X4),
+                    rhs_scale=h_sc[s][:, cols_h],
+                    start=True,
+                    stop=True,
+                )
+                if on_vector:
+                    nc.vector.tensor_scalar(staged[:, e, :], part, consts[:, i : i + 1], None, ALU.add)
+                else:
+                    nc.scalar.activation(staged[:, e, :], part, ACT.Identity, bias=consts[:, i : i + 1])
+            dst = out[tiles[0] * P : (tiles[-1] + 1) * P, tokens]
+            nc.sync.dma_start(dst.rearrange("(e p) n -> p e n", p=P), staged[:])
+
+        def first_layer(s, order, banks):
+            acc = [bank(b, "acc") for b in banks]
+            steps = [(u, a) for a in range(PASSES) for u in order]
+            for u, a in steps:
+                first_product(s, acc, u, a, (u, a) == steps[0], (u, a) == steps[-1])
+            return acc
+
+        for a in range(PASSES):
+            cast_w1(a)
+        reorder(w2_codes, w2_raw, 8)
+        reorder(w3_codes, w3_raw, 4)
+        for u in (2, 1, 0):
+            gather_scales(0, u)
+        for u in (1, 2, 0):
+            gather_words(0, u, 0)
+        w_sc = held("w_sc", [P, 2, PASSES, H // 4], I32, "w1_raw0")
+        w2_sc, w3_sc = w_sc[:, 0], w_sc[:, 1]
+        reorder(w2_sc, w2_sc_raw, 2)
+        reorder(w3_sc, w3_sc_raw, 2)
+        quantize_w1(0, 1)
+        quantize_w1(1, 4)
+        for u in (1, 2, 0):
+            gather_words(0, u, 1)
+        acc = first_layer(0, (1, 2, 0), range(4))
+        hidden(0, acc)
+        cast_wo(0, "w1_raw1")
+        quantize_wo(0)
+        for pair in range(2):
+            logits(slice(0, HALF), (2 * pair, 2 * pair + 1), (2 * pair, 2 * pair + 1), False)
+        cast_wo(1, "th0_0")
+        quantize_wo(1)
+        cast_wo(2, "th0_1")
+        logits(slice(0, HALF), (4, 5), (0, 1), False)
+
+        for u in range(3):
+            x_sc[1, u] = held("xs1_%d" % u, [P, HALF], U8)[:]
+        early_words = held("early_words", [P, 2, HALF], U32)
+        late_words = held("late_words", [P, 4, HALF], U32, "h_bf0")
+        for e, (u, a) in enumerate(((0, 0), (1, 0))):
+            x_words[1, u, a] = early_words[:, e, :]
+        for e, (u, a) in enumerate(((2, 0), (0, 1), (1, 1), (2, 1))):
+            x_words[1, u, a] = late_words[:, e, :]
+        for u in (2, 0, 1):
+            gather_scales(1, u)
+        for a in range(PASSES):
+            for u in range(3):
+                gather_words(1, u, a)
+        acc = first_layer(1, range(3), range(4, 8))
+        quantize_wo(2)
+        logits(slice(0, HALF), (8, 9), (2, 3), True)
+        hidden(1, acc)
+        logits(slice(0, HALF), (10, 11), (0, 1), True)
+        logits(slice(0, HALF), (6, 7), (2, 3), False)
+        for group, banks in enumerate(((4, 5), (6, 7), (0, 1))):
+            logits(slice(HALF, HALF + SUB), range(4 * group, 4 * group + 4), banks, False)
+        for group, banks in enumerate(((2, 3), (4, 5), (6, 7))):
+            logits(slice(HALF + SUB, S), range(4 * group, 4 * group + 4), banks, group < 2)

@@ -49,6 +49,8 @@ def tile_list_trigram_next_logits_kernel(
         w1_sc = held("w1_sc", [P, PASSES, H], U8)
         w2_codes = held("w2_codes", [P, PASSES, H], I32)
         w3_codes = held("w3_codes", [P, PASSES, H // 2], I32)
+        w2_sc = held("w2_sc", [P, PASSES, H // 4], I32)
+        w3_sc = held("w3_sc", [P, PASSES, H // 4], I32)
         w2_sc_raw = held("w2_sc_raw", [P, PASSES, H // 4], I32)
         w3_sc_raw = held("w3_sc_raw", [P, PASSES, H // 4], I32)
         wo_bf = {}
@@ -114,9 +116,10 @@ def tile_list_trigram_next_logits_kernel(
         load_scales(w2_sc_raw, w2_scales, range(3, 4))
         load_scales(w3_sc_raw, w3_scales, range(4))
         load_table(1)
+        load_wo(0)
         load_w1(1)
-        for c in range(3):
-            load_wo(c)
+        load_wo(1)
+        load_wo(2)
 
         turned = bank(7, "turned")
         nc.tensor.transpose(turned[:, 0:P], rows[:], ident[:])
@@ -128,16 +131,16 @@ def tile_list_trigram_next_logits_kernel(
         def gather_scales(s, u):
             nc.vector.tensor_copy(x_sc[s, u], table_scales[:].bitcast(U8).indirect(offsets(u, s)))
             if u == 2:
-                nc.gpsimd.dma_start(x3_sc_low[s][0:124, :], x_sc[s, u][4:128, :].bitcast(I32))
+                nc.scalar.dma_start(x3_sc_low[s][0:124, :], x_sc[s, u][4:128, :].bitcast(I32))
 
         def gather_words(s, u, a):
             nc.vector.tensor_copy(x_words[s, u, a], table[a][:].bitcast(U32).indirect(offsets(u, s)))
 
-        def cast_w1(a):
-            src = w1_raw[a][:].rearrange("p j (g t q) -> p t g j q", t=4, q=8)
-            dst = w1_bf[a][:].rearrange("p (t g q j) -> p t g j q", t=4, q=8, j=4)
-            for t in range(4):
-                nc.scalar.copy(dst[:, t], src[:, t])
+        def cast_w1(a, t, copy):
+            src = w1_raw[a][:].rearrange("p j (g t u i) -> p t u g j i", t=4, u=2, i=4)
+            dst = w1_bf[a][:].rearrange("p (t g u i j) -> p t u g j i", t=4, u=2, i=4, j=4)
+            for u in range(2):
+                copy(dst[:, t, u], src[:, t, u])
 
         def quantize_w1(a, pieces):
             width = H // pieces
@@ -191,9 +194,9 @@ def tile_list_trigram_next_logits_kernel(
                     )
             for v in range(2):
                 nc.vector.tensor_tensor(
-                    h_bf[s][:, v, :].rearrange("p (n t) -> p n t", t=4),
-                    th[s][v][:].rearrange("p t n -> p n t"),
-                    consts[:, 16:20].unsqueeze(1).to_broadcast([P, SUB, 4]),
+                    h_bf[s][:, v, :].rearrange("p (m i t) -> p m t i", i=4, t=4),
+                    th[s][v][:].rearrange("p t (m i) -> p m t i", i=4),
+                    consts[:, 16:20].unsqueeze(1).unsqueeze(3).to_broadcast([P, SUB // 4, 4, 4]),
                     ALU.mult,
                 )
             for v in range(2):
@@ -244,41 +247,39 @@ def tile_list_trigram_next_logits_kernel(
                 first_product(s, acc, u, a, (u, a) == steps[0], (u, a) == steps[-1])
             return acc
 
-        for a in range(PASSES):
-            cast_w1(a)
+        for t in range(4):
+            cast_w1(0, t, nc.scalar.copy)
         reorder(w2_codes, w2_raw, 8)
         reorder(w3_codes, w3_raw, 4)
         for u in (2, 1, 0):
             gather_scales(0, u)
         for u in (1, 2, 0):
             gather_words(0, u, 0)
-        w_sc = held("w_sc", [P, 2, PASSES, H // 4], I32, "w1_raw0")
-        w2_sc, w3_sc = w_sc[:, 0], w_sc[:, 1]
         reorder(w2_sc, w2_sc_raw, 2)
         reorder(w3_sc, w3_sc_raw, 2)
         quantize_w1(0, 1)
-        quantize_w1(1, 4)
         for u in (1, 2, 0):
             gather_words(0, u, 1)
+        for t in range(4):
+            cast_w1(1, t, nc.vector.tensor_copy if t < 2 else nc.scalar.copy)
+        quantize_w1(1, 4)
         acc = first_layer(0, (1, 2, 0), range(4))
-        hidden(0, acc)
-        cast_wo(0, "w1_raw1")
+        cast_wo(0, "wo_bf0")
         quantize_wo(0)
+        hidden(0, acc)
         for pair in range(2):
             logits(slice(0, HALF), (2 * pair, 2 * pair + 1), (2 * pair, 2 * pair + 1), False)
         cast_wo(1, "th0_0")
         quantize_wo(1)
         cast_wo(2, "th0_1")
-        logits(slice(0, HALF), (4, 5), (0, 1), False)
 
         for u in range(3):
             x_sc[1, u] = held("xs1_%d" % u, [P, HALF], U8)[:]
-        early_words = held("early_words", [P, 2, HALF], U32)
-        late_words = held("late_words", [P, 4, HALF], U32, "h_bf0")
-        for e, (u, a) in enumerate(((0, 0), (1, 0))):
-            x_words[1, u, a] = early_words[:, e, :]
-        for e, (u, a) in enumerate(((2, 0), (0, 1), (1, 1), (2, 1))):
-            x_words[1, u, a] = late_words[:, e, :]
+        early_words = held("early_words", [P, 3, HALF], U32)
+        late_words = held("late_words", [P, 3, HALF], U32, "h_bf0")
+        for u in range(3):
+            x_words[1, u, 0] = early_words[:, u, :]
+            x_words[1, u, 1] = late_words[:, u, :]
         for u in (2, 0, 1):
             gather_scales(1, u)
         for a in range(PASSES):
@@ -286,11 +287,12 @@ def tile_list_trigram_next_logits_kernel(
                 gather_words(1, u, a)
         acc = first_layer(1, range(3), range(4, 8))
         quantize_wo(2)
-        logits(slice(0, HALF), (8, 9), (2, 3), True)
+        logits(slice(0, HALF), (4, 5), (0, 1), True)
         hidden(1, acc)
-        logits(slice(0, HALF), (10, 11), (0, 1), True)
         logits(slice(0, HALF), (6, 7), (2, 3), False)
+        logits(slice(0, HALF), (8, 9), (0, 1), False)
+        logits(slice(0, HALF), (10, 11), (2, 3), True)
         for group, banks in enumerate(((4, 5), (6, 7), (0, 1))):
-            logits(slice(HALF, HALF + SUB), range(4 * group, 4 * group + 4), banks, False)
+            logits(slice(HALF, HALF + SUB), range(4 * group, 4 * group + 4), banks, group == 1)
         for group, banks in enumerate(((2, 3), (4, 5), (6, 7))):
-            logits(slice(HALF + SUB, S), range(4 * group, 4 * group + 4), banks, group < 2)
+            logits(slice(HALF + SUB, S), range(4 * group, 4 * group + 4), banks, group != 1)

@@ -31,7 +31,7 @@ def tile_list_trigram_next_logits_kernel(
     nc = tc.nc
     with ExitStack() as ctx:
         keep = ctx.enter_context(tc.tile_pool(name="keep", bufs=1))
-        ring = ctx.enter_context(tc.tile_pool(name="ring", bufs=6))
+        ring = ctx.enter_context(tc.tile_pool(name="ring", bufs=12))
         psum = ctx.enter_context(tc.psum_pool(name="psum", bufs=1))
 
         def held(name, shape, dtype, tag=None):
@@ -115,8 +115,8 @@ def tile_list_trigram_next_logits_kernel(
         load_w1(0)
         load_scales(w2_sc_raw, w2_scales, range(3, 4))
         load_scales(w3_sc_raw, w3_scales, range(4))
-        load_table(1)
         load_wo(0)
+        load_table(1)
         load_w1(1)
         load_wo(1)
         load_wo(2)
@@ -203,42 +203,40 @@ def tile_list_trigram_next_logits_kernel(
                 cols = slice(v * SUB, (v + 1) * SUB)
                 nc.vector.quantize_mx(out=h_codes[s][:, cols].bitcast(FP8X4), scales=h_sc[s][:, cols], in_=h_bf[s][:, v, :])
 
-        def cast_wo(c, tag):
+        def cast_wo(c, tag, copy, pieces):
             wo_bf[c] = held("wo_bf%d" % c, [P, 4 * CHUNK], BF16, tag)
             dst = wo_bf[c][:].rearrange("p (m i t) -> p m t i", i=4, t=4)
             src = wo_raw[c][:].rearrange("p t (m i) -> p m t i", i=4)
-            for first in range(0, CHUNK // 4, 32):
-                nc.scalar.copy(dst[:, first : first + 32], src[:, first : first + 32])
+            step = CHUNK // 4 // pieces
+            for first in range(0, CHUNK // 4, step):
+                copy(dst[:, first : first + step], src[:, first : first + step])
 
         def quantize_wo(c):
             nc.vector.quantize_mx(out=wo_codes[c][:].bitcast(FP8X4), scales=wo_sc[c][:], in_=wo_bf[c][:])
 
-        def logits(tokens, tiles, banks, on_vector):
-            s, first = divmod(tokens.start, HALF)
-            width = tokens.stop - tokens.start
-            cols_h = slice(first, first + width)
-            per_bank = HALF // width
-            staged = ring.tile([P, len(tiles), width], F32, name="staged")
-            for e, i in enumerate(tiles):
-                if e % per_bank == 0:
-                    y = bank(banks[e // per_bank], "y")
-                part = y[:, (e % per_bank) * width : (e % per_bank + 1) * width]
+        def logits(tiles, halves, banks, on_vector):
+            parts = [(i, s) for i in tiles for s in halves]
+            staged = ring.tile([P, len(parts), HALF], F32, name="staged")
+            for e, (i, s) in enumerate(parts):
+                y = bank(banks[e], "y")
                 c, cols = i // 4, slice((i % 4) * P, (i % 4 + 1) * P)
                 nc.tensor.matmul_mx(
-                    out=part,
+                    out=y[:],
                     lhsT=wo_codes[c][:, cols].bitcast(FP8X4),
                     lhsT_scale=wo_sc[c][:, cols],
-                    rhs=h_codes[s][:, cols_h].bitcast(FP8X4),
-                    rhs_scale=h_sc[s][:, cols_h],
+                    rhs=h_codes[s][:].bitcast(FP8X4),
+                    rhs_scale=h_sc[s][:],
                     start=True,
                     stop=True,
                 )
-                if on_vector:
-                    nc.vector.tensor_scalar(staged[:, e, :], part, consts[:, i : i + 1], None, ALU.add)
+                if on_vector[e]:
+                    nc.vector.tensor_scalar(staged[:, e, :], y[:], consts[:, i : i + 1], None, ALU.add)
                 else:
-                    nc.scalar.activation(staged[:, e, :], part, ACT.Identity, bias=consts[:, i : i + 1])
-            dst = out[tiles[0] * P : (tiles[-1] + 1) * P, tokens]
-            nc.sync.dma_start(dst.rearrange("(e p) n -> p e n", p=P), staged[:])
+                    nc.scalar.activation(staged[:, e, :], y[:], ACT.Identity, bias=consts[:, i : i + 1])
+            dst = out[tiles[0] * P : (tiles[-1] + 1) * P, halves[0] * HALF : (halves[-1] + 1) * HALF]
+            nc.sync.dma_start(
+                dst.rearrange("(e p) n -> p e n", p=P), staged[:].rearrange("p (e s) n -> p e (s n)", s=len(halves))
+            )
 
         def first_layer(s, order, banks):
             acc = [bank(b, "acc") for b in banks]
@@ -258,41 +256,41 @@ def tile_list_trigram_next_logits_kernel(
         reorder(w2_sc, w2_sc_raw, 2)
         reorder(w3_sc, w3_sc_raw, 2)
         quantize_w1(0, 1)
+        cast_wo(0, "wo_bf0", nc.scalar.copy, 1)
+        quantize_wo(0)
         for u in (1, 2, 0):
             gather_words(0, u, 1)
         for t in range(4):
-            cast_w1(1, t, nc.vector.tensor_copy if t < 2 else nc.scalar.copy)
+            cast_w1(1, t, nc.scalar.copy)
         quantize_w1(1, 4)
         acc = first_layer(0, (1, 2, 0), range(4))
-        cast_wo(0, "wo_bf0")
-        quantize_wo(0)
         hidden(0, acc)
+        cast_wo(1, "th0_0", nc.scalar.copy, 1)
         for pair in range(2):
-            logits(slice(0, HALF), (2 * pair, 2 * pair + 1), (2 * pair, 2 * pair + 1), False)
-        cast_wo(1, "th0_0")
-        quantize_wo(1)
-        cast_wo(2, "th0_1")
+            logits((2 * pair, 2 * pair + 1), (0,), (2 * pair, 2 * pair + 1), (False, False))
 
         for u in range(3):
             x_sc[1, u] = held("xs1_%d" % u, [P, HALF], U8)[:]
-        early_words = held("early_words", [P, 3, HALF], U32)
-        late_words = held("late_words", [P, 3, HALF], U32, "h_bf0")
+        early_words = held("early_words", [P, 3, HALF], U32, "w1_raw0")
+        late_words = held("late_words", [P, 2, HALF], U32, "h_bf0")
         for u in range(3):
             x_words[1, u, 0] = early_words[:, u, :]
-            x_words[1, u, 1] = late_words[:, u, :]
+        x_words[1, 0, 1] = held("mid_words", [P, HALF], U32, "w1_bf1")[:]
+        for u in (1, 2):
+            x_words[1, u, 1] = late_words[:, u - 1, :]
         for u in (2, 0, 1):
             gather_scales(1, u)
         for a in range(PASSES):
             for u in range(3):
                 gather_words(1, u, a)
         acc = first_layer(1, range(3), range(4, 8))
+        quantize_wo(1)
+        cast_wo(2, "table1", nc.vector.tensor_copy, 1)
         quantize_wo(2)
-        logits(slice(0, HALF), (4, 5), (0, 1), True)
         hidden(1, acc)
-        logits(slice(0, HALF), (6, 7), (2, 3), False)
-        logits(slice(0, HALF), (8, 9), (0, 1), False)
-        logits(slice(0, HALF), (10, 11), (2, 3), True)
-        for group, banks in enumerate(((4, 5), (6, 7), (0, 1))):
-            logits(slice(HALF, HALF + SUB), range(4 * group, 4 * group + 4), banks, group == 1)
-        for group, banks in enumerate(((2, 3), (4, 5), (6, 7))):
-            logits(slice(HALF + SUB, S), range(4 * group, 4 * group + 4), banks, group != 1)
+        for pair in range(2, 4):
+            logits((2 * pair, 2 * pair + 1), (0,), (2 * pair - 4, 2 * pair - 3), (False, False))
+        for pair in range(4):
+            logits((2 * pair, 2 * pair + 1), (1,), ((2 * pair + 4) % 8, (2 * pair + 5) % 8), (True, False))
+        for i in range(8, 12):
+            logits((i,), (0, 1), ((2 * i + 4) % 8, (2 * i + 5) % 8), (False, True))

@@ -31,7 +31,7 @@ def tile_list_trigram_next_logits_kernel(
     nc = tc.nc
     with ExitStack() as ctx:
         keep = ctx.enter_context(tc.tile_pool(name="keep", bufs=1))
-        ring = ctx.enter_context(tc.tile_pool(name="ring", bufs=12))
+        ring = ctx.enter_context(tc.tile_pool(name="ring", bufs=10))
         psum = ctx.enter_context(tc.psum_pool(name="psum", bufs=1))
 
         def held(name, shape, dtype, tag=None):
@@ -60,7 +60,7 @@ def tile_list_trigram_next_logits_kernel(
         x_sc = {(0, u): held("xs0_%d" % u, [P, HALF], U8)[:] for u in range(3)}
         x3_sc_low = [held("xs_low%d" % s, [P, HALF // 4], I32) for s in range(2)]
         th = [[held("th%d_%d" % (s, v), [P, 4, SUB], F32) for v in range(2)] for s in range(2)]
-        h_bf = [held("h_bf%d" % s, [P, 2, 4 * SUB], BF16) for s in range(2)]
+        h_bf = {0: held("h_bf0", [P, 2, 4 * SUB], BF16)}
         h_codes = [held("h_codes%d" % s, [P, HALF], U32) for s in range(2)]
         h_sc = [held("h_sc%d" % s, [P, HALF], U8) for s in range(2)]
 
@@ -214,9 +214,10 @@ def tile_list_trigram_next_logits_kernel(
         def quantize_wo(c):
             nc.vector.quantize_mx(out=wo_codes[c][:].bitcast(FP8X4), scales=wo_sc[c][:], in_=wo_bf[c][:])
 
-        def logits(tiles, halves, banks, on_vector):
+        def logits(tiles, halves, banks, on_vector, staged=None):
             parts = [(i, s) for i in tiles for s in halves]
-            staged = ring.tile([P, len(parts), HALF], F32, name="staged")
+            if staged is None:
+                staged = ring.tile([P, len(parts), HALF], F32, name="staged")
             for e, (i, s) in enumerate(parts):
                 y = bank(banks[e], "y")
                 c, cols = i // 4, slice((i % 4) * P, (i % 4 + 1) * P)
@@ -266,13 +267,16 @@ def tile_list_trigram_next_logits_kernel(
         acc = first_layer(0, (1, 2, 0), range(4))
         hidden(0, acc)
         cast_wo(1, "th0_0", nc.scalar.copy, 1)
-        for pair in range(2):
-            logits((2 * pair, 2 * pair + 1), (0,), (2 * pair, 2 * pair + 1), (False, False))
+        quantize_wo(1)
+        first_staged = held("first_staged", [P, 4, HALF], F32, "wo_raw1")
+        logits((0, 1), (0,), (6, 7), (False, False), first_staged[:, 0:2, :])
+        logits((2, 3), (0,), (2, 3), (False, False), first_staged[:, 2:4, :])
+        logits((4, 5), (0,), (6, 7), (False, False))
 
         for u in range(3):
             x_sc[1, u] = held("xs1_%d" % u, [P, HALF], U8)[:]
         early_words = held("early_words", [P, 3, HALF], U32, "w1_raw0")
-        late_words = held("late_words", [P, 2, HALF], U32, "h_bf0")
+        late_words = held("late_words", [P, 2, HALF], U32, "th0_0")
         for u in range(3):
             x_words[1, u, 0] = early_words[:, u, :]
         x_words[1, 0, 1] = held("mid_words", [P, HALF], U32, "w1_bf1")[:]
@@ -283,14 +287,13 @@ def tile_list_trigram_next_logits_kernel(
         for a in range(PASSES):
             for u in range(3):
                 gather_words(1, u, a)
-        acc = first_layer(1, range(3), range(4, 8))
-        quantize_wo(1)
+        acc = first_layer(1, range(3), (4, 5, 0, 1))
         cast_wo(2, "table1", nc.vector.tensor_copy, 1)
         quantize_wo(2)
+        h_bf[1] = held("h_bf1", [P, 2, 4 * SUB], BF16, "wo_raw2")
+        logits((6, 7), (0,), (2, 3), (False, True))
         hidden(1, acc)
-        for pair in range(2, 4):
-            logits((2 * pair, 2 * pair + 1), (0,), (2 * pair - 4, 2 * pair - 3), (False, False))
-        for pair in range(4):
-            logits((2 * pair, 2 * pair + 1), (1,), ((2 * pair + 4) % 8, (2 * pair + 5) % 8), (True, False))
-        for i in range(8, 12):
-            logits((i,), (0, 1), ((2 * i + 4) % 8, (2 * i + 5) % 8), (False, True))
+        logits((8, 9), (0,), (6, 7), (False, False))
+        logits((10, 11), (0,), (2, 3), (False, False))
+        for pair in range(6):
+            logits((2 * pair, 2 * pair + 1), (1,), ((4, 5), (0, 1), (6, 7), (2, 3))[pair % 4], (True, False))

@@ -31,7 +31,7 @@ def tile_list_trigram_next_logits_kernel(
     nc = tc.nc
     with ExitStack() as ctx:
         keep = ctx.enter_context(tc.tile_pool(name="keep", bufs=1))
-        ring = ctx.enter_context(tc.tile_pool(name="ring", bufs=10))
+        ring = ctx.enter_context(tc.tile_pool(name="ring", bufs=12))
         psum = ctx.enter_context(tc.psum_pool(name="psum", bufs=1))
 
         def held(name, shape, dtype, tag=None):
@@ -43,27 +43,21 @@ def tile_list_trigram_next_logits_kernel(
         lists = [held("list%d" % u, [P, S // 16], U16) for u in range(3)]
         table_scales = held("table_scales", [P, T // 4], I32)
         ident = held("ident", [P, P], F32)
-        consts = held("consts", [P, 20], F32)
         w1_bf = [held("w1_bf%d" % a, [P, 4 * H], BF16) for a in range(PASSES)]
-        w1_codes = held("w1_codes", [P, PASSES, H], U32)
-        w1_sc = held("w1_sc", [P, PASSES, H], U8)
+        w1_codes = [held("w1_codes%d" % a, [P, H], U32) for a in range(PASSES)]
+        w1_sc = [held("w1_sc%d" % a, [P, H], U8) for a in range(PASSES)]
         w2_codes = held("w2_codes", [P, PASSES, H], I32)
         w3_codes = held("w3_codes", [P, PASSES, H // 2], I32)
-        w2_sc = held("w2_sc", [P, PASSES, H // 4], I32)
-        w3_sc = held("w3_sc", [P, PASSES, H // 4], I32)
-        w2_sc_raw = held("w2_sc_raw", [P, PASSES, H // 4], I32)
-        w3_sc_raw = held("w3_sc_raw", [P, PASSES, H // 4], I32)
-        wo_bf = {}
+        w_sc_raw = held("w_sc_raw", [P, PASSES, H // 4], I32)
+        wo_bf = [held("wo_bf%d" % c, [P, 4 * CHUNK], BF16) for c in range(2)] + [None]
         wo_codes = [held("wo_codes%d" % c, [P, CHUNK], U32) for c in range(3)]
         wo_sc = [held("wo_sc%d" % c, [P, CHUNK], U8) for c in range(3)]
-        x_words = {(0, u, a): held("x%d_%d" % (u, a), [P, HALF], U32)[:] for u in range(3) for a in range(PASSES)}
-        x_sc = {(0, u): held("xs0_%d" % u, [P, HALF], U8)[:] for u in range(3)}
-        x3_sc_low = [held("xs_low%d" % s, [P, HALF // 4], I32) for s in range(2)]
-        th = [[held("th%d_%d" % (s, v), [P, 4, SUB], F32) for v in range(2)] for s in range(2)]
-        h_bf = {0: held("h_bf0", [P, 2, 4 * SUB], BF16)}
+        x_sc = [held("x_sc%d" % u, [P, S], U8) for u in range(3)]
+        x_words = [held("x_words%d" % b, [P, HALF], U32)[:] for b in range(5)]
+        x3_sc_low = held("x3_sc_low", [P, S // 4], I32)
+        h_bf = [held("h_bf%d" % s, [P, 2, 4 * SUB], BF16) for s in range(2)]
         h_codes = [held("h_codes%d" % s, [P, HALF], U32) for s in range(2)]
         h_sc = [held("h_sc%d" % s, [P, HALF], U8) for s in range(2)]
-
         table = [held("table%d" % a, [P, T], I32) for a in range(PASSES)]
         rows = held("rows", [P, P], F32)
         warm = held("warm", [P, 1], F32)
@@ -73,19 +67,18 @@ def tile_list_trigram_next_logits_kernel(
         wo_raw = [held("wo_raw%d" % c, [P, 4, CHUNK], F32) for c in range(3)]
 
         nc.vector.memset(table_scales[:], 0)
-        nc.vector.memset(w2_sc_raw[:], 0)
-        nc.vector.memset(w3_sc_raw[:], 0)
+        nc.vector.memset(w_sc_raw[:], 0)
+        nc.vector.memset(x3_sc_low[96:128, :], 0)
         nc.vector.memset(rows[0:96, :], 0.0)
         nc.vector.memset(rows[96:108, :], 0.0)
-        for s in range(2):
-            nc.vector.memset(x3_sc_low[s][:], 0)
         make_identity(nc, ident[:])
         nc.scalar.activation(warm[:], ident[:, 0:1], ACT.Tanh)
 
-        def load_scales(dst, src, quadrants):
-            for q in quadrants:
+        def load_weight_scales(first, src):
+            for q in range(4):
                 nc.sync.dma_start(
-                    dst[32 * q : 32 * q + 4, :, :], src[:, 4 * q : 4 * q + 4, :].bitcast(I32).rearrange("a r c -> r a c")
+                    w_sc_raw[32 * q + first : 32 * q + first + 4, :, :],
+                    src[:, 4 * q : 4 * q + 4, :].bitcast(I32).rearrange("a r c -> r a c"),
                 )
 
         def load_table(a):
@@ -101,101 +94,88 @@ def tile_list_trigram_next_logits_kernel(
 
         for tile, src in zip(lists, (offs, offs2, offs3)):
             nc.sync.dma_start(tile[:], src)
-        for a in range(PASSES):
-            for q in range(4):
-                first = 32 * q + 4 * a
-                nc.sync.dma_start(table_scales[first : first + 4, :], tab_scales[a, 4 * q : 4 * q + 4, :].bitcast(I32))
+        for q in range(4):
+            nc.sync.dma_start(table_scales[32 * q : 32 * q + 8, :], tab_scales[:, 4 * q : 4 * q + 4, :].bitcast(I32))
         nc.sync.dma_start(w2_raw[:], w2_words.rearrange("a p c i -> p a (c i)").bitcast(I32))
         nc.sync.dma_start(w3_raw[:], w3_words.rearrange("a p b -> p a b").bitcast(I32))
-        load_table(0)
-        nc.sync.dma_start(rows[108:120, :], bo.rearrange("(i p) -> i p", p=P))
-        nc.sync.dma_start(rows[120:124, :].rearrange("t (g q) -> t g q", q=8), bh.rearrange("(g t q) -> t g q", t=4, q=8))
-        nc.sync.dma_start(rows[124:128, :].rearrange("t (g q) -> t g q", q=8), gain.rearrange("(g t q) -> t g q", t=4, q=8))
-        load_scales(w2_sc_raw, w2_scales, range(3))
         load_w1(0)
-        load_scales(w2_sc_raw, w2_scales, range(3, 4))
-        load_scales(w3_sc_raw, w3_scales, range(4))
-        load_wo(0)
+        load_weight_scales(4, w2_scales)
+        load_table(0)
+        load_weight_scales(0, w3_scales)
+        nc.gpsimd.dma_start(rows[108:120, :], bo.rearrange("(i p) -> i p", p=P))
+        nc.gpsimd.dma_start(rows[120:124, :].rearrange("t (g q) -> t g q", q=8), bh.rearrange("(g t q) -> t g q", t=4, q=8))
+        nc.gpsimd.dma_start(rows[124:128, :].rearrange("t (g q) -> t g q", q=8), gain.rearrange("(g t q) -> t g q", t=4, q=8))
         load_table(1)
         load_w1(1)
+        load_wo(0)
         load_wo(1)
         load_wo(2)
 
-        turned = bank(7, "turned")
-        nc.tensor.transpose(turned[:, 0:P], rows[:], ident[:])
-        nc.scalar.copy(consts[:], turned[:, 108:128])
 
-        def offsets(u, s):
-            return lists[u][:, s * (HALF // 16) : (s + 1) * (HALF // 16)]
+        def gather_words(s, u, a, dst):
+            picks = lists[u][:, s * (HALF // 16) : (s + 1) * (HALF // 16)]
+            nc.vector.tensor_copy(dst, table[a][:].bitcast(U32).indirect(picks))
 
-        def gather_scales(s, u):
-            nc.vector.tensor_copy(x_sc[s, u], table_scales[:].bitcast(U8).indirect(offsets(u, s)))
-            if u == 2:
-                nc.scalar.dma_start(x3_sc_low[s][0:124, :], x_sc[s, u][4:128, :].bitcast(I32))
+        def cast_w1(a):
+            src = w1_raw[a][:].rearrange("p j (g t u i) -> p t g u j i", t=4, u=2, i=4)
+            dst = w1_bf[a][:].rearrange("p (t g u i j) -> p t g u j i", t=4, u=2, i=4, j=4)
+            for t in range(4):
+                nc.scalar.copy(dst[:, t], src[:, t])
 
-        def gather_words(s, u, a):
-            nc.vector.tensor_copy(x_words[s, u, a], table[a][:].bitcast(U32).indirect(offsets(u, s)))
-
-        def cast_w1(a, t, copy):
-            src = w1_raw[a][:].rearrange("p j (g t u i) -> p t u g j i", t=4, u=2, i=4)
-            dst = w1_bf[a][:].rearrange("p (t g u i j) -> p t u g j i", t=4, u=2, i=4, j=4)
-            for u in range(2):
-                copy(dst[:, t, u], src[:, t, u])
-
-        def quantize_w1(a, pieces):
-            width = H // pieces
-            for first in range(0, H, width):
-                cols = slice(first, first + width)
-                nc.vector.quantize_mx(
-                    out=w1_codes[:, a, cols].bitcast(FP8X4),
-                    scales=w1_sc[:, a, cols],
-                    in_=w1_bf[a][:, 4 * first : 4 * (first + width)],
-                )
+        def quantize_w1(a):
+            nc.vector.quantize_mx(out=w1_codes[a][:].bitcast(FP8X4), scales=w1_sc[a][:], in_=w1_bf[a][:])
 
         def reorder(dst, src, run):
-            for a in range(PASSES):
-                nc.vector.tensor_copy(
-                    dst[:, a, :].rearrange("p (t g q) -> p t g q", t=4, q=run),
-                    src[:, a, :].rearrange("p (g t q) -> p t g q", t=4, q=run),
-                )
+            nc.vector.tensor_copy(
+                dst[:].rearrange("p a (t g q) -> p a t g q", t=4, q=run),
+                src[:].rearrange("p a (g t q) -> p a t g q", t=4, q=run),
+            )
 
-        def first_product(s, acc, u, a, start, stop):
+        def first_product(s, acc, u, a, x_words, start, stop):
+            cols = slice(s * HALF, (s + 1) * HALF)
             for t in range(4):
                 if u == 0:
-                    lhs = w1_codes[:, a, t * P : (t + 1) * P].bitcast(FP8X4)
-                    lhs_sc = w1_sc[:, a, t * P : (t + 1) * P]
+                    lhs = w1_codes[a][:, t * P : (t + 1) * P].bitcast(FP8X4)
+                    lhs_sc = w1_sc[a][:, t * P : (t + 1) * P]
                 elif u == 1:
                     lhs = w2_codes[:, a, t * P : (t + 1) * P].bitcast(FP8X4)
-                    lhs_sc = w2_sc[:, a, t * 32 : (t + 1) * 32].bitcast(U8)
+                    lhs_sc = w_sc[4:128, a, t * 32 : (t + 1) * 32].bitcast(U8)
                 else:
                     lhs = w3_codes[:, a, t * 64 : (t + 1) * 64].bitcast(U8).bitcast(FP4X4)
-                    lhs_sc = w3_sc[:, a, t * 32 : (t + 1) * 32].bitcast(U8)
+                    lhs_sc = w_sc[:, a, t * 32 : (t + 1) * 32].bitcast(U8)
                 if a == 0:
-                    rhs_sc = x_sc[s, u]
+                    rhs_sc = x_sc[u][:, cols]
                 elif u == 2:
-                    rhs_sc = x3_sc_low[s][:].bitcast(U8)
+                    rhs_sc = x3_sc_low[:].bitcast(U8)[:, cols]
                 else:
-                    rhs_sc = x_sc[s, u][4:128, :]
+                    rhs_sc = x_sc[u][4:128, cols]
                 nc.tensor.matmul_mx(
                     out=acc[t][:],
                     lhsT=lhs,
                     lhsT_scale=lhs_sc,
-                    rhs=x_words[s, u, a].bitcast(FP8X4),
+                    rhs=x_words.bitcast(FP8X4),
                     rhs_scale=rhs_sc,
                     start=start,
                     stop=stop,
                 )
 
-        def hidden(s, acc):
+        def look_up_and_multiply(s, acc, a, order, buffers):
+            for u, b in zip(order, buffers):
+                gather_words(s, u, a, x_words[b])
+                first_product(s, acc, u, a, x_words[b], a == 0 and u == order[0], False)
+
+        def squash(acc, th):
             for v in range(2):
                 for t in range(4):
                     nc.scalar.activation(
-                        th[s][v][:, t, :], acc[t][:, v * SUB : (v + 1) * SUB], ACT.Tanh, bias=consts[:, 12 + t : 13 + t]
+                        th[v][:, t, :], acc[t][:, v * SUB : (v + 1) * SUB], ACT.Tanh, bias=consts[:, 12 + t : 13 + t]
                     )
+
+        def quantize_h(s, th):
             for v in range(2):
                 nc.vector.tensor_tensor(
                     h_bf[s][:, v, :].rearrange("p (m i t) -> p m t i", i=4, t=4),
-                    th[s][v][:].rearrange("p t (m i) -> p m t i", i=4),
+                    th[v][:].rearrange("p t (m i) -> p m t i", i=4),
                     consts[:, 16:20].unsqueeze(1).unsqueeze(3).to_broadcast([P, SUB // 4, 4, 4]),
                     ALU.mult,
                 )
@@ -203,97 +183,92 @@ def tile_list_trigram_next_logits_kernel(
                 cols = slice(v * SUB, (v + 1) * SUB)
                 nc.vector.quantize_mx(out=h_codes[s][:, cols].bitcast(FP8X4), scales=h_sc[s][:, cols], in_=h_bf[s][:, v, :])
 
-        def cast_wo(c, tag, copy, pieces):
-            wo_bf[c] = held("wo_bf%d" % c, [P, 4 * CHUNK], BF16, tag)
-            dst = wo_bf[c][:].rearrange("p (m i t) -> p m t i", i=4, t=4)
-            src = wo_raw[c][:].rearrange("p t (m i) -> p m t i", i=4)
-            step = CHUNK // 4 // pieces
-            for first in range(0, CHUNK // 4, step):
-                copy(dst[:, first : first + step], src[:, first : first + step])
+        def cast_wo(c, copy):
+            copy(
+                wo_bf[c][:].rearrange("p (m i t) -> p m t i", i=4, t=4), wo_raw[c][:].rearrange("p t (m i) -> p m t i", i=4)
+            )
 
         def quantize_wo(c):
             nc.vector.quantize_mx(out=wo_codes[c][:].bitcast(FP8X4), scales=wo_sc[c][:], in_=wo_bf[c][:])
 
-        def logits(tiles, halves, banks, on_vector, staged=None):
-            parts = [(i, s) for i in tiles for s in halves]
-            if staged is None:
-                staged = ring.tile([P, len(parts), HALF], F32, name="staged")
-            for e, (i, s) in enumerate(parts):
-                y = bank(banks[e], "y")
-                c, cols = i // 4, slice((i % 4) * P, (i % 4 + 1) * P)
-                nc.tensor.matmul_mx(
-                    out=y[:],
-                    lhsT=wo_codes[c][:, cols].bitcast(FP8X4),
-                    lhsT_scale=wo_sc[c][:, cols],
-                    rhs=h_codes[s][:].bitcast(FP8X4),
-                    rhs_scale=h_sc[s][:],
-                    start=True,
-                    stop=True,
-                )
-                if on_vector[e]:
-                    nc.vector.tensor_scalar(staged[:, e, :], y[:], consts[:, i : i + 1], None, ALU.add)
-                else:
-                    nc.scalar.activation(staged[:, e, :], y[:], ACT.Identity, bias=consts[:, i : i + 1])
-            dst = out[tiles[0] * P : (tiles[-1] + 1) * P, halves[0] * HALF : (halves[-1] + 1) * HALF]
-            nc.sync.dma_start(
-                dst.rearrange("(e p) n -> p e n", p=P), staged[:].rearrange("p (e s) n -> p e (s n)", s=len(halves))
+        staged = {}
+
+        def logits(i, s, b, on_vector):
+            if i % 2 == 0:
+                staged[i // 2, s] = ring.tile([P, 2, HALF], F32, name="staged")
+            pair = staged[i // 2, s]
+            y = bank(b, "y")
+            c, cols = i // 4, slice((i % 4) * P, (i % 4 + 1) * P)
+            nc.tensor.matmul_mx(
+                out=y[:],
+                lhsT=wo_codes[c][:, cols].bitcast(FP8X4),
+                lhsT_scale=wo_sc[c][:, cols],
+                rhs=h_codes[s][:].bitcast(FP8X4),
+                rhs_scale=h_sc[s][:],
+                start=True,
+                stop=True,
             )
+            if on_vector:
+                nc.vector.tensor_scalar(pair[:, i % 2, :], y[:], consts[:, i : i + 1], None, ALU.add)
+            else:
+                nc.scalar.activation(pair[:, i % 2, :], y[:], ACT.Identity, bias=consts[:, i : i + 1])
+            if i % 2 == 1:
+                dst = out[(i - 1) * P : (i + 1) * P, s * HALF : (s + 1) * HALF]
+                nc.sync.dma_start(dst.rearrange("(e p) n -> p e n", p=P), pair[:])
 
-        def first_layer(s, order, banks):
-            acc = [bank(b, "acc") for b in banks]
-            steps = [(u, a) for a in range(PASSES) for u in order]
-            for u, a in steps:
-                first_product(s, acc, u, a, (u, a) == steps[0], (u, a) == steps[-1])
-            return acc
-
-        for t in range(4):
-            cast_w1(0, t, nc.scalar.copy)
+        cast_w1(0)
+        turned = bank(7, "turned")
+        nc.tensor.transpose(turned[:, 0:P], rows[:], ident[:])
+        consts = held("consts", [P, 20], F32, "w1_raw0")
+        nc.scalar.copy(consts[:], turned[:, 108:128])
         reorder(w2_codes, w2_raw, 8)
         reorder(w3_codes, w3_raw, 4)
         for u in (2, 1, 0):
-            gather_scales(0, u)
-        for u in (1, 2, 0):
-            gather_words(0, u, 0)
-        reorder(w2_sc, w2_sc_raw, 2)
-        reorder(w3_sc, w3_sc_raw, 2)
-        quantize_w1(0, 1)
-        cast_wo(0, "wo_bf0", nc.scalar.copy, 1)
+            nc.vector.tensor_copy(x_sc[u][:], table_scales[:].bitcast(U8).indirect(lists[u][:]))
+        nc.gpsimd.dma_start(x3_sc_low[0:112, :], x_sc[2][4:116, :].bitcast(I32))
+        w_sc = held("w_sc", [P, PASSES, H // 4], I32, "table_scales")
+        reorder(w_sc, w_sc_raw, 2)
+        quantize_w1(0)
+        acc0 = [bank(b, "acc") for b in range(4)]
+        look_up_and_multiply(0, acc0, 0, (0, 1, 2), (0, 1, 2))
+        first_words = held("first_words", [P, HALF], U32)
+        gather_words(0, 0, 1, first_words[:])
+        look_up_and_multiply(0, acc0, 1, (1, 2), (3, 4))
+        cast_w1(1)
+        quantize_w1(1)
+        first_product(0, acc0, 0, 1, first_words[:], False, True)
+        acc1 = [bank(b, "acc") for b in range(4, 8)]
+        mid_words = held("mid_words", [P, 2, HALF], U32, "w1_bf1")
+        x_words.extend([mid_words[:, 0, :], mid_words[:, 1, :]])
+        look_up_and_multiply(1, acc1, 0, (0, 1, 2), (3, 5, 6))
+        cast_wo(0, nc.scalar.copy)
         quantize_wo(0)
-        for u in (1, 2, 0):
-            gather_words(0, u, 1)
-        for t in range(4):
-            cast_w1(1, t, nc.scalar.copy)
-        quantize_w1(1, 4)
-        acc = first_layer(0, (1, 2, 0), range(4))
-        hidden(0, acc)
-        cast_wo(1, "th0_0", nc.scalar.copy, 1)
+        th0 = [held("th0_%d" % v, [P, 4, SUB], F32, tag) for v, tag in enumerate(("wo_raw0", "th0_1"))]
+        squash(acc0, th0)
+        quantize_h(0, th0)
+        x_words.append(held("words_after_gain", [P, HALF], U32, "wo_raw0")[:])
+        look_up_and_multiply(1, acc1, 1, (0,), (7,))
+        cast_wo(1, nc.scalar.copy)
+        late = [held("late%d" % u, [P, HALF], U32, tag)[:] for u, tag in enumerate(("h_bf0", "wo_bf1"))]
+        gather_words(1, 1, 1, late[0])
         quantize_wo(1)
-        first_staged = held("first_staged", [P, 4, HALF], F32, "wo_raw1")
-        logits((0, 1), (0,), (6, 7), (False, False), first_staged[:, 0:2, :])
-        logits((2, 3), (0,), (2, 3), (False, False), first_staged[:, 2:4, :])
-        logits((4, 5), (0,), (6, 7), (False, False))
-
-        for u in range(3):
-            x_sc[1, u] = held("xs1_%d" % u, [P, HALF], U8)[:]
-        early_words = held("early_words", [P, 3, HALF], U32, "w1_raw0")
-        late_words = held("late_words", [P, 2, HALF], U32, "th0_0")
-        for u in range(3):
-            x_words[1, u, 0] = early_words[:, u, :]
-        x_words[1, 0, 1] = held("mid_words", [P, HALF], U32, "w1_bf1")[:]
-        for u in (1, 2):
-            x_words[1, u, 1] = late_words[:, u - 1, :]
-        for u in (2, 0, 1):
-            gather_scales(1, u)
-        for a in range(PASSES):
-            for u in range(3):
-                gather_words(1, u, a)
-        acc = first_layer(1, range(3), (4, 5, 0, 1))
-        cast_wo(2, "table1", nc.vector.tensor_copy, 1)
+        gather_words(1, 2, 1, late[1])
+        wo_bf[2] = held("wo_bf2", [P, 4 * CHUNK], BF16, "table1")
+        cast_wo(2, nc.vector.tensor_copy)
         quantize_wo(2)
-        h_bf[1] = held("h_bf1", [P, 2, 4 * SUB], BF16, "wo_raw2")
-        logits((6, 7), (0,), (2, 3), (False, True))
-        hidden(1, acc)
-        logits((8, 9), (0,), (6, 7), (False, False))
-        logits((10, 11), (0,), (2, 3), (False, False))
-        for pair in range(6):
-            logits((2 * pair, 2 * pair + 1), (1,), ((4, 5), (0, 1), (6, 7), (2, 3))[pair % 4], (True, False))
+        for i in range(4):
+            logits(i, 0, i % 4, False)
+        first_product(1, acc1, 1, 1, late[0], False, False)
+        for i in range(4, 6):
+            logits(i, 0, i % 4, False)
+        first_product(1, acc1, 2, 1, late[1], False, True)
+        for i in range(6, 8):
+            logits(i, 0, i % 4, False)
+
+        th1 = [held("th1_%d" % v, [P, 4, SUB], F32) for v in range(2)]
+        squash(acc1, th1)
+        quantize_h(1, th1)
+        for i in range(8, OUT_TILES):
+            logits(i, 0, i % 4, False)
+        for i in range(OUT_TILES):
+            logits(i, 1, (4 + i) % 8, i % 2 == 0)

@@ -71,6 +71,9 @@ def tile_list_trigram_next_logits_kernel(
         nc.vector.memset(x3_sc_low[96:128, :], 0)
         nc.vector.memset(rows[0:96, :], 0.0)
         nc.vector.memset(rows[96:108, :], 0.0)
+        nc.gpsimd.dma_start(rows[108:120, :], bo.rearrange("(i p) -> i p", p=P))
+        nc.gpsimd.dma_start(rows[120:124, :].rearrange("t (g q) -> t g q", q=8), bh.rearrange("(g t q) -> t g q", t=4, q=8))
+        nc.gpsimd.dma_start(rows[124:128, :].rearrange("t (g q) -> t g q", q=8), gain.rearrange("(g t q) -> t g q", t=4, q=8))
         make_identity(nc, ident[:])
         nc.scalar.activation(warm[:], ident[:, 0:1], ACT.Tanh)
 
@@ -80,6 +83,11 @@ def tile_list_trigram_next_logits_kernel(
                     w_sc_raw[32 * q + first : 32 * q + first + 4, :, :],
                     src[:, 4 * q : 4 * q + 4, :].bitcast(I32).rearrange("a r c -> r a c"),
                 )
+
+        def load_table_scales(a):
+            for q in range(4):
+                first = 32 * q + 4 * a
+                nc.sync.dma_start(table_scales[first : first + 4, :], tab_scales[a, 4 * q : 4 * q + 4, :].bitcast(I32))
 
         def load_table(a):
             nc.sync.dma_start(table[a][:], tab_words[a].rearrange("p t i -> p (t i)").bitcast(I32))
@@ -94,22 +102,15 @@ def tile_list_trigram_next_logits_kernel(
 
         for tile, src in zip(lists, (offs, offs2, offs3)):
             nc.sync.dma_start(tile[:], src)
-        for q in range(4):
-            nc.sync.dma_start(table_scales[32 * q : 32 * q + 8, :], tab_scales[:, 4 * q : 4 * q + 4, :].bitcast(I32))
+        load_table_scales(0)
         nc.sync.dma_start(w2_raw[:], w2_words.rearrange("a p c i -> p a (c i)").bitcast(I32))
+        load_table_scales(1)
         nc.sync.dma_start(w3_raw[:], w3_words.rearrange("a p b -> p a b").bitcast(I32))
         load_w1(0)
         load_weight_scales(4, w2_scales)
         load_table(0)
         load_weight_scales(0, w3_scales)
-        nc.gpsimd.dma_start(rows[108:120, :], bo.rearrange("(i p) -> i p", p=P))
-        nc.gpsimd.dma_start(rows[120:124, :].rearrange("t (g q) -> t g q", q=8), bh.rearrange("(g t q) -> t g q", t=4, q=8))
-        nc.gpsimd.dma_start(rows[124:128, :].rearrange("t (g q) -> t g q", q=8), gain.rearrange("(g t q) -> t g q", t=4, q=8))
         load_table(1)
-        load_w1(1)
-        load_wo(0)
-        load_wo(1)
-        load_wo(2)
 
 
         def gather_words(s, u, a, dst):
@@ -225,7 +226,10 @@ def tile_list_trigram_next_logits_kernel(
         reorder(w3_codes, w3_raw, 4)
         for u in (2, 1, 0):
             nc.vector.tensor_copy(x_sc[u][:], table_scales[:].bitcast(U8).indirect(lists[u][:]))
-        nc.gpsimd.dma_start(x3_sc_low[0:112, :], x_sc[2][4:116, :].bitcast(I32))
+        nc.sync.dma_start(x3_sc_low[0:112, :], x_sc[2][4:116, :].bitcast(I32))
+        load_w1(1)
+        for c in range(3):
+            load_wo(c)
         w_sc = held("w_sc", [P, PASSES, H // 4], I32, "table_scales")
         reorder(w_sc, w_sc_raw, 2)
         quantize_w1(0)

@@ -49,11 +49,9 @@ def tile_list_trigram_next_logits_kernel(
         w2_codes = held("w2_codes", [P, PASSES, H], I32)
         w3_codes = held("w3_codes", [P, PASSES, H // 2], I32)
         w_sc_raw = held("w_sc_raw", [P, PASSES, H // 4], I32)
-        wo_bf = [held("wo_bf%d" % c, [P, 4 * CHUNK], BF16) for c in range(2)] + [None]
-        wo_codes = [held("wo_codes%d" % c, [P, CHUNK], U32) for c in range(3)]
+        wo_codes = {c: held("wo_codes%d" % c, [P, CHUNK], U32) for c in (0, 2)}
         wo_sc = [held("wo_sc%d" % c, [P, CHUNK], U8) for c in range(3)]
         x_sc = [held("x_sc%d" % u, [P, S], U8) for u in range(3)]
-        x_words = [held("x_words%d" % b, [P, HALF], U32)[:] for b in range(5)]
         x3_sc_low = held("x3_sc_low", [P, S // 4], I32)
         h_bf = [held("h_bf%d" % s, [P, 2, 4 * SUB], BF16) for s in range(2)]
         h_codes = [held("h_codes%d" % s, [P, HALF], U32) for s in range(2)]
@@ -71,23 +69,18 @@ def tile_list_trigram_next_logits_kernel(
         nc.vector.memset(x3_sc_low[96:128, :], 0)
         nc.vector.memset(rows[0:96, :], 0.0)
         nc.vector.memset(rows[96:108, :], 0.0)
+        make_identity(nc, ident[:])
         nc.gpsimd.dma_start(rows[108:120, :], bo.rearrange("(i p) -> i p", p=P))
         nc.gpsimd.dma_start(rows[120:124, :].rearrange("t (g q) -> t g q", q=8), bh.rearrange("(g t q) -> t g q", t=4, q=8))
         nc.gpsimd.dma_start(rows[124:128, :].rearrange("t (g q) -> t g q", q=8), gain.rearrange("(g t q) -> t g q", t=4, q=8))
-        make_identity(nc, ident[:])
         nc.scalar.activation(warm[:], ident[:, 0:1], ACT.Tanh)
 
-        def load_weight_scales(first, src):
-            for q in range(4):
+        def load_weight_scales(first, src, quadrants):
+            for q in quadrants:
                 nc.sync.dma_start(
                     w_sc_raw[32 * q + first : 32 * q + first + 4, :, :],
                     src[:, 4 * q : 4 * q + 4, :].bitcast(I32).rearrange("a r c -> r a c"),
                 )
-
-        def load_table_scales(a):
-            for q in range(4):
-                first = 32 * q + 4 * a
-                nc.sync.dma_start(table_scales[first : first + 4, :], tab_scales[a, 4 * q : 4 * q + 4, :].bitcast(I32))
 
         def load_table(a):
             nc.sync.dma_start(table[a][:], tab_words[a].rearrange("p t i -> p (t i)").bitcast(I32))
@@ -102,14 +95,17 @@ def tile_list_trigram_next_logits_kernel(
 
         for tile, src in zip(lists, (offs, offs2, offs3)):
             nc.sync.dma_start(tile[:], src)
-        load_table_scales(0)
+        for a in range(PASSES):
+            for q in range(4):
+                first = 32 * q + 4 * a
+                nc.sync.dma_start(table_scales[first : first + 4, :], tab_scales[a, 4 * q : 4 * q + 4, :].bitcast(I32))
         nc.sync.dma_start(w2_raw[:], w2_words.rearrange("a p c i -> p a (c i)").bitcast(I32))
-        load_table_scales(1)
         nc.sync.dma_start(w3_raw[:], w3_words.rearrange("a p b -> p a b").bitcast(I32))
-        load_w1(0)
-        load_weight_scales(4, w2_scales)
+        load_weight_scales(4, w2_scales, range(3))
         load_table(0)
-        load_weight_scales(0, w3_scales)
+        load_weight_scales(4, w2_scales, range(3, 4))
+        load_weight_scales(0, w3_scales, range(4))
+        load_w1(0)
         load_table(1)
 
 
@@ -118,8 +114,8 @@ def tile_list_trigram_next_logits_kernel(
             nc.vector.tensor_copy(dst, table[a][:].bitcast(U32).indirect(picks))
 
         def cast_w1(a):
-            src = w1_raw[a][:].rearrange("p j (g t u i) -> p t g u j i", t=4, u=2, i=4)
-            dst = w1_bf[a][:].rearrange("p (t g u i j) -> p t g u j i", t=4, u=2, i=4, j=4)
+            src = w1_raw[a][:].rearrange("p j (g t u i) -> p t g u j i", t=4, u=4, i=2)
+            dst = w1_bf[a][:].rearrange("p (t g u i j) -> p t g u j i", t=4, u=4, i=2, j=4)
             for t in range(4):
                 nc.scalar.copy(dst[:, t], src[:, t])
 
@@ -160,11 +156,6 @@ def tile_list_trigram_next_logits_kernel(
                     stop=stop,
                 )
 
-        def look_up_and_multiply(s, acc, a, order, buffers):
-            for u, b in zip(order, buffers):
-                gather_words(s, u, a, x_words[b])
-                first_product(s, acc, u, a, x_words[b], a == 0 and u == order[0], False)
-
         def squash(acc, th):
             for v in range(2):
                 for t in range(4):
@@ -175,53 +166,53 @@ def tile_list_trigram_next_logits_kernel(
         def quantize_h(s, th):
             for v in range(2):
                 nc.vector.tensor_tensor(
-                    h_bf[s][:, v, :].rearrange("p (m i t) -> p m t i", i=4, t=4),
-                    th[v][:].rearrange("p t (m i) -> p m t i", i=4),
-                    consts[:, 16:20].unsqueeze(1).unsqueeze(3).to_broadcast([P, SUB // 4, 4, 4]),
+                    h_bf[s][:, v, :].rearrange("p (m i t) -> p m t i", i=2, t=4),
+                    th[v][:].rearrange("p t (m i) -> p m t i", i=2),
+                    consts[:, 16:20].unsqueeze(1).unsqueeze(3).to_broadcast([P, SUB // 2, 4, 2]),
                     ALU.mult,
                 )
             for v in range(2):
                 cols = slice(v * SUB, (v + 1) * SUB)
                 nc.vector.quantize_mx(out=h_codes[s][:, cols].bitcast(FP8X4), scales=h_sc[s][:, cols], in_=h_bf[s][:, v, :])
 
-        def cast_wo(c, copy):
+        def cast_wo(dst, c, cols, copy):
             copy(
-                wo_bf[c][:].rearrange("p (m i t) -> p m t i", i=4, t=4), wo_raw[c][:].rearrange("p t (m i) -> p m t i", i=4)
+                dst[:].rearrange("p (m i t) -> p m t i", i=2, t=4),
+                wo_raw[c][:, :, cols].rearrange("p t (m i) -> p m t i", i=2),
             )
 
-        def quantize_wo(c):
-            nc.vector.quantize_mx(out=wo_codes[c][:].bitcast(FP8X4), scales=wo_sc[c][:], in_=wo_bf[c][:])
+        def quantize_wo(c, cols, src):
+            nc.vector.quantize_mx(out=wo_codes[c][:, cols].bitcast(FP8X4), scales=wo_sc[c][:, cols], in_=src[:])
 
-        staged = {}
-
-        def logits(i, s, b, on_vector):
-            if i % 2 == 0:
-                staged[i // 2, s] = ring.tile([P, 2, HALF], F32, name="staged")
-            pair = staged[i // 2, s]
-            y = bank(b, "y")
-            c, cols = i // 4, slice((i % 4) * P, (i % 4 + 1) * P)
-            nc.tensor.matmul_mx(
-                out=y[:],
-                lhsT=wo_codes[c][:, cols].bitcast(FP8X4),
-                lhsT_scale=wo_sc[c][:, cols],
-                rhs=h_codes[s][:].bitcast(FP8X4),
-                rhs_scale=h_sc[s][:],
-                start=True,
-                stop=True,
+        def logits(parts, banks, on_vector):
+            staged = ring.tile([P, 2, HALF], F32, name="staged")
+            for e, (i, s) in enumerate(parts):
+                y = bank(banks[e], "y")
+                c, cols = i // 4, slice((i % 4) * P, (i % 4 + 1) * P)
+                nc.tensor.matmul_mx(
+                    out=y[:],
+                    lhsT=wo_codes[c][:, cols].bitcast(FP8X4),
+                    lhsT_scale=wo_sc[c][:, cols],
+                    rhs=h_codes[s][:].bitcast(FP8X4),
+                    rhs_scale=h_sc[s][:],
+                    start=True,
+                    stop=True,
+                )
+                if on_vector[e]:
+                    nc.vector.tensor_scalar(staged[:, e, :], y[:], consts[:, i : i + 1], None, ALU.add)
+                else:
+                    nc.scalar.activation(staged[:, e, :], y[:], ACT.Identity, bias=consts[:, i : i + 1])
+            (i0, s0), (i1, s1) = parts
+            dst = out[i0 * P : (i1 + 1) * P, s0 * HALF : (s1 + 1) * HALF]
+            nc.sync.dma_start(
+                dst.rearrange("(e p) n -> p e n", p=P), staged[:].rearrange("p (e s) n -> p e (s n)", s=s1 - s0 + 1)
             )
-            if on_vector:
-                nc.vector.tensor_scalar(pair[:, i % 2, :], y[:], consts[:, i : i + 1], None, ALU.add)
-            else:
-                nc.scalar.activation(pair[:, i % 2, :], y[:], ACT.Identity, bias=consts[:, i : i + 1])
-            if i % 2 == 1:
-                dst = out[(i - 1) * P : (i + 1) * P, s * HALF : (s + 1) * HALF]
-                nc.sync.dma_start(dst.rearrange("(e p) n -> p e n", p=P), pair[:])
 
-        cast_w1(0)
         turned = bank(7, "turned")
         nc.tensor.transpose(turned[:, 0:P], rows[:], ident[:])
-        consts = held("consts", [P, 20], F32, "w1_raw0")
+        consts = held("consts", [P, 20], F32)
         nc.scalar.copy(consts[:], turned[:, 108:128])
+        cast_w1(0)
         reorder(w2_codes, w2_raw, 8)
         reorder(w3_codes, w3_raw, 4)
         for u in (2, 1, 0):
@@ -232,47 +223,45 @@ def tile_list_trigram_next_logits_kernel(
             load_wo(c)
         w_sc = held("w_sc", [P, PASSES, H // 4], I32, "table_scales")
         reorder(w_sc, w_sc_raw, 2)
-        quantize_w1(0)
+        first_words = held("first_words", [P, 4, HALF], U32, "w_sc_raw")
+        second_words = held("second_words", [P, 4, HALF], U32)
         acc0 = [bank(b, "acc") for b in range(4)]
-        look_up_and_multiply(0, acc0, 0, (0, 1, 2), (0, 1, 2))
-        first_words = held("first_words", [P, HALF], U32)
-        gather_words(0, 0, 1, first_words[:])
-        look_up_and_multiply(0, acc0, 1, (1, 2), (3, 4))
-        cast_w1(1)
-        quantize_w1(1)
-        first_product(0, acc0, 0, 1, first_words[:], False, True)
         acc1 = [bank(b, "acc") for b in range(4, 8)]
-        mid_words = held("mid_words", [P, 2, HALF], U32, "w1_bf1")
-        x_words.extend([mid_words[:, 0, :], mid_words[:, 1, :]])
-        look_up_and_multiply(1, acc1, 0, (0, 1, 2), (3, 5, 6))
-        cast_wo(0, nc.scalar.copy)
-        quantize_wo(0)
+        for a, free in enumerate((first_words, second_words)):
+            for u in (1, 2, 0):
+                gather_words(0, u, a, free[:, u, :])
+            gather_words(1, 1, a, free[:, 3, :])
+            if a == 1:
+                cast_w1(1)
+            quantize_w1(a)
+            held_back = held("held_back%d" % a, [P, 2, HALF], U32, "w1_bf%d" % a)
+            gather_words(1, 2, a, held_back[:, 0, :])
+            gather_words(1, 0, a, held_back[:, 1, :])
+            for u in (1, 2, 0):
+                first_product(0, acc0, u, a, free[:, u, :], a == 0 and u == 1, a == 1 and u == 0)
+            for u, words in ((1, free[:, 3, :]), (2, held_back[:, 0, :]), (0, held_back[:, 1, :])):
+                first_product(1, acc1, u, a, words, a == 0 and u == 1, a == 1 and u == 0)
+        whole, low, high = slice(0, CHUNK), slice(0, CHUNK // 2), slice(CHUNK // 2, CHUNK)
+        wo0_bf = held("wo0_bf", [P, 4 * CHUNK], BF16)
+        cast_wo(wo0_bf, 0, whole, nc.scalar.copy)
+        quantize_wo(0, whole, wo0_bf)
         th0 = [held("th0_%d" % v, [P, 4, SUB], F32, tag) for v, tag in enumerate(("wo_raw0", "th0_1"))]
-        squash(acc0, th0)
-        quantize_h(0, th0)
-        x_words.append(held("words_after_gain", [P, HALF], U32, "wo_raw0")[:])
-        look_up_and_multiply(1, acc1, 1, (0,), (7,))
-        cast_wo(1, nc.scalar.copy)
-        late = [held("late%d" % u, [P, HALF], U32, tag)[:] for u, tag in enumerate(("h_bf0", "wo_bf1"))]
-        gather_words(1, 1, 1, late[0])
-        quantize_wo(1)
-        gather_words(1, 2, 1, late[1])
-        wo_bf[2] = held("wo_bf2", [P, 4 * CHUNK], BF16, "table1")
-        cast_wo(2, nc.vector.tensor_copy)
-        quantize_wo(2)
-        for i in range(4):
-            logits(i, 0, i % 4, False)
-        first_product(1, acc1, 1, 1, late[0], False, False)
-        for i in range(4, 6):
-            logits(i, 0, i % 4, False)
-        first_product(1, acc1, 2, 1, late[1], False, True)
-        for i in range(6, 8):
-            logits(i, 0, i % 4, False)
-
         th1 = [held("th1_%d" % v, [P, 4, SUB], F32) for v in range(2)]
+        squash(acc0, th0)
+        wo1_low_bf = held("wo1_low_bf", [P, 2 * CHUNK], BF16)
+        cast_wo(wo1_low_bf, 1, low, nc.scalar.copy)
         squash(acc1, th1)
+        quantize_h(0, th0)
         quantize_h(1, th1)
-        for i in range(8, OUT_TILES):
-            logits(i, 0, i % 4, False)
-        for i in range(OUT_TILES):
-            logits(i, 1, (4 + i) % 8, i % 2 == 0)
+        wo_codes[1] = held("wo_codes1", [P, CHUNK], U32, "h_bf0")
+        quantize_wo(1, low, wo1_low_bf)
+        wo1_high_bf = held("wo1_high_bf", [P, 2 * CHUNK], BF16, "th1_0")
+        cast_wo(wo1_high_bf, 1, high, nc.vector.tensor_copy)
+        wo2_bf = held("wo2_bf", [P, 4 * CHUNK], BF16, "th1_1")
+        cast_wo(wo2_bf, 2, whole, nc.vector.tensor_copy)
+        quantize_wo(1, high, wo1_high_bf)
+        quantize_wo(2, whole, wo2_bf)
+        pairs = [((i, s), (i + 1, s)) for s in range(2) for i in range(0, 4, 2)]
+        pairs.extend(((i, 0), (i, 1)) for i in range(4, OUT_TILES))
+        for n, parts in enumerate(pairs):
+            logits(parts, ((2 * n) % 8, (2 * n + 1) % 8), (n >= 6, False))

@@ -18,11 +18,19 @@ ACT = mybir.ActivationFunctionType
 ALU = mybir.AluOpType
 
 P = 128
-PASSES = 2
-HALF = 512
-SUB = 256
+PASSES = K // 512
+HALF = S // 2
+SUB = HALF // 2
 CHUNK = 512
 OUT_TILES = N // P
+EARLY_TILES = 6
+STORES = EARLY_TILES + EARLY_TILES // 2 + (OUT_TILES - EARLY_TILES)
+SCALAR_ONLY_PAIRS = 2
+BANKS = 8
+SHIFT = 4
+SHIFTED_ROWS = 112
+BO_ROW, BH_ROW, GAIN_ROW = 108, 120, 124
+BH_COL, GAIN_COL = BH_ROW - BO_ROW, GAIN_ROW - BO_ROW
 
 
 def tile_list_trigram_next_logits_kernel(
@@ -31,7 +39,7 @@ def tile_list_trigram_next_logits_kernel(
     nc = tc.nc
     with ExitStack() as ctx:
         keep = ctx.enter_context(tc.tile_pool(name="keep", bufs=1))
-        ring = ctx.enter_context(tc.tile_pool(name="ring", bufs=12))
+        ring = ctx.enter_context(tc.tile_pool(name="ring", bufs=STORES))
         psum = ctx.enter_context(tc.psum_pool(name="psum", bufs=1))
 
         def held(name, shape, dtype, tag=None):
@@ -49,7 +57,7 @@ def tile_list_trigram_next_logits_kernel(
         w2_codes = held("w2_codes", [P, PASSES, H], I32)
         w3_codes = held("w3_codes", [P, PASSES, H // 2], I32)
         w_sc_raw = held("w_sc_raw", [P, PASSES, H // 4], I32)
-        wo_codes = {c: held("wo_codes%d" % c, [P, CHUNK], U32) for c in (0, 2)}
+        wo_codes = [held("wo_codes%d" % c, [P, CHUNK], U32) for c in range(3)]
         wo_sc = [held("wo_sc%d" % c, [P, CHUNK], U8) for c in range(3)]
         x_sc = [held("x_sc%d" % u, [P, S], U8) for u in range(3)]
         x3_sc_low = held("x3_sc_low", [P, S // 4], I32)
@@ -58,7 +66,6 @@ def tile_list_trigram_next_logits_kernel(
         h_sc = [held("h_sc%d" % s, [P, HALF], U8) for s in range(2)]
         table = [held("table%d" % a, [P, T], I32) for a in range(PASSES)]
         rows = held("rows", [P, P], F32)
-        warm = held("warm", [P, 1], F32)
         w1_raw = [held("w1_raw%d" % a, [P, 4, H], F32) for a in range(PASSES)]
         w2_raw = held("w2_raw", [P, PASSES, H], I32)
         w3_raw = held("w3_raw", [P, PASSES, H // 2], I32)
@@ -66,14 +73,16 @@ def tile_list_trigram_next_logits_kernel(
 
         nc.vector.memset(table_scales[:], 0)
         nc.vector.memset(w_sc_raw[:], 0)
-        nc.vector.memset(x3_sc_low[96:128, :], 0)
-        nc.vector.memset(rows[0:96, :], 0.0)
-        nc.vector.memset(rows[96:108, :], 0.0)
+        nc.vector.memset(x3_sc_low[96:P, :], 0)
+        nc.vector.memset(rows[96:BO_ROW, :], 0.0)
         make_identity(nc, ident[:])
-        nc.gpsimd.dma_start(rows[108:120, :], bo.rearrange("(i p) -> i p", p=P))
-        nc.gpsimd.dma_start(rows[120:124, :].rearrange("t (g q) -> t g q", q=8), bh.rearrange("(g t q) -> t g q", t=4, q=8))
-        nc.gpsimd.dma_start(rows[124:128, :].rearrange("t (g q) -> t g q", q=8), gain.rearrange("(g t q) -> t g q", t=4, q=8))
-        nc.scalar.activation(warm[:], ident[:, 0:1], ACT.Tanh)
+        nc.gpsimd.dma_start(rows[BO_ROW:BH_ROW, :], bo.rearrange("(i p) -> i p", p=P))
+        for first, vector in ((BH_ROW, bh), (GAIN_ROW, gain)):
+            nc.gpsimd.dma_start(
+                rows[first : first + 4, :].rearrange("t (g q) -> t g q", q=8),
+                vector.rearrange("(g t q) -> t g q", t=4, q=8),
+            )
+        nc.scalar.activation(rows[0:96, :], ident[0:96, :], ACT.Tanh, scale=0.0)
 
         def load_weight_scales(first, src, quadrants):
             for q in quadrants:
@@ -97,20 +106,22 @@ def tile_list_trigram_next_logits_kernel(
             nc.sync.dma_start(tile[:], src)
         for a in range(PASSES):
             for q in range(4):
-                first = 32 * q + 4 * a
+                first = 32 * q + SHIFT * a
                 nc.sync.dma_start(table_scales[first : first + 4, :], tab_scales[a, 4 * q : 4 * q + 4, :].bitcast(I32))
+        load_table(0)
         nc.sync.dma_start(w2_raw[:], w2_words.rearrange("a p c i -> p a (c i)").bitcast(I32))
         nc.sync.dma_start(w3_raw[:], w3_words.rearrange("a p b -> p a b").bitcast(I32))
-        load_weight_scales(4, w2_scales, range(3))
-        load_table(0)
-        load_weight_scales(4, w2_scales, range(3, 4))
-        load_weight_scales(0, w3_scales, range(4))
+        load_weight_scales(SHIFT, w2_scales, range(4))
+        load_weight_scales(0, w3_scales, range(1))
         load_w1(0)
+        load_weight_scales(0, w3_scales, range(1, 4))
         load_table(1)
 
+        everyone = slice(0, S)
+        halves = [slice(0, HALF), slice(HALF, S)]
 
-        def gather_words(s, u, a, dst):
-            picks = lists[u][:, s * (HALF // 16) : (s + 1) * (HALF // 16)]
+        def gather_words(contexts, u, a, dst):
+            picks = lists[u][:, contexts.start // 16 : contexts.stop // 16]
             nc.vector.tensor_copy(dst, table[a][:].bitcast(U32).indirect(picks))
 
         def cast_w1(a):
@@ -129,23 +140,22 @@ def tile_list_trigram_next_logits_kernel(
             )
 
         def first_product(s, acc, u, a, x_words, start, stop):
-            cols = slice(s * HALF, (s + 1) * HALF)
             for t in range(4):
                 if u == 0:
                     lhs = w1_codes[a][:, t * P : (t + 1) * P].bitcast(FP8X4)
                     lhs_sc = w1_sc[a][:, t * P : (t + 1) * P]
                 elif u == 1:
                     lhs = w2_codes[:, a, t * P : (t + 1) * P].bitcast(FP8X4)
-                    lhs_sc = w_sc[4:128, a, t * 32 : (t + 1) * 32].bitcast(U8)
+                    lhs_sc = w_sc[SHIFT:P, a, t * 32 : (t + 1) * 32].bitcast(U8)
                 else:
                     lhs = w3_codes[:, a, t * 64 : (t + 1) * 64].bitcast(U8).bitcast(FP4X4)
                     lhs_sc = w_sc[:, a, t * 32 : (t + 1) * 32].bitcast(U8)
                 if a == 0:
-                    rhs_sc = x_sc[u][:, cols]
+                    rhs_sc = x_sc[u][:, halves[s]]
                 elif u == 2:
-                    rhs_sc = x3_sc_low[:].bitcast(U8)[:, cols]
+                    rhs_sc = x3_sc_low[:].bitcast(U8)[:, halves[s]]
                 else:
-                    rhs_sc = x_sc[u][4:128, cols]
+                    rhs_sc = x_sc[u][SHIFT:P, halves[s]]
                 nc.tensor.matmul_mx(
                     out=acc[t][:],
                     lhsT=lhs,
@@ -160,15 +170,19 @@ def tile_list_trigram_next_logits_kernel(
             for v in range(2):
                 for t in range(4):
                     nc.scalar.activation(
-                        th[v][:, t, :], acc[t][:, v * SUB : (v + 1) * SUB], ACT.Tanh, bias=consts[:, 12 + t : 13 + t]
+                        th[v][:, t, :],
+                        acc[t][:, v * SUB : (v + 1) * SUB],
+                        ACT.Tanh,
+                        bias=consts[:, BH_COL + t : BH_COL + t + 1],
                     )
 
         def quantize_h(s, th):
+            gains = consts[:, GAIN_COL : GAIN_COL + 4].unsqueeze(1).unsqueeze(3).to_broadcast([P, SUB // 2, 4, 2])
             for v in range(2):
                 nc.vector.tensor_tensor(
                     h_bf[s][:, v, :].rearrange("p (m i t) -> p m t i", i=2, t=4),
                     th[v][:].rearrange("p t (m i) -> p m t i", i=2),
-                    consts[:, 16:20].unsqueeze(1).unsqueeze(3).to_broadcast([P, SUB // 2, 4, 2]),
+                    gains,
                     ALU.mult,
                 )
             for v in range(2):
@@ -185,7 +199,7 @@ def tile_list_trigram_next_logits_kernel(
             nc.vector.quantize_mx(out=wo_codes[c][:, cols].bitcast(FP8X4), scales=wo_sc[c][:, cols], in_=src[:])
 
         def logits(parts, banks, on_vector):
-            staged = ring.tile([P, 2, HALF], F32, name="staged")
+            staged = ring.tile([P, len(parts), HALF], F32, name="staged")
             for e, (i, s) in enumerate(parts):
                 y = bank(banks[e], "y")
                 c, cols = i // 4, slice((i % 4) * P, (i % 4 + 1) * P)
@@ -202,45 +216,55 @@ def tile_list_trigram_next_logits_kernel(
                     nc.vector.tensor_scalar(staged[:, e, :], y[:], consts[:, i : i + 1], None, ALU.add)
                 else:
                     nc.scalar.activation(staged[:, e, :], y[:], ACT.Identity, bias=consts[:, i : i + 1])
-            (i0, s0), (i1, s1) = parts
+            (i0, s0), (i1, s1) = parts[0], parts[-1]
             dst = out[i0 * P : (i1 + 1) * P, s0 * HALF : (s1 + 1) * HALF]
             nc.sync.dma_start(
                 dst.rearrange("(e p) n -> p e n", p=P), staged[:].rearrange("p (e s) n -> p e (s n)", s=s1 - s0 + 1)
             )
 
-        turned = bank(7, "turned")
+        turned = bank(BANKS - 1, "turned")
         nc.tensor.transpose(turned[:, 0:P], rows[:], ident[:])
-        consts = held("consts", [P, 20], F32)
-        nc.scalar.copy(consts[:], turned[:, 108:128])
+        consts = held("consts", [P, P - BO_ROW], F32)
+        nc.scalar.copy(consts[:], turned[:, BO_ROW:P])
         cast_w1(0)
         reorder(w2_codes, w2_raw, 8)
         reorder(w3_codes, w3_raw, 4)
         for u in (2, 1, 0):
             nc.vector.tensor_copy(x_sc[u][:], table_scales[:].bitcast(U8).indirect(lists[u][:]))
-        nc.sync.dma_start(x3_sc_low[0:112, :], x_sc[2][4:116, :].bitcast(I32))
+        nc.sync.dma_start(x3_sc_low[0:SHIFTED_ROWS, :], x_sc[2][SHIFT : SHIFT + SHIFTED_ROWS, :].bitcast(I32))
         load_w1(1)
         for c in range(3):
             load_wo(c)
-        w_sc = held("w_sc", [P, PASSES, H // 4], I32, "table_scales")
+
+        words_of_w2 = held("words_of_w2", [P, S], U32)
+        gather_words(everyone, 1, 0, words_of_w2[:])
+        w_sc = held("w_sc", [P, PASSES, H // 4], I32)
         reorder(w_sc, w_sc_raw, 2)
-        first_words = held("first_words", [P, 4, HALF], U32, "w_sc_raw")
-        second_words = held("second_words", [P, 4, HALF], U32)
+        words_behind_scales = held("words_behind_scales", [P, 2, S], U32, "w_sc_raw")
+        first_words = [words_behind_scales[:, 1, :], words_of_w2[:], words_behind_scales[:, 0, :]]
         acc0 = [bank(b, "acc") for b in range(4)]
-        acc1 = [bank(b, "acc") for b in range(4, 8)]
-        for a, free in enumerate((first_words, second_words)):
-            for u in (1, 2, 0):
-                gather_words(0, u, a, free[:, u, :])
-            gather_words(1, 1, a, free[:, 3, :])
-            if a == 1:
-                cast_w1(1)
-            quantize_w1(a)
-            held_back = held("held_back%d" % a, [P, 2, HALF], U32, "w1_bf%d" % a)
-            gather_words(1, 2, a, held_back[:, 0, :])
-            gather_words(1, 0, a, held_back[:, 1, :])
-            for u in (1, 2, 0):
-                first_product(0, acc0, u, a, free[:, u, :], a == 0 and u == 1, a == 1 and u == 0)
-            for u, words in ((1, free[:, 3, :]), (2, held_back[:, 0, :]), (0, held_back[:, 1, :])):
-                first_product(1, acc1, u, a, words, a == 0 and u == 1, a == 1 and u == 0)
+        acc1 = [bank(b, "acc") for b in range(4, BANKS)]
+        for u in (2, 0):
+            gather_words(everyone, u, 0, first_words[u])
+        quantize_w1(0)
+        for u in (1, 2, 0):
+            for s, acc in enumerate((acc0, acc1)):
+                first_product(s, acc, u, 0, first_words[u][:, halves[s]], u == 1, False)
+
+        second_words = held("second_words", [P, 4, HALF], U32)
+        for u in (1, 2, 0):
+            gather_words(halves[0], u, 1, second_words[:, u, :])
+        gather_words(halves[1], 1, 1, second_words[:, 3, :])
+        cast_w1(1)
+        quantize_w1(1)
+        last_words = held("last_words", [P, 2, HALF], U32, "w1_bf1")
+        gather_words(halves[1], 2, 1, last_words[:, 0, :])
+        gather_words(halves[1], 0, 1, last_words[:, 1, :])
+        for u in (1, 2, 0):
+            first_product(0, acc0, u, 1, second_words[:, u, :], False, u == 0)
+        for u, words in ((1, second_words[:, 3, :]), (2, last_words[:, 0, :]), (0, last_words[:, 1, :])):
+            first_product(1, acc1, u, 1, words, False, u == 0)
+
         whole, low, high = slice(0, CHUNK), slice(0, CHUNK // 2), slice(CHUNK // 2, CHUNK)
         wo0_bf = held("wo0_bf", [P, 4 * CHUNK], BF16)
         cast_wo(wo0_bf, 0, whole, nc.scalar.copy)
@@ -248,20 +272,23 @@ def tile_list_trigram_next_logits_kernel(
         th0 = [held("th0_%d" % v, [P, 4, SUB], F32, tag) for v, tag in enumerate(("wo_raw0", "th0_1"))]
         th1 = [held("th1_%d" % v, [P, 4, SUB], F32) for v in range(2)]
         squash(acc0, th0)
-        wo1_low_bf = held("wo1_low_bf", [P, 2 * CHUNK], BF16)
-        cast_wo(wo1_low_bf, 1, low, nc.scalar.copy)
         squash(acc1, th1)
         quantize_h(0, th0)
-        quantize_h(1, th1)
-        wo_codes[1] = held("wo_codes1", [P, CHUNK], U32, "h_bf0")
+        wo1_low_bf = held("wo1_low_bf", [P, 2 * CHUNK], BF16, "th0_1")
+        cast_wo(wo1_low_bf, 1, low, nc.vector.tensor_copy)
         quantize_wo(1, low, wo1_low_bf)
+        quantize_h(1, th1)
         wo1_high_bf = held("wo1_high_bf", [P, 2 * CHUNK], BF16, "th1_0")
         cast_wo(wo1_high_bf, 1, high, nc.vector.tensor_copy)
         wo2_bf = held("wo2_bf", [P, 4 * CHUNK], BF16, "th1_1")
         cast_wo(wo2_bf, 2, whole, nc.vector.tensor_copy)
         quantize_wo(1, high, wo1_high_bf)
         quantize_wo(2, whole, wo2_bf)
-        pairs = [((i, s), (i + 1, s)) for s in range(2) for i in range(0, 4, 2)]
-        pairs.extend(((i, 0), (i, 1)) for i in range(4, OUT_TILES))
+
+        for i in range(EARLY_TILES):
+            logits([(i, 0)], [i], [False])
+        pairs = [((i, 1), (i + 1, 1)) for i in range(0, EARLY_TILES, 2)]
+        pairs.extend(((i, 0), (i, 1)) for i in range(EARLY_TILES, OUT_TILES))
         for n, parts in enumerate(pairs):
-            logits(parts, ((2 * n) % 8, (2 * n + 1) % 8), (n >= 6, False))
+            b = (EARLY_TILES + 2 * n) % BANKS
+            logits(parts, (b, b + 1), (n >= SCALAR_ONLY_PAIRS, False))

@@ -24,11 +24,10 @@ SUB = HALF // 2
 CHUNK = 512
 OUT_TILES = N // P
 EARLY_TILES = 6
-STORES = EARLY_TILES + EARLY_TILES // 2 + (OUT_TILES - EARLY_TILES)
-SCALAR_ONLY_PAIRS = 2
+SCALAR_ONLY_PAIRS = 3
 BANKS = 8
 SHIFT = 4
-SHIFTED_ROWS = 112
+STAGE_ROW = 96
 BO_ROW, BH_ROW, GAIN_ROW = 108, 120, 124
 BH_COL, GAIN_COL = BH_ROW - BO_ROW, GAIN_ROW - BO_ROW
 
@@ -39,7 +38,6 @@ def tile_list_trigram_next_logits_kernel(
     nc = tc.nc
     with ExitStack() as ctx:
         keep = ctx.enter_context(tc.tile_pool(name="keep", bufs=1))
-        ring = ctx.enter_context(tc.tile_pool(name="ring", bufs=STORES))
         psum = ctx.enter_context(tc.psum_pool(name="psum", bufs=1))
 
         def held(name, shape, dtype, tag=None):
@@ -50,6 +48,8 @@ def tile_list_trigram_next_logits_kernel(
 
         lists = [held("list%d" % u, [P, S // 16], U16) for u in range(3)]
         table_scales = held("table_scales", [P, T // 4], I32)
+        picked_scales = held("picked_scales", [P, 3 * S], U8)
+        planes = [held("planes%d" % a, [P, 3 * S // 4], I32) for a in range(PASSES)]
         ident = held("ident", [P, P], F32)
         w1_bf = [held("w1_bf%d" % a, [P, 4 * H], BF16) for a in range(PASSES)]
         w1_codes = [held("w1_codes%d" % a, [P, H], U32) for a in range(PASSES)]
@@ -57,10 +57,9 @@ def tile_list_trigram_next_logits_kernel(
         w2_codes = held("w2_codes", [P, PASSES, H], I32)
         w3_codes = held("w3_codes", [P, PASSES, H // 2], I32)
         w_sc_raw = held("w_sc_raw", [P, PASSES, H // 4], I32)
-        wo_codes = [held("wo_codes%d" % c, [P, CHUNK], U32) for c in range(3)]
-        wo_sc = [held("wo_sc%d" % c, [P, CHUNK], U8) for c in range(3)]
-        x_sc = [held("x_sc%d" % u, [P, S], U8) for u in range(3)]
-        x3_sc_low = held("x3_sc_low", [P, S // 4], I32)
+        w_sc = held("w_sc", [P, PASSES, H // 4], I32)
+        wo_codes = held("wo_codes", [P, N], U32)
+        wo_sc = held("wo_sc", [P, N], U8)
         h_bf = [held("h_bf%d" % s, [P, 2, 4 * SUB], BF16) for s in range(2)]
         h_codes = [held("h_codes%d" % s, [P, HALF], U32) for s in range(2)]
         h_sc = [held("h_sc%d" % s, [P, HALF], U8) for s in range(2)]
@@ -69,12 +68,14 @@ def tile_list_trigram_next_logits_kernel(
         w1_raw = [held("w1_raw%d" % a, [P, 4, H], F32) for a in range(PASSES)]
         w2_raw = held("w2_raw", [P, PASSES, H], I32)
         w3_raw = held("w3_raw", [P, PASSES, H // 2], I32)
-        wo_raw = [held("wo_raw%d" % c, [P, 4, CHUNK], F32) for c in range(3)]
+        wo_first = held("wo_first", [P, 4, CHUNK], F32)
+        wo_rest = held("wo_rest", [P, 4, N - CHUNK], F32)
 
-        nc.vector.memset(table_scales[:], 0)
         nc.vector.memset(w_sc_raw[:], 0)
-        nc.vector.memset(x3_sc_low[96:P, :], 0)
-        nc.vector.memset(rows[96:BO_ROW, :], 0.0)
+        nc.vector.memset(table_scales[0:STAGE_ROW, :], 0)
+        nc.gpsimd.memset(rows[96:BO_ROW, :], 0.0)
+        for a in range(PASSES):
+            nc.gpsimd.memset(planes[a][:], 0)
         make_identity(nc, ident[:])
         nc.gpsimd.dma_start(rows[BO_ROW:BH_ROW, :], bo.rearrange("(i p) -> i p", p=P))
         for first, vector in ((BH_ROW, bh), (GAIN_ROW, gain)):
@@ -97,25 +98,27 @@ def tile_list_trigram_next_logits_kernel(
         def load_w1(a):
             nc.sync.dma_start(w1_raw[a][:], w1[a * 512 : (a + 1) * 512, :].rearrange("(p j) c -> p j c", j=4))
 
-        def load_wo(c):
-            src = wo[:, c * CHUNK : (c + 1) * CHUNK].rearrange("(g t q) n -> t g q n", t=4, q=8)
+        def load_wo(dst, cols):
+            src = wo[:, cols].rearrange("(g t q) n -> t g q n", t=4, q=8)
             for t in range(4):
-                nc.sync.dma_start(wo_raw[c][:, t, :], src[t])
+                nc.sync.dma_start(dst[:, t, :], src[t])
 
-        for tile, src in zip(lists, (offs, offs2, offs3)):
-            nc.sync.dma_start(tile[:], src)
-        for a in range(PASSES):
+        def move_planes(a):
             for q in range(4):
-                first = 32 * q + SHIFT * a
-                nc.sync.dma_start(table_scales[first : first + 4, :], tab_scales[a, 4 * q : 4 * q + 4, :].bitcast(I32))
-        load_table(0)
-        nc.sync.dma_start(w2_raw[:], w2_words.rearrange("a p c i -> p a (c i)").bitcast(I32))
-        nc.sync.dma_start(w3_raw[:], w3_words.rearrange("a p b -> p a b").bitcast(I32))
-        load_weight_scales(SHIFT, w2_scales, range(4))
-        load_weight_scales(0, w3_scales, range(1))
+                first = STAGE_ROW + 16 * a + 4 * q
+                nc.sync.dma_start(planes[a][32 * q : 32 * q + 4, :], picked_scales[first : first + 4, :].bitcast(I32))
+
+        nc.sync.dma_start(table_scales[STAGE_ROW:P, :], tab_scales.rearrange("a q t -> (a q) t").bitcast(I32))
+        nc.sync.dma_start(lists[0][:], offs)
+        nc.sync.dma_start(lists[1][:], offs2)
         load_w1(0)
-        load_weight_scales(0, w3_scales, range(1, 4))
-        load_table(1)
+        nc.sync.dma_start(lists[2][:], offs3)
+        load_weight_scales(SHIFT, w2_scales, range(4))
+        load_table(0)
+        load_weight_scales(0, w3_scales, range(4))
+        nc.sync.dma_start(w3_raw[:], w3_words.rearrange("a p b -> p a b").bitcast(I32))
+        nc.sync.dma_start(w2_raw[:], w2_words.rearrange("a p c i -> p a (c i)").bitcast(I32))
+        load_w1(1)
 
         everyone = slice(0, S)
         halves = [slice(0, HALF), slice(HALF, S)]
@@ -150,18 +153,12 @@ def tile_list_trigram_next_logits_kernel(
                 else:
                     lhs = w3_codes[:, a, t * 64 : (t + 1) * 64].bitcast(U8).bitcast(FP4X4)
                     lhs_sc = w_sc[:, a, t * 32 : (t + 1) * 32].bitcast(U8)
-                if a == 0:
-                    rhs_sc = x_sc[u][:, halves[s]]
-                elif u == 2:
-                    rhs_sc = x3_sc_low[:].bitcast(U8)[:, halves[s]]
-                else:
-                    rhs_sc = x_sc[u][SHIFT:P, halves[s]]
                 nc.tensor.matmul_mx(
                     out=acc[t][:],
                     lhsT=lhs,
                     lhsT_scale=lhs_sc,
                     rhs=x_words.bitcast(FP8X4),
-                    rhs_scale=rhs_sc,
+                    rhs_scale=planes[a][:].bitcast(U8)[:, u * S + s * HALF : u * S + (s + 1) * HALF],
                     start=start,
                     stop=stop,
                 )
@@ -176,37 +173,34 @@ def tile_list_trigram_next_logits_kernel(
                         bias=consts[:, BH_COL + t : BH_COL + t + 1],
                     )
 
-        def quantize_h(s, th):
+        def apply_gain(s, v, th):
             gains = consts[:, GAIN_COL : GAIN_COL + 4].unsqueeze(1).unsqueeze(3).to_broadcast([P, SUB // 2, 4, 2])
-            for v in range(2):
-                nc.vector.tensor_tensor(
-                    h_bf[s][:, v, :].rearrange("p (m i t) -> p m t i", i=2, t=4),
-                    th[v][:].rearrange("p t (m i) -> p m t i", i=2),
-                    gains,
-                    ALU.mult,
-                )
-            for v in range(2):
-                cols = slice(v * SUB, (v + 1) * SUB)
-                nc.vector.quantize_mx(out=h_codes[s][:, cols].bitcast(FP8X4), scales=h_sc[s][:, cols], in_=h_bf[s][:, v, :])
-
-        def cast_wo(dst, c, cols, copy):
-            copy(
-                dst[:].rearrange("p (m i t) -> p m t i", i=2, t=4),
-                wo_raw[c][:, :, cols].rearrange("p t (m i) -> p m t i", i=2),
+            nc.vector.tensor_tensor(
+                h_bf[s][:, v, :].rearrange("p (m i t) -> p m t i", i=2, t=4),
+                th[v][:].rearrange("p t (m i) -> p m t i", i=2),
+                gains,
+                ALU.mult,
             )
 
-        def quantize_wo(c, cols, src):
-            nc.vector.quantize_mx(out=wo_codes[c][:, cols].bitcast(FP8X4), scales=wo_sc[c][:, cols], in_=src[:])
+        def quantize_h(s, v):
+            cols = slice(v * SUB, (v + 1) * SUB)
+            nc.vector.quantize_mx(out=h_codes[s][:, cols].bitcast(FP8X4), scales=h_sc[s][:, cols], in_=h_bf[s][:, v, :])
 
-        def logits(parts, banks, on_vector):
-            staged = ring.tile([P, len(parts), HALF], F32, name="staged")
+        def cast_wo(dst, src, copy):
+            copy(dst.rearrange("p (m i t) -> p m t i", i=2, t=4), src.rearrange("p t (m i) -> p m t i", i=2))
+
+        def quantize_wo(cols, src):
+            nc.vector.quantize_mx(out=wo_codes[:, cols].bitcast(FP8X4), scales=wo_sc[:, cols], in_=src)
+
+        def logits(n, parts, banks, on_vector):
+            staged = held("staged%d" % n, [P, len(parts), HALF], F32)
             for e, (i, s) in enumerate(parts):
                 y = bank(banks[e], "y")
-                c, cols = i // 4, slice((i % 4) * P, (i % 4 + 1) * P)
+                cols = slice(i * P, (i + 1) * P)
                 nc.tensor.matmul_mx(
                     out=y[:],
-                    lhsT=wo_codes[c][:, cols].bitcast(FP8X4),
-                    lhsT_scale=wo_sc[c][:, cols],
+                    lhsT=wo_codes[:, cols].bitcast(FP8X4),
+                    lhsT_scale=wo_sc[:, cols],
                     rhs=h_codes[s][:].bitcast(FP8X4),
                     rhs_scale=h_sc[s][:],
                     start=True,
@@ -222,73 +216,77 @@ def tile_list_trigram_next_logits_kernel(
                 dst.rearrange("(e p) n -> p e n", p=P), staged[:].rearrange("p (e s) n -> p e (s n)", s=s1 - s0 + 1)
             )
 
+        for u in range(3):
+            nc.vector.tensor_copy(
+                picked_scales[:, u * S : (u + 1) * S], table_scales[:].bitcast(U8).indirect(lists[u][:])
+            )
+        move_planes(0)
+        load_table(1)
+        move_planes(1)
+        load_wo(wo_first, slice(0, CHUNK))
+        load_wo(wo_rest, slice(CHUNK, N))
+        for a in range(PASSES):
+            cast_w1(a)
+            quantize_w1(a)
+
         turned = bank(BANKS - 1, "turned")
         nc.tensor.transpose(turned[:, 0:P], rows[:], ident[:])
         consts = held("consts", [P, P - BO_ROW], F32)
         nc.scalar.copy(consts[:], turned[:, BO_ROW:P])
-        cast_w1(0)
-        reorder(w2_codes, w2_raw, 8)
-        reorder(w3_codes, w3_raw, 4)
-        for u in (2, 1, 0):
-            nc.vector.tensor_copy(x_sc[u][:], table_scales[:].bitcast(U8).indirect(lists[u][:]))
-        nc.sync.dma_start(x3_sc_low[0:SHIFTED_ROWS, :], x_sc[2][SHIFT : SHIFT + SHIFTED_ROWS, :].bitcast(I32))
-        load_w1(1)
-        for c in range(3):
-            load_wo(c)
 
-        words_of_w2 = held("words_of_w2", [P, S], U32)
-        gather_words(everyone, 1, 0, words_of_w2[:])
-        w_sc = held("w_sc", [P, PASSES, H // 4], I32)
-        reorder(w_sc, w_sc_raw, 2)
-        words_behind_scales = held("words_behind_scales", [P, 2, S], U32, "w_sc_raw")
-        first_words = [words_behind_scales[:, 1, :], words_of_w2[:], words_behind_scales[:, 0, :]]
         acc0 = [bank(b, "acc") for b in range(4)]
         acc1 = [bank(b, "acc") for b in range(4, BANKS)]
-        for u in (2, 0):
+        words0 = held("words0", [P, S], U32)
+        gather_words(everyone, 0, 0, words0[:])
+        reorder(w_sc, w_sc_raw, 2)
+        reorder(w3_codes, w3_raw, 4)
+        reorder(w2_codes, w2_raw, 8)
+        words12 = held("words12", [P, 2, S], U32, "w2_raw")
+        first_words = [words0[:], words12[:, 0, :], words12[:, 1, :]]
+        for u in (1, 2):
             gather_words(everyone, u, 0, first_words[u])
-        quantize_w1(0)
-        for u in (1, 2, 0):
+        for u in range(3):
             for s, acc in enumerate((acc0, acc1)):
-                first_product(s, acc, u, 0, first_words[u][:, halves[s]], u == 1, False)
+                first_product(s, acc, u, 0, first_words[u][:, halves[s]], u == 0, False)
 
-        second_words = held("second_words", [P, 4, HALF], U32)
-        for u in (1, 2, 0):
-            gather_words(halves[0], u, 1, second_words[:, u, :])
-        gather_words(halves[1], 1, 1, second_words[:, 3, :])
-        cast_w1(1)
-        quantize_w1(1)
-        last_words = held("last_words", [P, 2, HALF], U32, "w1_bf1")
-        gather_words(halves[1], 2, 1, last_words[:, 0, :])
-        gather_words(halves[1], 0, 1, last_words[:, 1, :])
-        for u in (1, 2, 0):
-            first_product(0, acc0, u, 1, second_words[:, u, :], False, u == 0)
-        for u, words in ((1, second_words[:, 3, :]), (2, last_words[:, 0, :]), (0, last_words[:, 1, :])):
-            first_product(1, acc1, u, 1, words, False, u == 0)
+        second_words = held("second_words", [P, 6, HALF], U32)
+        for s, acc in enumerate((acc0, acc1)):
+            for u in range(3):
+                gather_words(halves[s], u, 1, second_words[:, 3 * s + u, :])
+        for s, acc in enumerate((acc0, acc1)):
+            for u in range(3):
+                first_product(s, acc, u, 1, second_words[:, 3 * s + u, :], False, u == 2)
 
-        whole, low, high = slice(0, CHUNK), slice(0, CHUNK // 2), slice(CHUNK // 2, CHUNK)
         wo0_bf = held("wo0_bf", [P, 4 * CHUNK], BF16)
-        cast_wo(wo0_bf, 0, whole, nc.scalar.copy)
-        quantize_wo(0, whole, wo0_bf)
-        th0 = [held("th0_%d" % v, [P, 4, SUB], F32, tag) for v, tag in enumerate(("wo_raw0", "th0_1"))]
+        cast_wo(wo0_bf[:], wo_first[:], nc.scalar.copy)
+        quantize_wo(slice(0, 256), wo0_bf[:, 0:1024])
+        th0 = [held("th0_%d" % v, [P, 4, SUB], F32, tag) for v, tag in enumerate(("wo_first", "th0_1"))]
         th1 = [held("th1_%d" % v, [P, 4, SUB], F32) for v in range(2)]
         squash(acc0, th0)
         squash(acc1, th1)
-        quantize_h(0, th0)
-        wo1_low_bf = held("wo1_low_bf", [P, 2 * CHUNK], BF16, "th0_1")
-        cast_wo(wo1_low_bf, 1, low, nc.vector.tensor_copy)
-        quantize_wo(1, low, wo1_low_bf)
-        quantize_h(1, th1)
-        wo1_high_bf = held("wo1_high_bf", [P, 2 * CHUNK], BF16, "th1_0")
-        cast_wo(wo1_high_bf, 1, high, nc.vector.tensor_copy)
-        wo2_bf = held("wo2_bf", [P, 4 * CHUNK], BF16, "th1_1")
-        cast_wo(wo2_bf, 2, whole, nc.vector.tensor_copy)
-        quantize_wo(1, high, wo1_high_bf)
-        quantize_wo(2, whole, wo2_bf)
+        wo1_bf = held("wo1_bf", [P, 1024], BF16)
+        cast_wo(wo1_bf[:], wo_rest[:, :, 0:256], nc.scalar.copy)
+        for v in range(2):
+            apply_gain(0, v, th0)
+        for v in range(2):
+            quantize_h(0, v)
+        quantize_wo(slice(256, 512), wo0_bf[:, 1024:2048])
+        apply_gain(1, 0, th1)
+        quantize_wo(slice(512, 768), wo1_bf[:])
+        apply_gain(1, 1, th1)
+        for v in range(2):
+            quantize_h(1, v)
+        wo2_bf = held("wo2_bf", [P, 1024], BF16, "th1_0")
+        wo3_bf = held("wo3_bf", [P, 2048], BF16, "th1_1")
+        cast_wo(wo2_bf[:], wo_rest[:, :, 256:512], nc.vector.tensor_copy)
+        cast_wo(wo3_bf[:], wo_rest[:, :, 512:1024], nc.vector.tensor_copy)
+        quantize_wo(slice(768, 1024), wo2_bf[:])
+        quantize_wo(slice(1024, 1536), wo3_bf[:])
 
         for i in range(EARLY_TILES):
-            logits([(i, 0)], [i], [False])
+            logits(i, [(i, 0)], [i], [False])
         pairs = [((i, 1), (i + 1, 1)) for i in range(0, EARLY_TILES, 2)]
         pairs.extend(((i, 0), (i, 1)) for i in range(EARLY_TILES, OUT_TILES))
         for n, parts in enumerate(pairs):
             b = (EARLY_TILES + 2 * n) % BANKS
-            logits(parts, (b, b + 1), (n >= SCALAR_ONLY_PAIRS, False))
+            logits(EARLY_TILES + n, parts, (b, b + 1), (n >= SCALAR_ONLY_PAIRS, False))

@@ -28,8 +28,7 @@ SCALAR_ONLY_PAIRS = 3
 BANKS = 8
 SHIFT = 4
 STAGE_ROW = 96
-BO_ROW, BH_ROW, GAIN_ROW = 108, 120, 124
-BH_COL, GAIN_COL = BH_ROW - BO_ROW, GAIN_ROW - BO_ROW
+BO_ROW = P - OUT_TILES
 
 
 def tile_list_trigram_next_logits_kernel(
@@ -49,7 +48,7 @@ def tile_list_trigram_next_logits_kernel(
         lists = [held("list%d" % u, [P, S // 16], U16) for u in range(3)]
         table_scales = held("table_scales", [P, T // 4], I32)
         picked_scales = held("picked_scales", [P, 3 * S], U8)
-        planes = [held("planes%d" % a, [P, 3 * S // 4], I32) for a in range(PASSES)]
+        planes = held("planes", [P, PASSES, 3 * S // 4], I32)
         ident = held("ident", [P, P], F32)
         w1_bf = [held("w1_bf%d" % a, [P, 4 * H], BF16) for a in range(PASSES)]
         w1_codes = [held("w1_codes%d" % a, [P, H], U32) for a in range(PASSES)]
@@ -74,15 +73,13 @@ def tile_list_trigram_next_logits_kernel(
         nc.vector.memset(w_sc_raw[:], 0)
         nc.vector.memset(table_scales[0:STAGE_ROW, :], 0)
         nc.gpsimd.memset(rows[96:BO_ROW, :], 0.0)
-        for a in range(PASSES):
-            nc.gpsimd.memset(planes[a][:], 0)
+        nc.gpsimd.memset(planes[:], 0)
         make_identity(nc, ident[:])
-        nc.gpsimd.dma_start(rows[BO_ROW:BH_ROW, :], bo.rearrange("(i p) -> i p", p=P))
-        for first, vector in ((BH_ROW, bh), (GAIN_ROW, gain)):
-            nc.gpsimd.dma_start(
-                rows[first : first + 4, :].rearrange("t (g q) -> t g q", q=8),
-                vector.rearrange("(g t q) -> t g q", t=4, q=8),
-            )
+        nc.gpsimd.dma_start(rows[BO_ROW:P, :], bo.rearrange("(i p) -> i p", p=P))
+        bh_cols = held("bh_cols", [P, 4], F32)
+        gain_cols = held("gain_cols", [P, 4], F32)
+        nc.gpsimd.dma_start(bh_cols[:], bh.rearrange("(p t) -> p t", t=4))
+        nc.gpsimd.dma_start(gain_cols[:], gain.rearrange("(p t) -> p t", t=4))
         nc.scalar.activation(rows[0:96, :], ident[0:96, :], ACT.Tanh, scale=0.0)
 
         def load_weight_scales(first, src, quadrants):
@@ -99,16 +96,14 @@ def tile_list_trigram_next_logits_kernel(
             nc.sync.dma_start(w1_raw[a][:], w1[a * 512 : (a + 1) * 512, :].rearrange("(p j) c -> p j c", j=4))
 
         def load_wo(dst, cols):
-            src = wo[:, cols].rearrange("(g t q) n -> t g q n", t=4, q=8)
-            for t in range(4):
-                nc.sync.dma_start(dst[:, t, :], src[t])
+            nc.sync.dma_start(dst[:], wo[:, cols].rearrange("(p t) n -> p t n", t=4))
 
-        def move_planes(a):
-            for q in range(4):
-                first = STAGE_ROW + 16 * a + 4 * q
-                nc.sync.dma_start(planes[a][32 * q : 32 * q + 4, :], picked_scales[first : first + 4, :].bitcast(I32))
+        def move_planes():
+            for q in (0, 2, 1, 3):
+                first = STAGE_ROW + 8 * q
+                nc.sync.dma_start(planes[32 * q : 32 * q + 4, :, :], picked_scales[first : first + 8, :].bitcast(I32))
 
-        nc.sync.dma_start(table_scales[STAGE_ROW:P, :], tab_scales.rearrange("a q t -> (a q) t").bitcast(I32))
+        nc.sync.dma_start(table_scales[STAGE_ROW:P, :], tab_scales.bitcast(I32).rearrange("a q t -> q a t"))
         nc.sync.dma_start(lists[0][:], offs)
         nc.sync.dma_start(lists[1][:], offs2)
         load_w1(0)
@@ -128,18 +123,17 @@ def tile_list_trigram_next_logits_kernel(
             nc.vector.tensor_copy(dst, table[a][:].bitcast(U32).indirect(picks))
 
         def cast_w1(a):
-            src = w1_raw[a][:].rearrange("p j (g t u i) -> p t g u j i", t=4, u=4, i=2)
-            dst = w1_bf[a][:].rearrange("p (t g u i j) -> p t g u j i", t=4, u=4, i=2, j=4)
-            for t in range(4):
-                nc.scalar.copy(dst[:, t], src[:, t])
+            src = w1_raw[a][:].rearrange("p j (m t) -> p m t j", t=4)
+            dst = w1_bf[a][:].rearrange("p (t m j) -> p m t j", t=4, j=4)
+            nc.scalar.copy(dst, src)
 
         def quantize_w1(a):
             nc.vector.quantize_mx(out=w1_codes[a][:].bitcast(FP8X4), scales=w1_sc[a][:], in_=w1_bf[a][:])
 
-        def reorder(dst, src, run):
+        def reorder(dst, src, dtype, line):
             nc.vector.tensor_copy(
-                dst[:].rearrange("p a (t g q) -> p a t g q", t=4, q=run),
-                src[:].rearrange("p a (g t q) -> p a t g q", t=4, q=run),
+                dst[:].bitcast(dtype).rearrange("p a (t m i) -> p a m t i", t=4, i=line),
+                src[:].bitcast(dtype).rearrange("p a (m i t) -> p a m t i", t=4, i=line),
             )
 
         def first_product(s, acc, u, a, x_words, start, stop):
@@ -158,7 +152,7 @@ def tile_list_trigram_next_logits_kernel(
                     lhsT=lhs,
                     lhsT_scale=lhs_sc,
                     rhs=x_words.bitcast(FP8X4),
-                    rhs_scale=planes[a][:].bitcast(U8)[:, u * S + s * HALF : u * S + (s + 1) * HALF],
+                    rhs_scale=planes[:, a, :].bitcast(U8)[:, u * S + s * HALF : u * S + (s + 1) * HALF],
                     start=start,
                     stop=stop,
                 )
@@ -170,11 +164,11 @@ def tile_list_trigram_next_logits_kernel(
                         th[v][:, t, :],
                         acc[t][:, v * SUB : (v + 1) * SUB],
                         ACT.Tanh,
-                        bias=consts[:, BH_COL + t : BH_COL + t + 1],
+                        bias=bh_cols[:, t : t + 1],
                     )
 
         def apply_gain(s, v, th):
-            gains = consts[:, GAIN_COL : GAIN_COL + 4].unsqueeze(1).unsqueeze(3).to_broadcast([P, SUB // 2, 4, 2])
+            gains = gain_cols[:].unsqueeze(1).unsqueeze(3).to_broadcast([P, SUB // 2, 4, 2])
             nc.vector.tensor_tensor(
                 h_bf[s][:, v, :].rearrange("p (m i t) -> p m t i", i=2, t=4),
                 th[v][:].rearrange("p t (m i) -> p m t i", i=2),
@@ -220,9 +214,8 @@ def tile_list_trigram_next_logits_kernel(
             nc.vector.tensor_copy(
                 picked_scales[:, u * S : (u + 1) * S], table_scales[:].bitcast(U8).indirect(lists[u][:])
             )
-        move_planes(0)
+        move_planes()
         load_table(1)
-        move_planes(1)
         load_wo(wo_first, slice(0, CHUNK))
         load_wo(wo_rest, slice(CHUNK, N))
         for a in range(PASSES):
@@ -238,9 +231,9 @@ def tile_list_trigram_next_logits_kernel(
         acc1 = [bank(b, "acc") for b in range(4, BANKS)]
         words0 = held("words0", [P, S], U32)
         gather_words(everyone, 0, 0, words0[:])
-        reorder(w_sc, w_sc_raw, 2)
-        reorder(w3_codes, w3_raw, 4)
-        reorder(w2_codes, w2_raw, 8)
+        reorder(w_sc, w_sc_raw, U8, 16)
+        reorder(w3_codes, w3_raw, U16, 8)
+        reorder(w2_codes, w2_raw, I32, 4)
         words12 = held("words12", [P, 2, S], U32, "w2_raw")
         first_words = [words0[:], words12[:, 0, :], words12[:, 1, :]]
         for u in (1, 2):

@@ -24,7 +24,7 @@ SUB = HALF // 2
 CHUNK = 512
 OUT_TILES = N // P
 EARLY_TILES = 6
-SCALAR_ONLY_PAIRS = 3
+SCALAR_ONLY = 12
 BANKS = 8
 SHIFT = 4
 STAGE_ROW = 96
@@ -47,8 +47,9 @@ def tile_list_trigram_next_logits_kernel(
 
         lists = [held("list%d" % u, [P, S // 16], U16) for u in range(3)]
         table_scales = held("table_scales", [P, T // 4], I32)
-        picked_scales = held("picked_scales", [P, 3 * S], U8)
-        planes = held("planes", [P, PASSES, 3 * S // 4], I32)
+        widths = (S, 2 * S)
+        picked_scales = [held("picked_scales%d" % e, [P, w], U8) for e, w in enumerate(widths)]
+        planes = [held("planes%d" % e, [P, PASSES, w // 4], I32) for e, w in enumerate(widths)]
         ident = held("ident", [P, P], F32)
         w1_bf = [held("w1_bf%d" % a, [P, 4 * H], BF16) for a in range(PASSES)]
         w1_codes = [held("w1_codes%d" % a, [P, H], U32) for a in range(PASSES)]
@@ -67,20 +68,17 @@ def tile_list_trigram_next_logits_kernel(
         w1_raw = [held("w1_raw%d" % a, [P, 4, H], F32) for a in range(PASSES)]
         w2_raw = held("w2_raw", [P, PASSES, H], I32)
         w3_raw = held("w3_raw", [P, PASSES, H // 2], I32)
-        wo_first = held("wo_first", [P, 4, CHUNK], F32)
-        wo_rest = held("wo_rest", [P, 4, N - CHUNK], F32)
+        wo_raw = [held("wo_raw%d" % c, [P, 4, CHUNK], F32) for c in range(3)]
 
         nc.vector.memset(w_sc_raw[:], 0)
         nc.vector.memset(table_scales[0:STAGE_ROW, :], 0)
-        nc.gpsimd.memset(rows[96:BO_ROW, :], 0.0)
-        nc.gpsimd.memset(planes[:], 0)
+        nc.vector.memset(rows[96:BO_ROW, :], 0.0)
+        for tile in planes:
+            nc.gpsimd.memset(tile[:], 0)
         make_identity(nc, ident[:])
         nc.gpsimd.dma_start(rows[BO_ROW:P, :], bo.rearrange("(i p) -> i p", p=P))
         bh_cols = held("bh_cols", [P, 4], F32)
         gain_cols = held("gain_cols", [P, 4], F32)
-        nc.gpsimd.dma_start(bh_cols[:], bh.rearrange("(p t) -> p t", t=4))
-        nc.gpsimd.dma_start(gain_cols[:], gain.rearrange("(p t) -> p t", t=4))
-        nc.scalar.activation(rows[0:96, :], ident[0:96, :], ACT.Tanh, scale=0.0)
 
         def load_weight_scales(first, src, quadrants):
             for q in quadrants:
@@ -98,10 +96,10 @@ def tile_list_trigram_next_logits_kernel(
         def load_wo(dst, cols):
             nc.sync.dma_start(dst[:], wo[:, cols].rearrange("(p t) n -> p t n", t=4))
 
-        def move_planes():
+        def move_planes(e):
             for q in (0, 2, 1, 3):
                 first = STAGE_ROW + 8 * q
-                nc.sync.dma_start(planes[32 * q : 32 * q + 4, :, :], picked_scales[first : first + 8, :].bitcast(I32))
+                nc.sync.dma_start(planes[e][32 * q : 32 * q + 4, :, :], picked_scales[e][first : first + 8, :].bitcast(I32))
 
         nc.sync.dma_start(table_scales[STAGE_ROW:P, :], tab_scales.bitcast(I32).rearrange("a q t -> q a t"))
         nc.sync.dma_start(lists[0][:], offs)
@@ -113,7 +111,6 @@ def tile_list_trigram_next_logits_kernel(
         load_weight_scales(0, w3_scales, range(4))
         nc.sync.dma_start(w3_raw[:], w3_words.rearrange("a p b -> p a b").bitcast(I32))
         nc.sync.dma_start(w2_raw[:], w2_words.rearrange("a p c i -> p a (c i)").bitcast(I32))
-        load_w1(1)
 
         everyone = slice(0, S)
         halves = [slice(0, HALF), slice(HALF, S)]
@@ -137,6 +134,7 @@ def tile_list_trigram_next_logits_kernel(
             )
 
         def first_product(s, acc, u, a, x_words, start, stop):
+            x_first = max(u - 1, 0) * S + s * HALF
             for t in range(4):
                 if u == 0:
                     lhs = w1_codes[a][:, t * P : (t + 1) * P].bitcast(FP8X4)
@@ -152,19 +150,19 @@ def tile_list_trigram_next_logits_kernel(
                     lhsT=lhs,
                     lhsT_scale=lhs_sc,
                     rhs=x_words.bitcast(FP8X4),
-                    rhs_scale=planes[:, a, :].bitcast(U8)[:, u * S + s * HALF : u * S + (s + 1) * HALF],
+                    rhs_scale=planes[min(u, 1)][:, a, :].bitcast(U8)[:, x_first : x_first + HALF],
                     start=start,
                     stop=stop,
                 )
 
-        def squash(acc, th):
+        def squash(acc, th, bias):
             for v in range(2):
                 for t in range(4):
                     nc.scalar.activation(
                         th[v][:, t, :],
                         acc[t][:, v * SUB : (v + 1) * SUB],
                         ACT.Tanh,
-                        bias=bh_cols[:, t : t + 1],
+                        bias=bias[:, t : t + 1],
                     )
 
         def apply_gain(s, v, th):
@@ -210,22 +208,24 @@ def tile_list_trigram_next_logits_kernel(
                 dst.rearrange("(e p) n -> p e n", p=P), staged[:].rearrange("p (e s) n -> p e (s n)", s=s1 - s0 + 1)
             )
 
-        for u in range(3):
-            nc.vector.tensor_copy(
-                picked_scales[:, u * S : (u + 1) * S], table_scales[:].bitcast(U8).indirect(lists[u][:])
-            )
-        move_planes()
+        for u, dst in enumerate((picked_scales[0][:], picked_scales[1][:, 0:S], picked_scales[1][:, S : 2 * S])):
+            nc.vector.tensor_copy(dst, table_scales[:].bitcast(U8).indirect(lists[u][:]))
+        move_planes(0)
+        load_w1(1)
+        move_planes(1)
         load_table(1)
-        load_wo(wo_first, slice(0, CHUNK))
-        load_wo(wo_rest, slice(CHUNK, N))
+        first_bias = held("first_bias", [P, 4], F32)
+        load_wo(wo_raw[0], slice(0, CHUNK))
+        nc.sync.dma_start(bh_cols[:], bh.rearrange("(p t) -> p t", t=4))
+        nc.sync.dma_start(gain_cols[:], gain.rearrange("(p t) -> p t", t=4))
+        for c in (1, 2):
+            load_wo(wo_raw[c], slice(c * CHUNK, (c + 1) * CHUNK))
+        nc.scalar.activation(rows[0:96, :], w1_raw[0][0:96, 0, 0:P], ACT.Tanh, scale=0.0)
         for a in range(PASSES):
             cast_w1(a)
             quantize_w1(a)
 
-        turned = bank(BANKS - 1, "turned")
-        nc.tensor.transpose(turned[:, 0:P], rows[:], ident[:])
-        consts = held("consts", [P, P - BO_ROW], F32)
-        nc.scalar.copy(consts[:], turned[:, BO_ROW:P])
+        nc.scalar.copy(first_bias[:], bh_cols[:])
 
         acc0 = [bank(b, "acc") for b in range(4)]
         acc1 = [bank(b, "acc") for b in range(4, BANKS)]
@@ -237,7 +237,8 @@ def tile_list_trigram_next_logits_kernel(
         words12 = held("words12", [P, 2, S], U32, "w2_raw")
         first_words = [words0[:], words12[:, 0, :], words12[:, 1, :]]
         for u in (1, 2):
-            gather_words(everyone, u, 0, first_words[u])
+            for half in halves:
+                gather_words(half, u, 0, first_words[u][:, half])
         for u in range(3):
             for s, acc in enumerate((acc0, acc1)):
                 first_product(s, acc, u, 0, first_words[u][:, halves[s]], u == 0, False)
@@ -251,14 +252,18 @@ def tile_list_trigram_next_logits_kernel(
                 first_product(s, acc, u, 1, second_words[:, 3 * s + u, :], False, u == 2)
 
         wo0_bf = held("wo0_bf", [P, 4 * CHUNK], BF16)
-        cast_wo(wo0_bf[:], wo_first[:], nc.scalar.copy)
+        cast_wo(wo0_bf[:], wo_raw[0][:], nc.scalar.copy)
         quantize_wo(slice(0, 256), wo0_bf[:, 0:1024])
-        th0 = [held("th0_%d" % v, [P, 4, SUB], F32, tag) for v, tag in enumerate(("wo_first", "th0_1"))]
+        th0 = [held("th0_%d" % v, [P, 4, SUB], F32, tag) for v, tag in enumerate(("wo_raw0", "th0_1"))]
         th1 = [held("th1_%d" % v, [P, 4, SUB], F32) for v in range(2)]
-        squash(acc0, th0)
-        squash(acc1, th1)
-        wo1_bf = held("wo1_bf", [P, 1024], BF16)
-        cast_wo(wo1_bf[:], wo_rest[:, :, 0:256], nc.scalar.copy)
+        squash(acc0, th0, first_bias)
+        wo1_bf = held("wo1_bf", [P, 1024], BF16, "first_bias")
+        cast_wo(wo1_bf[:], wo_raw[1][:, :, 0:256], nc.scalar.copy)
+        squash(acc1, th1, bh_cols)
+        turned = bank(4, "turned")
+        nc.tensor.transpose(turned[:, 0:P], rows[:], ident[:])
+        consts = held("consts", [P, OUT_TILES], F32)
+        nc.scalar.copy(consts[:], turned[:, BO_ROW:P])
         for v in range(2):
             apply_gain(0, v, th0)
         for v in range(2):
@@ -271,15 +276,17 @@ def tile_list_trigram_next_logits_kernel(
             quantize_h(1, v)
         wo2_bf = held("wo2_bf", [P, 1024], BF16, "th1_0")
         wo3_bf = held("wo3_bf", [P, 2048], BF16, "th1_1")
-        cast_wo(wo2_bf[:], wo_rest[:, :, 256:512], nc.vector.tensor_copy)
-        cast_wo(wo3_bf[:], wo_rest[:, :, 512:1024], nc.vector.tensor_copy)
+        cast_wo(wo2_bf[:], wo_raw[1][:, :, 256:512], nc.vector.tensor_copy)
+        cast_wo(wo3_bf[:], wo_raw[2][:], nc.vector.tensor_copy)
         quantize_wo(slice(768, 1024), wo2_bf[:])
         quantize_wo(slice(1024, 1536), wo3_bf[:])
 
-        for i in range(EARLY_TILES):
-            logits(i, [(i, 0)], [i], [False])
-        pairs = [((i, 1), (i + 1, 1)) for i in range(0, EARLY_TILES, 2)]
-        pairs.extend(((i, 0), (i, 1)) for i in range(EARLY_TILES, OUT_TILES))
-        for n, parts in enumerate(pairs):
-            b = (EARLY_TILES + 2 * n) % BANKS
-            logits(EARLY_TILES + n, parts, (b, b + 1), (n >= SCALAR_ONLY_PAIRS, False))
+        stores = [[(i, 0)] for i in range(EARLY_TILES)]
+        stores.extend([(i, 1), (i + 1, 1)] for i in range(0, EARLY_TILES, 2))
+        for first, last in ((6, 7), (7, 9), (9, 12)):
+            stores.append([(i, s) for i in range(first, last) for s in range(2)])
+        done = 0
+        for n, parts in enumerate(stores):
+            turns = range(done, done + len(parts))
+            logits(n, parts, [k % BANKS for k in turns], [k >= SCALAR_ONLY and k % 2 == 0 for k in turns])
+            done = done + len(parts)

@@ -58,17 +58,19 @@ def tile_list_trigram_next_logits_kernel(
         w3_codes = held("w3_codes", [P, PASSES, H // 2], I32)
         w_sc_raw = held("w_sc_raw", [P, PASSES, H // 4], I32)
         w_sc = held("w_sc", [P, PASSES, H // 4], I32)
-        wo_codes = held("wo_codes", [P, N], U32)
         wo_sc = held("wo_sc", [P, N], U8)
+        wo_codes = {}
         h_bf = [held("h_bf%d" % s, [P, 2, 4 * SUB], BF16) for s in range(2)]
         h_codes = [held("h_codes%d" % s, [P, HALF], U32) for s in range(2)]
         h_sc = [held("h_sc%d" % s, [P, HALF], U8) for s in range(2)]
         table = [held("table%d" % a, [P, T], I32) for a in range(PASSES)]
         rows = held("rows", [P, P], F32)
-        w1_raw = [held("w1_raw%d" % a, [P, 4, H], F32) for a in range(PASSES)]
+        w1_raw0 = held("w1_raw0", [P, 4, H], F32)
+        w1_raw1 = [held("w1_raw1_%d" % e, [P, 4, H // 2], F32) for e in range(2)]
         w2_raw = held("w2_raw", [P, PASSES, H], I32)
         w3_raw = held("w3_raw", [P, PASSES, H // 2], I32)
-        wo_raw = [held("wo_raw%d" % c, [P, 4, CHUNK], F32) for c in range(3)]
+        wo_cols = (slice(0, 256), slice(256, 768), slice(768, N))
+        wo_raw = [held("wo_raw%d" % c, [P, 4, cols.stop - cols.start], F32) for c, cols in enumerate(wo_cols)]
 
         nc.vector.memset(w_sc_raw[:], 0)
         nc.vector.memset(table_scales[0:STAGE_ROW, :], 0)
@@ -90,8 +92,8 @@ def tile_list_trigram_next_logits_kernel(
         def load_table(a):
             nc.sync.dma_start(table[a][:], tab_words[a].rearrange("p t i -> p (t i)").bitcast(I32))
 
-        def load_w1(a):
-            nc.sync.dma_start(w1_raw[a][:], w1[a * 512 : (a + 1) * 512, :].rearrange("(p j) c -> p j c", j=4))
+        def load_w1(dst, a, cols):
+            nc.sync.dma_start(dst[:], w1[a * 512 : (a + 1) * 512, cols].rearrange("(p j) c -> p j c", j=4))
 
         def load_wo(dst, cols):
             nc.sync.dma_start(dst[:], wo[:, cols].rearrange("(p t) n -> p t n", t=4))
@@ -104,7 +106,7 @@ def tile_list_trigram_next_logits_kernel(
         nc.sync.dma_start(table_scales[STAGE_ROW:P, :], tab_scales.bitcast(I32).rearrange("a q t -> q a t"))
         nc.sync.dma_start(lists[0][:], offs)
         nc.sync.dma_start(lists[1][:], offs2)
-        load_w1(0)
+        load_w1(w1_raw0, 0, slice(0, H))
         nc.sync.dma_start(lists[2][:], offs3)
         load_weight_scales(SHIFT, w2_scales, range(4))
         load_table(0)
@@ -119,10 +121,9 @@ def tile_list_trigram_next_logits_kernel(
             picks = lists[u][:, contexts.start // 16 : contexts.stop // 16]
             nc.vector.tensor_copy(dst, table[a][:].bitcast(U32).indirect(picks))
 
-        def cast_w1(a):
-            src = w1_raw[a][:].rearrange("p j (m t) -> p m t j", t=4)
+        def cast_w1(a, raw, places):
             dst = w1_bf[a][:].rearrange("p (t m j) -> p m t j", t=4, j=4)
-            nc.scalar.copy(dst, src)
+            nc.scalar.copy(dst[:, places], raw[:].rearrange("p j (m t) -> p m t j", t=4))
 
         def quantize_w1(a):
             nc.vector.quantize_mx(out=w1_codes[a][:].bitcast(FP8X4), scales=w1_sc[a][:], in_=w1_bf[a][:])
@@ -181,8 +182,14 @@ def tile_list_trigram_next_logits_kernel(
         def cast_wo(dst, src, copy):
             copy(dst.rearrange("p (m i t) -> p m t i", i=2, t=4), src.rearrange("p t (m i) -> p m t i", i=2))
 
-        def quantize_wo(cols, src):
-            nc.vector.quantize_mx(out=wo_codes[:, cols].bitcast(FP8X4), scales=wo_sc[:, cols], in_=src)
+        def gpsimd_cast(dst, src):
+            nc.gpsimd.tensor_scalar(dst, src, 1.0, 0.0, ALU.mult, ALU.add)
+
+        def quantize_wo(cols, src, tag=None):
+            codes = held("wo_codes%d" % cols.start, [P, cols.stop - cols.start], U32, tag)
+            nc.vector.quantize_mx(out=codes[:].bitcast(FP8X4), scales=wo_sc[:, cols], in_=src)
+            for first in range(cols.start, cols.stop, P):
+                wo_codes[first // P] = codes[:, first - cols.start : first - cols.start + P]
 
         def logits(n, parts, banks, on_vector):
             staged = held("staged%d" % n, [P, len(parts), HALF], F32)
@@ -191,7 +198,7 @@ def tile_list_trigram_next_logits_kernel(
                 cols = slice(i * P, (i + 1) * P)
                 nc.tensor.matmul_mx(
                     out=y[:],
-                    lhsT=wo_codes[:, cols].bitcast(FP8X4),
+                    lhsT=wo_codes[i].bitcast(FP8X4),
                     lhsT_scale=wo_sc[:, cols],
                     rhs=h_codes[s][:].bitcast(FP8X4),
                     rhs_scale=h_sc[s][:],
@@ -211,20 +218,25 @@ def tile_list_trigram_next_logits_kernel(
         for u, dst in enumerate((picked_scales[0][:], picked_scales[1][:, 0:S], picked_scales[1][:, S : 2 * S])):
             nc.vector.tensor_copy(dst, table_scales[:].bitcast(U8).indirect(lists[u][:]))
         move_planes(0)
-        load_w1(1)
+        load_w1(w1_raw1[0], 1, slice(0, H // 2))
         move_planes(1)
         load_table(1)
+        load_w1(w1_raw1[1], 1, slice(H // 2, H))
         first_bias = held("first_bias", [P, 4], F32)
-        load_wo(wo_raw[0], slice(0, CHUNK))
+        load_wo(wo_raw[0], wo_cols[0])
         nc.sync.dma_start(bh_cols[:], bh.rearrange("(p t) -> p t", t=4))
         nc.sync.dma_start(gain_cols[:], gain.rearrange("(p t) -> p t", t=4))
         for c in (1, 2):
-            load_wo(wo_raw[c], slice(c * CHUNK, (c + 1) * CHUNK))
-        nc.scalar.activation(rows[0:96, :], w1_raw[0][0:96, 0, 0:P], ACT.Tanh, scale=0.0)
-        for a in range(PASSES):
-            cast_w1(a)
-            quantize_w1(a)
+            load_wo(wo_raw[c], wo_cols[c])
+        nc.scalar.activation(rows[0:96, :], w1_raw0[0:96, 0, 0:P], ACT.Tanh, scale=0.0)
+        cast_w1(0, w1_raw0, slice(0, P))
+        quantize_w1(0)
+        cast_w1(1, w1_raw1[0], slice(0, P // 2))
 
+        turned = bank(BANKS - 1, "turned")
+        nc.tensor.transpose(turned[:, 0:P], rows[:], ident[:])
+        consts = held("consts", [P, OUT_TILES], F32)
+        nc.scalar.copy(consts[:], turned[:, BO_ROW:P])
         nc.scalar.copy(first_bias[:], bh_cols[:])
 
         acc0 = [bank(b, "acc") for b in range(4)]
@@ -243,43 +255,41 @@ def tile_list_trigram_next_logits_kernel(
             for s, acc in enumerate((acc0, acc1)):
                 first_product(s, acc, u, 0, first_words[u][:, halves[s]], u == 0, False)
 
-        second_words = held("second_words", [P, 6, HALF], U32)
-        for s, acc in enumerate((acc0, acc1)):
-            for u in range(3):
-                gather_words(halves[s], u, 1, second_words[:, 3 * s + u, :])
-        for s, acc in enumerate((acc0, acc1)):
-            for u in range(3):
-                first_product(s, acc, u, 1, second_words[:, 3 * s + u, :], False, u == 2)
+        second_words = held("second_words", [P, 3, HALF], U32)
+        for u in (1, 2, 0):
+            gather_words(halves[0], u, 1, second_words[:, u, :])
+        cast_w1(1, w1_raw1[1], slice(P // 2, P))
+        quantize_w1(1)
+        last_words = held("last_words", [P, 3, HALF], U32, "w1_bf1")
+        for u in (1, 2, 0):
+            gather_words(halves[1], u, 1, last_words[:, u, :])
+        for s, acc, words in ((0, acc0, second_words), (1, acc1, last_words)):
+            for u in (1, 2, 0):
+                first_product(s, acc, u, 1, words[:, u, :], False, u == 0)
 
-        wo0_bf = held("wo0_bf", [P, 4 * CHUNK], BF16)
+        wo0_bf = held("wo0_bf", [P, 1024], BF16)
         cast_wo(wo0_bf[:], wo_raw[0][:], nc.scalar.copy)
-        quantize_wo(slice(0, 256), wo0_bf[:, 0:1024])
+        quantize_wo(slice(0, 256), wo0_bf[:])
+        wo2_bf = held("wo2_bf", [P, 1024], BF16)
+        cast_wo(wo2_bf[:], wo_raw[1][:, :, 256:512], gpsimd_cast)
         th0 = [held("th0_%d" % v, [P, 4, SUB], F32, tag) for v, tag in enumerate(("wo_raw0", "th0_1"))]
         th1 = [held("th1_%d" % v, [P, 4, SUB], F32) for v in range(2)]
         squash(acc0, th0, first_bias)
         wo1_bf = held("wo1_bf", [P, 1024], BF16, "first_bias")
         cast_wo(wo1_bf[:], wo_raw[1][:, :, 0:256], nc.scalar.copy)
         squash(acc1, th1, bh_cols)
-        turned = bank(4, "turned")
-        nc.tensor.transpose(turned[:, 0:P], rows[:], ident[:])
-        consts = held("consts", [P, OUT_TILES], F32)
-        nc.scalar.copy(consts[:], turned[:, BO_ROW:P])
         for v in range(2):
             apply_gain(0, v, th0)
         for v in range(2):
             quantize_h(0, v)
-        quantize_wo(slice(256, 512), wo0_bf[:, 1024:2048])
+        quantize_wo(slice(256, 512), wo1_bf[:], "h_bf0")
         apply_gain(1, 0, th1)
-        quantize_wo(slice(512, 768), wo1_bf[:])
+        quantize_wo(slice(512, 768), wo2_bf[:], "th0_1")
         apply_gain(1, 1, th1)
         for v in range(2):
             quantize_h(1, v)
-        wo2_bf = held("wo2_bf", [P, 1024], BF16, "th1_0")
-        wo3_bf = held("wo3_bf", [P, 2048], BF16, "th1_1")
-        cast_wo(wo2_bf[:], wo_raw[1][:, :, 256:512], nc.vector.tensor_copy)
-        cast_wo(wo3_bf[:], wo_raw[2][:], nc.vector.tensor_copy)
-        quantize_wo(slice(768, 1024), wo2_bf[:])
-        quantize_wo(slice(1024, 1536), wo3_bf[:])
+        wo3_bf = held("wo3_bf", [P, 1024], BF16, "th1_0")
+        wo4_bf = held("wo4_bf", [P, 2048], BF16, "th1_1")
 
         stores = [[(i, 0)] for i in range(EARLY_TILES)]
         stores.extend([(i, 1), (i + 1, 1)] for i in range(0, EARLY_TILES, 2))
@@ -288,5 +298,10 @@ def tile_list_trigram_next_logits_kernel(
         done = 0
         for n, parts in enumerate(stores):
             turns = range(done, done + len(parts))
-            logits(n, parts, [k % BANKS for k in turns], [k >= SCALAR_ONLY and k % 2 == 0 for k in turns])
+            logits(n, parts, [k % BANKS for k in turns], [k == EARLY_TILES + 1 or (k >= SCALAR_ONLY and k % 2 == 0) for k in turns])
             done = done + len(parts)
+            if n == EARLY_TILES:
+                cast_wo(wo3_bf[:], wo_raw[2][:, :, 0:256], nc.vector.tensor_copy)
+                cast_wo(wo4_bf[:], wo_raw[2][:, :, 256:768], nc.vector.tensor_copy)
+                quantize_wo(slice(768, 1024), wo3_bf[:])
+                quantize_wo(slice(1024, 1536), wo4_bf[:])

@@ -37,10 +37,14 @@ def tile_list_trigram_next_logits_kernel(
     nc = tc.nc
     with ExitStack() as ctx:
         keep = ctx.enter_context(tc.tile_pool(name="keep", bufs=1))
+        shared = ctx.enter_context(tc.tile_pool(name="shared", bufs=1))
         psum = ctx.enter_context(tc.psum_pool(name="psum", bufs=1))
 
         def held(name, shape, dtype, tag=None):
             return keep.tile(shape, dtype, name=name, tag=tag or name, align_bytes=64)
+
+        def over_table(name, shape, dtype, offset):
+            return shared.tile(shape, dtype, name=name, offset=offset, align_bytes=64)
 
         def bank(b, name):
             return psum.tile([P, HALF], F32, name=name, tag="bank%d" % b)
@@ -54,16 +58,16 @@ def tile_list_trigram_next_logits_kernel(
         w1_bf = [held("w1_bf%d" % a, [P, 4 * H], BF16) for a in range(PASSES)]
         w1_codes = [held("w1_codes%d" % a, [P, H], U32) for a in range(PASSES)]
         w1_sc = [held("w1_sc%d" % a, [P, H], U8) for a in range(PASSES)]
-        w2_codes = held("w2_codes", [P, PASSES, H], I32)
+        w2_codes = [held("w2_codes%d" % a, [P, H], I32) for a in range(PASSES)]
         w3_codes = held("w3_codes", [P, PASSES, H // 2], I32)
         w_sc_raw = held("w_sc_raw", [P, PASSES, H // 4], I32)
-        w_sc = held("w_sc", [P, PASSES, H // 4], I32)
+        w_sc = [held("w_sc%d" % a, [P, H // 4], I32) for a in range(PASSES)]
         wo_sc = held("wo_sc", [P, N], U8)
         wo_codes = {}
         h_bf = [held("h_bf%d" % s, [P, 2, 4 * SUB], BF16) for s in range(2)]
-        h_codes = [held("h_codes%d" % s, [P, HALF], U32) for s in range(2)]
+        h_codes = {1: held("h_codes1", [P, HALF], U32)[:]}
         h_sc = [held("h_sc%d" % s, [P, HALF], U8) for s in range(2)]
-        table = [held("table%d" % a, [P, T], I32) for a in range(PASSES)]
+        table = [held("table0", [P, T], I32), over_table("table1", [P, T], I32, 0)]
         rows = held("rows", [P, P], F32)
         w1_raw0 = held("w1_raw0", [P, 4, H], F32)
         w1_raw1 = [held("w1_raw1_%d" % e, [P, 4, H // 2], F32) for e in range(2)]
@@ -89,8 +93,8 @@ def tile_list_trigram_next_logits_kernel(
                     src[:, 4 * q : 4 * q + 4, :].bitcast(I32).rearrange("a r c -> r a c"),
                 )
 
-        def load_table(a):
-            nc.sync.dma_start(table[a][:], tab_words[a].rearrange("p t i -> p (t i)").bitcast(I32))
+        def load_table(a, cols):
+            nc.sync.dma_start(table[a][:, cols], tab_words[a].rearrange("p t i -> p (t i)").bitcast(I32)[:, cols])
 
         def load_w1(dst, a, cols):
             nc.sync.dma_start(dst[:], w1[a * 512 : (a + 1) * 512, cols].rearrange("(p j) c -> p j c", j=4))
@@ -109,12 +113,11 @@ def tile_list_trigram_next_logits_kernel(
         load_w1(w1_raw0, 0, slice(0, H))
         nc.sync.dma_start(lists[2][:], offs3)
         load_weight_scales(SHIFT, w2_scales, range(4))
-        load_table(0)
+        load_table(0, slice(0, T))
         load_weight_scales(0, w3_scales, range(4))
         nc.sync.dma_start(w3_raw[:], w3_words.rearrange("a p b -> p a b").bitcast(I32))
         nc.sync.dma_start(w2_raw[:], w2_words.rearrange("a p c i -> p a (c i)").bitcast(I32))
 
-        everyone = slice(0, S)
         halves = [slice(0, HALF), slice(HALF, S)]
 
         def gather_words(contexts, u, a, dst):
@@ -134,6 +137,12 @@ def tile_list_trigram_next_logits_kernel(
                 src[:].bitcast(dtype).rearrange("p a (m i t) -> p a m t i", t=4, i=line),
             )
 
+        def reorder_pass(dst, src, dtype, line):
+            nc.gpsimd.tensor_copy(
+                dst.bitcast(dtype).rearrange("p (t m i) -> p m t i", t=4, i=line),
+                src.bitcast(dtype).rearrange("p (m i t) -> p m t i", t=4, i=line),
+            )
+
         def first_product(s, acc, u, a, x_words, start, stop):
             x_first = max(u - 1, 0) * S + s * HALF
             for t in range(4):
@@ -141,11 +150,11 @@ def tile_list_trigram_next_logits_kernel(
                     lhs = w1_codes[a][:, t * P : (t + 1) * P].bitcast(FP8X4)
                     lhs_sc = w1_sc[a][:, t * P : (t + 1) * P]
                 elif u == 1:
-                    lhs = w2_codes[:, a, t * P : (t + 1) * P].bitcast(FP8X4)
-                    lhs_sc = w_sc[SHIFT:P, a, t * 32 : (t + 1) * 32].bitcast(U8)
+                    lhs = w2_codes[a][:, t * P : (t + 1) * P].bitcast(FP8X4)
+                    lhs_sc = w_sc[a][SHIFT:P, t * 32 : (t + 1) * 32].bitcast(U8)
                 else:
                     lhs = w3_codes[:, a, t * 64 : (t + 1) * 64].bitcast(U8).bitcast(FP4X4)
-                    lhs_sc = w_sc[:, a, t * 32 : (t + 1) * 32].bitcast(U8)
+                    lhs_sc = w_sc[a][:, t * 32 : (t + 1) * 32].bitcast(U8)
                 nc.tensor.matmul_mx(
                     out=acc[t][:],
                     lhsT=lhs,
@@ -166,18 +175,17 @@ def tile_list_trigram_next_logits_kernel(
                         bias=bias[:, t : t + 1],
                     )
 
-        def apply_gain(s, v, th):
-            gains = gain_cols[:].unsqueeze(1).unsqueeze(3).to_broadcast([P, SUB // 2, 4, 2])
+        def vector_gain(dst, src):
+            gains = gain_cols[:].unsqueeze(1).unsqueeze(3).to_broadcast([P, src.shape[2] // 2, 4, 2])
             nc.vector.tensor_tensor(
-                h_bf[s][:, v, :].rearrange("p (m i t) -> p m t i", i=2, t=4),
-                th[v][:].rearrange("p t (m i) -> p m t i", i=2),
+                dst.rearrange("p (m i t) -> p m t i", i=2, t=4),
+                src.rearrange("p t (m i) -> p m t i", i=2),
                 gains,
                 ALU.mult,
             )
 
-        def quantize_h(s, v):
-            cols = slice(v * SUB, (v + 1) * SUB)
-            nc.vector.quantize_mx(out=h_codes[s][:, cols].bitcast(FP8X4), scales=h_sc[s][:, cols], in_=h_bf[s][:, v, :])
+        def quantize_h(s, cols, src):
+            nc.vector.quantize_mx(out=h_codes[s][:, cols].bitcast(FP8X4), scales=h_sc[s][:, cols], in_=src)
 
         def cast_wo(dst, src, copy):
             copy(dst.rearrange("p (m i t) -> p m t i", i=2, t=4), src.rearrange("p t (m i) -> p m t i", i=2))
@@ -185,8 +193,9 @@ def tile_list_trigram_next_logits_kernel(
         def gpsimd_cast(dst, src):
             nc.gpsimd.tensor_scalar(dst, src, 1.0, 0.0, ALU.mult, ALU.add)
 
-        def quantize_wo(cols, src, tag=None):
-            codes = held("wo_codes%d" % cols.start, [P, cols.stop - cols.start], U32, tag)
+        def quantize_wo(cols, src, codes=None):
+            if codes is None:
+                codes = held("wo_codes%d" % cols.start, [P, cols.stop - cols.start], U32)
             nc.vector.quantize_mx(out=codes[:].bitcast(FP8X4), scales=wo_sc[:, cols], in_=src)
             for first in range(cols.start, cols.stop, P):
                 wo_codes[first // P] = codes[:, first - cols.start : first - cols.start + P]
@@ -200,7 +209,7 @@ def tile_list_trigram_next_logits_kernel(
                     out=y[:],
                     lhsT=wo_codes[i].bitcast(FP8X4),
                     lhsT_scale=wo_sc[:, cols],
-                    rhs=h_codes[s][:].bitcast(FP8X4),
+                    rhs=h_codes[s].bitcast(FP8X4),
                     rhs_scale=h_sc[s][:],
                     start=True,
                     stop=True,
@@ -218,15 +227,15 @@ def tile_list_trigram_next_logits_kernel(
         for u, dst in enumerate((picked_scales[0][:], picked_scales[1][:, 0:S], picked_scales[1][:, S : 2 * S])):
             nc.vector.tensor_copy(dst, table_scales[:].bitcast(U8).indirect(lists[u][:]))
         move_planes(0)
-        load_w1(w1_raw1[0], 1, slice(0, H // 2))
+        load_table(1, slice(0, T // 2))
         move_planes(1)
-        load_table(1)
-        load_w1(w1_raw1[1], 1, slice(H // 2, H))
-        first_bias = held("first_bias", [P, 4], F32)
-        load_wo(wo_raw[0], wo_cols[0])
+        load_table(1, slice(T // 2, T))
         nc.sync.dma_start(bh_cols[:], bh.rearrange("(p t) -> p t", t=4))
         nc.sync.dma_start(gain_cols[:], gain.rearrange("(p t) -> p t", t=4))
-        for c in (1, 2):
+        load_w1(w1_raw1[0], 1, slice(0, H // 2))
+        load_w1(w1_raw1[1], 1, slice(H // 2, H))
+        first_bias = held("first_bias", [P, 4], F32)
+        for c in range(3):
             load_wo(wo_raw[c], wo_cols[c])
         nc.scalar.activation(rows[0:96, :], w1_raw0[0:96, 0, 0:P], ACT.Tanh, scale=0.0)
         cast_w1(0, w1_raw0, slice(0, P))
@@ -242,65 +251,88 @@ def tile_list_trigram_next_logits_kernel(
         acc0 = [bank(b, "acc") for b in range(4)]
         acc1 = [bank(b, "acc") for b in range(4, BANKS)]
         words0 = held("words0", [P, S], U32)
-        gather_words(everyone, 0, 0, words0[:])
-        reorder(w_sc, w_sc_raw, U8, 16)
+        for half in halves:
+            gather_words(half, 0, 0, words0[:, half])
         reorder(w3_codes, w3_raw, U16, 8)
-        reorder(w2_codes, w2_raw, I32, 4)
-        words12 = held("words12", [P, 2, S], U32, "w2_raw")
+        for a in range(PASSES):
+            reorder_pass(w_sc[a][:], w_sc_raw[:, a, :], U8, 16)
+            reorder_pass(w2_codes[a][:], w2_raw[:, a, :], I32, 4)
+        words12 = held("words12", [P, 2, S], U32, "w3_raw")
         first_words = [words0[:], words12[:, 0, :], words12[:, 1, :]]
-        for u in (1, 2):
-            for half in halves:
-                gather_words(half, u, 0, first_words[u][:, half])
-        for u in range(3):
-            for s, acc in enumerate((acc0, acc1)):
-                first_product(s, acc, u, 0, first_words[u][:, halves[s]], u == 0, False)
+        early = [(0, 0), (0, 1), (2, 0), (1, 0), (1, 1)]
+        for u, s in early[2:]:
+            gather_words(halves[s], u, 0, first_words[u][:, halves[s]])
+        for u, s in early:
+            first_product(s, (acc0, acc1)[s], u, 0, first_words[u][:, halves[s]], u == 0, False)
 
         second_words = held("second_words", [P, 3, HALF], U32)
         for u in (1, 2, 0):
             gather_words(halves[0], u, 1, second_words[:, u, :])
         cast_w1(1, w1_raw1[1], slice(P // 2, P))
         quantize_w1(1)
-        last_words = held("last_words", [P, 3, HALF], U32, "w1_bf1")
+        last_words = held("last_words", [P, 4, HALF], U32, "w1_bf1")
+        last = ((2, 0), (1, 1), (2, 1), (0, 1))
+        for e, (u, a) in enumerate(last):
+            gather_words(halves[1], u, a, last_words[:, e, :])
         for u in (1, 2, 0):
-            gather_words(halves[1], u, 1, last_words[:, u, :])
-        for s, acc, words in ((0, acc0, second_words), (1, acc1, last_words)):
-            for u in (1, 2, 0):
-                first_product(s, acc, u, 1, words[:, u, :], False, u == 0)
+            first_product(0, acc0, u, 1, second_words[:, u, :], False, u == 0)
+        for e, (u, a) in enumerate(last):
+            first_product(1, acc1, u, a, last_words[:, e, :], False, u == 0)
 
         wo0_bf = held("wo0_bf", [P, 1024], BF16)
-        cast_wo(wo0_bf[:], wo_raw[0][:], nc.scalar.copy)
-        quantize_wo(slice(0, 256), wo0_bf[:])
-        wo2_bf = held("wo2_bf", [P, 1024], BF16)
-        cast_wo(wo2_bf[:], wo_raw[1][:, :, 256:512], gpsimd_cast)
-        th0 = [held("th0_%d" % v, [P, 4, SUB], F32, tag) for v, tag in enumerate(("wo_raw0", "th0_1"))]
+        gpsimd_cast(wo0_bf[:].rearrange("p (m t) -> p m t", t=4), wo_raw[0][:].rearrange("p t m -> p m t"))
+        th0 = [held("th0_%d" % v, [P, 4, SUB], F32) for v in range(2)]
         th1 = [held("th1_%d" % v, [P, 4, SUB], F32) for v in range(2)]
         squash(acc0, th0, first_bias)
-        wo1_bf = held("wo1_bf", [P, 1024], BF16, "first_bias")
-        cast_wo(wo1_bf[:], wo_raw[1][:, :, 0:256], nc.scalar.copy)
+        wo1_bf = held("wo1_bf", [P, 2048], BF16, "first_bias")
+        for e in range(2):
+            cast_wo(wo1_bf[:, 1024 * e : 1024 * (e + 1)], wo_raw[1][:, :, 256 * e : 256 * (e + 1)], nc.scalar.copy)
         squash(acc1, th1, bh_cols)
-        for v in range(2):
-            apply_gain(0, v, th0)
-        for v in range(2):
-            quantize_h(0, v)
-        quantize_wo(slice(256, 512), wo1_bf[:], "h_bf0")
-        apply_gain(1, 0, th1)
-        quantize_wo(slice(512, 768), wo2_bf[:], "th0_1")
-        apply_gain(1, 1, th1)
-        for v in range(2):
-            quantize_h(1, v)
-        wo3_bf = held("wo3_bf", [P, 1024], BF16, "th1_0")
-        wo4_bf = held("wo4_bf", [P, 2048], BF16, "th1_1")
+
+        def gpsimd_gain(dst, src):
+            width = src.shape[2]
+            nc.gpsimd.tensor_tensor(
+                dst.rearrange("p (m t) -> p m t", t=4),
+                src.rearrange("p t m -> p m t"),
+                gain_cols[:].unsqueeze(1).to_broadcast([P, width, 4]),
+                ALU.mult,
+            )
+
+        gpsimd_gain(h_bf[0][:, 0, :], th0[0][:])
+        late = over_table("late", [P, 768], U32, 0)
+        h_codes[0] = late[:, 0:HALF]
+        tail_bf = over_table("tail_bf", [P, 1024], BF16, 4096)[:]
+        vector_gain(tail_bf, th0[1][:])
+        nc.vector.quantize_mx(out=late[:, 512:768].bitcast(FP8X4), scales=wo_sc[:, 0:256], in_=wo0_bf[:])
+        wo_codes[0] = late[:, 512:640]
+        wo_codes[1] = late[:, 640:768]
+        quantize_h(0, slice(0, 256), h_bf[0][:, 0, :])
+        quantize_h(0, slice(256, 512), tail_bf)
+
+        quantize_wo(slice(256, 768), wo1_bf[:], over_table("wo_codes256", [P, 512], U32, 4096))
+
+        def second_half():
+            vector_gain(h_bf[1][:, 0, :], th1[0][:])
+            vector_gain(h_bf[1][:, 1, :], th1[1][:])
+            for v in range(2):
+                quantize_h(1, slice(v * SUB, (v + 1) * SUB), h_bf[1][:, v, :])
+
 
         stores = [[(i, 0)] for i in range(EARLY_TILES)]
-        stores.extend([(i, 1), (i + 1, 1)] for i in range(0, EARLY_TILES, 2))
+        stores.extend([(i, 1)] for i in range(2))
+        stores.extend([(i, 1), (i + 1, 1)] for i in range(2, EARLY_TILES, 2))
         for first, last in ((6, 7), (7, 9), (9, 12)):
             stores.append([(i, s) for i in range(first, last) for s in range(2)])
         done = 0
         for n, parts in enumerate(stores):
             turns = range(done, done + len(parts))
-            logits(n, parts, [k % BANKS for k in turns], [k == EARLY_TILES + 1 or (k >= SCALAR_ONLY and k % 2 == 0) for k in turns])
+            logits(n, parts, [k % BANKS for k in turns], [k == 0 or (k >= SCALAR_ONLY and k % 2 == 0) for k in turns])
             done = done + len(parts)
-            if n == EARLY_TILES:
+            if n == 0:
+                second_half()
+            if n == EARLY_TILES - 1:
+                wo3_bf = held("wo3_bf", [P, 1024], BF16, "th1_0")
+                wo4_bf = held("wo4_bf", [P, 2048], BF16, "th1_1")
                 cast_wo(wo3_bf[:], wo_raw[2][:, :, 0:256], nc.vector.tensor_copy)
                 cast_wo(wo4_bf[:], wo_raw[2][:, :, 256:768], nc.vector.tensor_copy)
                 quantize_wo(slice(768, 1024), wo3_bf[:])

@@ -51,33 +51,34 @@ def tile_list_trigram_next_logits_kernel(
 
         lists = [held("list%d" % u, [P, S // 16], U16) for u in range(3)]
         table_scales = held("table_scales", [P, T // 4], I32)
-        widths = (S, 2 * S)
-        picked_scales = [held("picked_scales%d" % e, [P, w], U8) for e, w in enumerate(widths)]
-        planes = [held("planes%d" % e, [P, PASSES, w // 4], I32) for e, w in enumerate(widths)]
+        picked_scales = [held("picked_scales%d" % u, [P, S], U8) for u in range(3)]
+        planes = [held("planes%d" % u, [P, PASSES, S // 4], I32) for u in range(3)]
+        plane_row = (2 * SHIFT, SHIFT, 0)
         ident = held("ident", [P, P], F32)
         w1_bf = [held("w1_bf%d" % a, [P, 4 * H], BF16) for a in range(PASSES)]
         w1_codes = [held("w1_codes%d" % a, [P, H], U32) for a in range(PASSES)]
         w1_sc = [held("w1_sc%d" % a, [P, H], U8) for a in range(PASSES)]
         w2_codes = [held("w2_codes%d" % a, [P, H], I32) for a in range(PASSES)]
         w3_codes = held("w3_codes", [P, PASSES, H // 2], I32)
-        w_sc_raw = held("w_sc_raw", [P, PASSES, H // 4], I32)
-        w_sc = [held("w_sc%d" % a, [P, H // 4], I32) for a in range(PASSES)]
+        w_sc_raw = {u: held("w_sc_raw%d" % u, [P, PASSES, H // 4], I32) for u in (1, 2)}
+        w_sc = {(u, a): held("w_sc%d%d" % (u, a), [P, H // 4], I32) for u in (1, 2) for a in range(PASSES)}
         wo_sc = held("wo_sc", [P, N], U8)
         wo_codes = {}
-        h_bf = [held("h_bf%d" % s, [P, 2, 4 * SUB], BF16) for s in range(2)]
+        h1_bf = held("h1_bf", [P, 2, 4 * SUB], BF16)
         h_codes = {1: held("h_codes1", [P, HALF], U32)[:]}
         h_sc = [held("h_sc%d" % s, [P, HALF], U8) for s in range(2)]
         table = [held("table0", [P, T], I32), over_table("table1", [P, T], I32, 0)]
         rows = held("rows", [P, P], F32)
         w1_raw0 = held("w1_raw0", [P, 4, H], F32)
-        w1_raw1 = [held("w1_raw1_%d" % e, [P, 4, H // 2], F32) for e in range(2)]
+        w1_raw1 = held("w1_raw1", [P, 4, H], F32)
         w2_raw = held("w2_raw", [P, PASSES, H], I32)
         w3_raw = held("w3_raw", [P, PASSES, H // 2], I32)
-        wo_cols = (slice(0, 256), slice(256, 768), slice(768, N))
+        wo_cols = (slice(0, 512), slice(512, 768), slice(768, N))
         wo_raw = [held("wo_raw%d" % c, [P, 4, cols.stop - cols.start], F32) for c, cols in enumerate(wo_cols)]
 
-        nc.vector.memset(w_sc_raw[:], 0)
+        nc.vector.memset(w_sc_raw[2][:], 0)
         nc.vector.memset(table_scales[0:STAGE_ROW, :], 0)
+        nc.vector.memset(w_sc_raw[1][:], 0)
         nc.vector.memset(rows[96:BO_ROW, :], 0.0)
         for tile in planes:
             nc.gpsimd.memset(tile[:], 0)
@@ -86,10 +87,11 @@ def tile_list_trigram_next_logits_kernel(
         bh_cols = held("bh_cols", [P, 4], F32)
         gain_cols = held("gain_cols", [P, 4], F32)
 
-        def load_weight_scales(first, src, quadrants):
-            for q in quadrants:
+        def load_weight_scales(u, src):
+            for q in (0, 2, 1, 3):
+                row = 32 * q + plane_row[u]
                 nc.sync.dma_start(
-                    w_sc_raw[32 * q + first : 32 * q + first + 4, :, :],
+                    w_sc_raw[u][row : row + 4, :, :],
                     src[:, 4 * q : 4 * q + 4, :].bitcast(I32).rearrange("a r c -> r a c"),
                 )
 
@@ -105,18 +107,16 @@ def tile_list_trigram_next_logits_kernel(
         def move_planes(e):
             for q in (0, 2, 1, 3):
                 first = STAGE_ROW + 8 * q
-                nc.sync.dma_start(planes[e][32 * q : 32 * q + 4, :, :], picked_scales[e][first : first + 8, :].bitcast(I32))
+                row = 32 * q + plane_row[e]
+                nc.sync.dma_start(planes[e][row : row + 4, :, :], picked_scales[e][first : first + 8, :].bitcast(I32))
 
         nc.sync.dma_start(table_scales[STAGE_ROW:P, :], tab_scales.bitcast(I32).rearrange("a q t -> q a t"))
         nc.sync.dma_start(lists[0][:], offs)
-        nc.sync.dma_start(lists[1][:], offs2)
-        load_w1(w1_raw0, 0, slice(0, H))
         nc.sync.dma_start(lists[2][:], offs3)
-        load_weight_scales(SHIFT, w2_scales, range(4))
+        load_w1(w1_raw0, 0, slice(0, H))
+        nc.sync.dma_start(lists[1][:], offs2)
+        load_weight_scales(2, w3_scales)
         load_table(0, slice(0, T))
-        load_weight_scales(0, w3_scales, range(4))
-        nc.sync.dma_start(w3_raw[:], w3_words.rearrange("a p b -> p a b").bitcast(I32))
-        nc.sync.dma_start(w2_raw[:], w2_words.rearrange("a p c i -> p a (c i)").bitcast(I32))
 
         halves = [slice(0, HALF), slice(HALF, S)]
 
@@ -124,9 +124,9 @@ def tile_list_trigram_next_logits_kernel(
             picks = lists[u][:, contexts.start // 16 : contexts.stop // 16]
             nc.vector.tensor_copy(dst, table[a][:].bitcast(U32).indirect(picks))
 
-        def cast_w1(a, raw, places):
+        def cast_w1(a, raw, places, copy):
             dst = w1_bf[a][:].rearrange("p (t m j) -> p m t j", t=4, j=4)
-            nc.scalar.copy(dst[:, places], raw[:].rearrange("p j (m t) -> p m t j", t=4))
+            copy(dst[:, places], raw[:].rearrange("p j (m t) -> p m t j", t=4)[:, places])
 
         def quantize_w1(a):
             nc.vector.quantize_mx(out=w1_codes[a][:].bitcast(FP8X4), scales=w1_sc[a][:], in_=w1_bf[a][:])
@@ -144,23 +144,23 @@ def tile_list_trigram_next_logits_kernel(
             )
 
         def first_product(s, acc, u, a, x_words, start, stop):
-            x_first = max(u - 1, 0) * S + s * HALF
+            x_first = s * HALF
             for t in range(4):
                 if u == 0:
                     lhs = w1_codes[a][:, t * P : (t + 1) * P].bitcast(FP8X4)
                     lhs_sc = w1_sc[a][:, t * P : (t + 1) * P]
                 elif u == 1:
                     lhs = w2_codes[a][:, t * P : (t + 1) * P].bitcast(FP8X4)
-                    lhs_sc = w_sc[a][SHIFT:P, t * 32 : (t + 1) * 32].bitcast(U8)
+                    lhs_sc = w_sc[1, a][SHIFT:P, t * 32 : (t + 1) * 32].bitcast(U8)
                 else:
                     lhs = w3_codes[:, a, t * 64 : (t + 1) * 64].bitcast(U8).bitcast(FP4X4)
-                    lhs_sc = w_sc[a][:, t * 32 : (t + 1) * 32].bitcast(U8)
+                    lhs_sc = w_sc[2, a][:, t * 32 : (t + 1) * 32].bitcast(U8)
                 nc.tensor.matmul_mx(
                     out=acc[t][:],
                     lhsT=lhs,
                     lhsT_scale=lhs_sc,
                     rhs=x_words.bitcast(FP8X4),
-                    rhs_scale=planes[min(u, 1)][:, a, :].bitcast(U8)[:, x_first : x_first + HALF],
+                    rhs_scale=planes[u][plane_row[u] : P, a, :].bitcast(U8)[:, x_first : x_first + HALF],
                     start=start,
                     stop=stop,
                 )
@@ -224,29 +224,30 @@ def tile_list_trigram_next_logits_kernel(
                 dst.rearrange("(e p) n -> p e n", p=P), staged[:].rearrange("p (e s) n -> p e (s n)", s=s1 - s0 + 1)
             )
 
-        for u, dst in enumerate((picked_scales[0][:], picked_scales[1][:, 0:S], picked_scales[1][:, S : 2 * S])):
-            nc.vector.tensor_copy(dst, table_scales[:].bitcast(U8).indirect(lists[u][:]))
+        for u in (0, 2, 1):
+            nc.vector.tensor_copy(picked_scales[u][:], table_scales[:].bitcast(U8).indirect(lists[u][:]))
         move_planes(0)
-        load_table(1, slice(0, T // 2))
+        nc.sync.dma_start(w3_raw[:], w3_words.rearrange("a p b -> p a b").bitcast(I32))
+        nc.sync.dma_start(w2_raw[:], w2_words.rearrange("a p c i -> p a (c i)").bitcast(I32))
+        load_weight_scales(1, w2_scales)
+        load_table(1, slice(0, 1536))
+        move_planes(2)
+        load_table(1, slice(1536, 3072))
         move_planes(1)
-        load_table(1, slice(T // 2, T))
+        load_table(1, slice(3072, T))
         nc.sync.dma_start(bh_cols[:], bh.rearrange("(p t) -> p t", t=4))
         nc.sync.dma_start(gain_cols[:], gain.rearrange("(p t) -> p t", t=4))
-        load_w1(w1_raw1[0], 1, slice(0, H // 2))
-        load_w1(w1_raw1[1], 1, slice(H // 2, H))
-        first_bias = held("first_bias", [P, 4], F32)
+        load_w1(w1_raw1, 1, slice(0, H))
         for c in range(3):
             load_wo(wo_raw[c], wo_cols[c])
         nc.scalar.activation(rows[0:96, :], w1_raw0[0:96, 0, 0:P], ACT.Tanh, scale=0.0)
-        cast_w1(0, w1_raw0, slice(0, P))
+        cast_w1(0, w1_raw0, slice(0, P), nc.scalar.copy)
         quantize_w1(0)
-        cast_w1(1, w1_raw1[0], slice(0, P // 2))
 
         turned = bank(BANKS - 1, "turned")
         nc.tensor.transpose(turned[:, 0:P], rows[:], ident[:])
         consts = held("consts", [P, OUT_TILES], F32)
         nc.scalar.copy(consts[:], turned[:, BO_ROW:P])
-        nc.scalar.copy(first_bias[:], bh_cols[:])
 
         acc0 = [bank(b, "acc") for b in range(4)]
         acc1 = [bank(b, "acc") for b in range(4, BANKS)]
@@ -255,84 +256,80 @@ def tile_list_trigram_next_logits_kernel(
             gather_words(half, 0, 0, words0[:, half])
         reorder(w3_codes, w3_raw, U16, 8)
         for a in range(PASSES):
-            reorder_pass(w_sc[a][:], w_sc_raw[:, a, :], U8, 16)
+            reorder_pass(w_sc[2, a][:], w_sc_raw[2][:, a, :], U8, 16)
+        for a in range(PASSES):
             reorder_pass(w2_codes[a][:], w2_raw[:, a, :], I32, 4)
+            reorder_pass(w_sc[1, a][:], w_sc_raw[1][:, a, :], U8, 16)
         words12 = held("words12", [P, 2, S], U32, "w3_raw")
         first_words = [words0[:], words12[:, 0, :], words12[:, 1, :]]
-        early = [(0, 0), (0, 1), (2, 0), (1, 0), (1, 1)]
+        early = [(u, s) for u in (0, 2, 1) for s in range(2)]
         for u, s in early[2:]:
             gather_words(halves[s], u, 0, first_words[u][:, halves[s]])
         for u, s in early:
             first_product(s, (acc0, acc1)[s], u, 0, first_words[u][:, halves[s]], u == 0, False)
 
-        second_words = held("second_words", [P, 3, HALF], U32)
-        for u in (1, 2, 0):
+        second_words = held("second_words", [P, 4, HALF], U32)
+        for u in (2, 1, 0):
             gather_words(halves[0], u, 1, second_words[:, u, :])
-        cast_w1(1, w1_raw1[1], slice(P // 2, P))
+        gather_words(halves[1], 2, 1, second_words[:, 3, :])
+        cast_w1(1, w1_raw1, slice(0, P // 2), nc.scalar.copy)
+        cast_w1(1, w1_raw1, slice(P // 2, P), gpsimd_cast)
         quantize_w1(1)
-        last_words = held("last_words", [P, 4, HALF], U32, "w1_bf1")
-        last = ((2, 0), (1, 1), (2, 1), (0, 1))
-        for e, (u, a) in enumerate(last):
-            gather_words(halves[1], u, a, last_words[:, e, :])
-        for u in (1, 2, 0):
-            first_product(0, acc0, u, 1, second_words[:, u, :], False, u == 0)
-        for e, (u, a) in enumerate(last):
-            first_product(1, acc1, u, a, last_words[:, e, :], False, u == 0)
+        last_words = held("last_words", [P, 2, HALF], U32, "w1_bf1")
+        for e, u in enumerate((1, 0)):
+            gather_words(halves[1], u, 1, last_words[:, e, :])
+        for u in (2, 1):
+            first_product(0, acc0, u, 1, second_words[:, u, :], False, False)
+        first_product(1, acc1, 2, 1, second_words[:, 3, :], False, False)
+        first_product(0, acc0, 0, 1, second_words[:, 0, :], False, True)
+        for e, u in enumerate((1, 0)):
+            first_product(1, acc1, u, 1, last_words[:, e, :], False, u == 0)
 
         wo0_bf = held("wo0_bf", [P, 1024], BF16)
-        gpsimd_cast(wo0_bf[:].rearrange("p (m t) -> p m t", t=4), wo_raw[0][:].rearrange("p t m -> p m t"))
-        th0 = [held("th0_%d" % v, [P, 4, SUB], F32) for v in range(2)]
-        th1 = [held("th1_%d" % v, [P, 4, SUB], F32) for v in range(2)]
-        squash(acc0, th0, first_bias)
-        wo1_bf = held("wo1_bf", [P, 2048], BF16, "first_bias")
-        for e in range(2):
-            cast_wo(wo1_bf[:, 1024 * e : 1024 * (e + 1)], wo_raw[1][:, :, 256 * e : 256 * (e + 1)], nc.scalar.copy)
-        squash(acc1, th1, bh_cols)
+        cast_wo(wo0_bf[:], wo_raw[0][:, :, 0:256], nc.scalar.copy)
+        wo1_bf = held("wo1_bf", [P, 2048], BF16)
+        for e, src in enumerate((wo_raw[0][:, :, 256:512], wo_raw[1][:])):
+            gpsimd_cast(wo1_bf[:, 1024 * e : 1024 * (e + 1)].rearrange("p (m t) -> p m t", t=4), src.rearrange("p t m -> p m t"))
+        th0 = [held("th0_%d" % v, [P, 4, SUB], F32, tag) for v, tag in enumerate(("wo_raw0", "th0_1"))]
+        th1 = held("th1", [P, 4, HALF], F32)
+        squash(acc0, th0, bh_cols)
+        for t in range(4):
+            nc.scalar.activation(th1[:, t, :], acc1[t][:], ACT.Tanh, bias=bh_cols[:, t : t + 1])
 
-        def gpsimd_gain(dst, src):
-            width = src.shape[2]
-            nc.gpsimd.tensor_tensor(
-                dst.rearrange("p (m t) -> p m t", t=4),
-                src.rearrange("p t m -> p m t"),
-                gain_cols[:].unsqueeze(1).to_broadcast([P, width, 4]),
-                ALU.mult,
-            )
-
-        gpsimd_gain(h_bf[0][:, 0, :], th0[0][:])
         late = over_table("late", [P, 768], U32, 0)
         h_codes[0] = late[:, 0:HALF]
-        tail_bf = over_table("tail_bf", [P, 1024], BF16, 4096)[:]
-        vector_gain(tail_bf, th0[1][:])
+        h0_bf = [over_table("h0_bf%d" % v, [P, 4 * SUB], BF16, 4096 + 2048 * v) for v in range(2)]
+        for v in range(2):
+            vector_gain(h0_bf[v][:], th0[v][:])
         nc.vector.quantize_mx(out=late[:, 512:768].bitcast(FP8X4), scales=wo_sc[:, 0:256], in_=wo0_bf[:])
         wo_codes[0] = late[:, 512:640]
         wo_codes[1] = late[:, 640:768]
-        quantize_h(0, slice(0, 256), h_bf[0][:, 0, :])
-        quantize_h(0, slice(256, 512), tail_bf)
+        for v in range(2):
+            quantize_h(0, slice(v * SUB, (v + 1) * SUB), h0_bf[v][:])
 
-        quantize_wo(slice(256, 768), wo1_bf[:], over_table("wo_codes256", [P, 512], U32, 4096))
+        quantize_wo(slice(256, 768), wo1_bf[:], over_table("wo_codes256", [P, 512], U32, 6144))
 
         def second_half():
-            vector_gain(h_bf[1][:, 0, :], th1[0][:])
-            vector_gain(h_bf[1][:, 1, :], th1[1][:])
+            vector_gain(h1_bf[:, 0, :], th1[:, :, 0:SUB])
+            vector_gain(h1_bf[:, 1, :], th1[:, :, SUB:HALF])
             for v in range(2):
-                quantize_h(1, slice(v * SUB, (v + 1) * SUB), h_bf[1][:, v, :])
+                quantize_h(1, slice(v * SUB, (v + 1) * SUB), h1_bf[:, v, :])
 
 
         stores = [[(i, 0)] for i in range(EARLY_TILES)]
-        stores.extend([(i, 1)] for i in range(2))
-        stores.extend([(i, 1), (i + 1, 1)] for i in range(2, EARLY_TILES, 2))
+        stores.extend([(i, 1)] for i in range(EARLY_TILES))
         for first, last in ((6, 7), (7, 9), (9, 12)):
             stores.append([(i, s) for i in range(first, last) for s in range(2)])
         done = 0
         for n, parts in enumerate(stores):
             turns = range(done, done + len(parts))
-            logits(n, parts, [k % BANKS for k in turns], [k == 0 or (k >= SCALAR_ONLY and k % 2 == 0) for k in turns])
+            logits(n, parts, [k % BANKS for k in turns], [k >= SCALAR_ONLY and k % 2 == 0 for k in turns])
             done = done + len(parts)
             if n == 0:
                 second_half()
             if n == EARLY_TILES - 1:
-                wo3_bf = held("wo3_bf", [P, 1024], BF16, "th1_0")
-                wo4_bf = held("wo4_bf", [P, 2048], BF16, "th1_1")
+                wo3_bf = held("wo3_bf", [P, 1024], BF16, "th1")
+                wo4_bf = held("wo4_bf", [P, 2048], BF16, "h1_bf")
                 cast_wo(wo3_bf[:], wo_raw[2][:, :, 0:256], nc.vector.tensor_copy)
                 cast_wo(wo4_bf[:], wo_raw[2][:, :, 256:768], nc.vector.tensor_copy)
                 quantize_wo(slice(768, 1024), wo3_bf[:])

@@ -59,7 +59,7 @@ def tile_list_trigram_next_logits_kernel(
         w1_codes = [held("w1_codes%d" % a, [P, H], U32) for a in range(PASSES)]
         w1_sc = [held("w1_sc%d" % a, [P, H], U8) for a in range(PASSES)]
         w2_codes = [held("w2_codes%d" % a, [P, H], I32) for a in range(PASSES)]
-        w3_codes = held("w3_codes", [P, PASSES, H // 2], I32)
+        w3_codes = [held("w3_codes%d" % a, [P, H // 2], I32) for a in range(PASSES)]
         w_sc_raw = {u: held("w_sc_raw%d" % u, [P, PASSES, H // 4], I32) for u in (1, 2)}
         w_sc = {(u, a): held("w_sc%d%d" % (u, a), [P, H // 4], I32) for u in (1, 2) for a in range(PASSES)}
         wo_sc = held("wo_sc", [P, N], U8)
@@ -131,12 +131,6 @@ def tile_list_trigram_next_logits_kernel(
         def quantize_w1(a):
             nc.vector.quantize_mx(out=w1_codes[a][:].bitcast(FP8X4), scales=w1_sc[a][:], in_=w1_bf[a][:])
 
-        def reorder(dst, src, dtype, line):
-            nc.vector.tensor_copy(
-                dst[:].bitcast(dtype).rearrange("p a (t m i) -> p a m t i", t=4, i=line),
-                src[:].bitcast(dtype).rearrange("p a (m i t) -> p a m t i", t=4, i=line),
-            )
-
         def reorder_pass(dst, src, dtype, line):
             nc.gpsimd.tensor_copy(
                 dst.bitcast(dtype).rearrange("p (t m i) -> p m t i", t=4, i=line),
@@ -153,7 +147,7 @@ def tile_list_trigram_next_logits_kernel(
                     lhs = w2_codes[a][:, t * P : (t + 1) * P].bitcast(FP8X4)
                     lhs_sc = w_sc[1, a][SHIFT:P, t * 32 : (t + 1) * 32].bitcast(U8)
                 else:
-                    lhs = w3_codes[:, a, t * 64 : (t + 1) * 64].bitcast(U8).bitcast(FP4X4)
+                    lhs = w3_codes[a][:, t * 64 : (t + 1) * 64].bitcast(U8).bitcast(FP4X4)
                     lhs_sc = w_sc[2, a][:, t * 32 : (t + 1) * 32].bitcast(U8)
                 nc.tensor.matmul_mx(
                     out=acc[t][:],
@@ -254,13 +248,13 @@ def tile_list_trigram_next_logits_kernel(
         words0 = held("words0", [P, S], U32)
         for half in halves:
             gather_words(half, 0, 0, words0[:, half])
-        reorder(w3_codes, w3_raw, U16, 8)
         for a in range(PASSES):
             reorder_pass(w_sc[2, a][:], w_sc_raw[2][:, a, :], U8, 16)
         for a in range(PASSES):
+            reorder_pass(w3_codes[a][:], w3_raw[:, a, :], U16, 8)
             reorder_pass(w2_codes[a][:], w2_raw[:, a, :], I32, 4)
             reorder_pass(w_sc[1, a][:], w_sc_raw[1][:, a, :], U8, 16)
-        words12 = held("words12", [P, 2, S], U32, "w3_raw")
+        words12 = held("words12", [P, 2, S], U32)
         first_words = [words0[:], words12[:, 0, :], words12[:, 1, :]]
         early = [(u, s) for u in (0, 2, 1) for s in range(2)]
         for u, s in early[2:]:
@@ -296,18 +290,18 @@ def tile_list_trigram_next_logits_kernel(
         for t in range(4):
             nc.scalar.activation(th1[:, t, :], acc1[t][:], ACT.Tanh, bias=bh_cols[:, t : t + 1])
 
-        late = over_table("late", [P, 768], U32, 0)
+        late = over_table("late", [P, 640], U32, 0)
         h_codes[0] = late[:, 0:HALF]
         h0_bf = [over_table("h0_bf%d" % v, [P, 4 * SUB], BF16, 4096 + 2048 * v) for v in range(2)]
         for v in range(2):
             vector_gain(h0_bf[v][:], th0[v][:])
-        nc.vector.quantize_mx(out=late[:, 512:768].bitcast(FP8X4), scales=wo_sc[:, 0:256], in_=wo0_bf[:])
+        nc.vector.quantize_mx(out=late[:, 512:640].bitcast(FP8X4), scales=wo_sc[:, 0:P], in_=wo0_bf[:, 0:512])
         wo_codes[0] = late[:, 512:640]
-        wo_codes[1] = late[:, 640:768]
         for v in range(2):
             quantize_h(0, slice(v * SUB, (v + 1) * SUB), h0_bf[v][:])
 
-        quantize_wo(slice(256, 768), wo1_bf[:], over_table("wo_codes256", [P, 512], U32, 6144))
+        quantize_wo(slice(P, 256), wo0_bf[:, 512:1024], over_table("wo_codes128", [P, P], U32, 6144))
+        quantize_wo(slice(256, 768), wo1_bf[:], over_table("wo_codes256", [P, 512], U32, 6144 + 512))
 
         def second_half():
             vector_gain(h1_bf[:, 0, :], th1[:, :, 0:SUB])

from contextlib import ExitStack

import concourse.mybir as mybir
from concourse.masks import make_identity

K, T, S, H, N = 1024, 4096, 1024, 512, 1536
FLOPS = 2 * S * (3 * K * H + H * N)

F32 = mybir.dt.float32
BF16 = mybir.dt.bfloat16
I32 = mybir.dt.int32
U32 = mybir.dt.uint32
U16 = mybir.dt.uint16
U8 = mybir.dt.uint8
FP8X4 = mybir.dt.float8_e4m3fn_x4
FP4X4 = mybir.dt.float4_e2m1fn_x4
ACT = mybir.ActivationFunctionType
ALU = mybir.AluOpType

P = 128
PASSES = K // 512
HALF = S // 2
SUB = HALF // 2
CHUNK = 512
OUT_TILES = N // P
EARLY_TILES = 6
SCALAR_ONLY = 12
BANKS = 8
SHIFT = 4
STAGE_ROW = 96
BO_ROW = P - OUT_TILES


def tile_list_trigram_next_logits_kernel(
    tc, tab_words, tab_scales, offs, offs2, offs3, w1, w2_words, w2_scales, w3_words, w3_scales, bh, gain, wo, bo, out
):
    nc = tc.nc
    with ExitStack() as ctx:
        keep = ctx.enter_context(tc.tile_pool(name="keep", bufs=1))
        shared = ctx.enter_context(tc.tile_pool(name="shared", bufs=1))
        psum = ctx.enter_context(tc.psum_pool(name="psum", bufs=1))

        def held(name, shape, dtype, tag=None):
            return keep.tile(shape, dtype, name=name, tag=tag or name, align_bytes=64)

        def over_table(name, shape, dtype, offset):
            return shared.tile(shape, dtype, name=name, offset=offset, align_bytes=64)

        def bank(b, name):
            return psum.tile([P, HALF], F32, name=name, tag="bank%d" % b)

        lists = [held("list%d" % u, [P, S // 16], U16) for u in range(3)]
        table_scales = held("table_scales", [P, T // 4], I32)
        picked_scales = [held("picked_scales%d" % u, [P, S], U8) for u in range(3)]
        planes = [held("planes%d" % u, [P, PASSES, S // 4], I32) for u in range(3)]
        plane_row = (2 * SHIFT, SHIFT, 0)
        ident = held("ident", [P, P], F32)
        w1_bf = [held("w1_bf%d" % a, [P, 4 * H], BF16) for a in range(PASSES)]
        w1_codes = [held("w1_codes%d" % a, [P, H], U32) for a in range(PASSES)]
        w1_sc = [held("w1_sc%d" % a, [P, H], U8) for a in range(PASSES)]
        w2_codes = [held("w2_codes%d" % a, [P, H], I32) for a in range(PASSES)]
        w3_codes = [held("w3_codes%d" % a, [P, H // 2], I32) for a in range(PASSES)]
        w_sc_raw = {u: held("w_sc_raw%d" % u, [P, PASSES, H // 4], I32) for u in (1, 2)}
        w_sc = {(u, a): held("w_sc%d%d" % (u, a), [P, H // 4], I32) for u in (1, 2) for a in range(PASSES)}
        wo_sc = held("wo_sc", [P, N], U8)
        wo_codes = {}
        h1_bf = held("h1_bf", [P, 2, 4 * SUB], BF16)
        h_codes = {1: held("h_codes1", [P, HALF], U32)[:]}
        h_sc = [held("h_sc%d" % s, [P, HALF], U8) for s in range(2)]
        table = [held("table0", [P, T], I32), over_table("table1", [P, T], I32, 0)]
        rows = held("rows", [P, P], F32)
        w1_raw0 = held("w1_raw0", [P, 4, H], F32)
        w1_raw1 = held("w1_raw1", [P, 4, H], F32)
        w2_raw = held("w2_raw", [P, PASSES, H], I32)
        w3_raw = held("w3_raw", [P, PASSES, H // 2], I32)
        wo_cols = (slice(0, 512), slice(512, 768), slice(768, N))
        wo_raw = [held("wo_raw%d" % c, [P, 4, cols.stop - cols.start], F32) for c, cols in enumerate(wo_cols)]

        nc.vector.memset(w_sc_raw[2][:], 0)
        nc.vector.memset(table_scales[0:STAGE_ROW, :], 0)
        nc.vector.memset(w_sc_raw[1][:], 0)
        nc.vector.memset(rows[96:BO_ROW, :], 0.0)
        for tile in planes:
            nc.gpsimd.memset(tile[:], 0)
        make_identity(nc, ident[:])
        nc.gpsimd.dma_start(rows[BO_ROW:P, :], bo.rearrange("(i p) -> i p", p=P))
        bh_cols = held("bh_cols", [P, 4], F32)
        gain_cols = held("gain_cols", [P, 4], F32)

        def load_weight_scales(u, src):
            for q in (0, 2, 1, 3):
                row = 32 * q + plane_row[u]
                nc.sync.dma_start(
                    w_sc_raw[u][row : row + 4, :, :],
                    src[:, 4 * q : 4 * q + 4, :].bitcast(I32).rearrange("a r c -> r a c"),
                )

        def load_table(a, cols):
            nc.sync.dma_start(table[a][:, cols], tab_words[a].rearrange("p t i -> p (t i)").bitcast(I32)[:, cols])

        def load_w1(dst, a, cols):
            nc.sync.dma_start(dst[:], w1[a * 512 : (a + 1) * 512, cols].rearrange("(p j) c -> p j c", j=4))

        def load_wo(dst, cols):
            nc.sync.dma_start(dst[:], wo[:, cols].rearrange("(p t) n -> p t n", t=4))

        def move_planes(e):
            for q in (0, 2, 1, 3):
                first = STAGE_ROW + 8 * q
                row = 32 * q + plane_row[e]
                nc.sync.dma_start(planes[e][row : row + 4, :, :], picked_scales[e][first : first + 8, :].bitcast(I32))

        nc.sync.dma_start(table_scales[STAGE_ROW:P, :], tab_scales.bitcast(I32).rearrange("a q t -> q a t"))
        nc.sync.dma_start(lists[0][:], offs)
        nc.sync.dma_start(lists[2][:], offs3)
        load_w1(w1_raw0, 0, slice(0, H))
        nc.sync.dma_start(lists[1][:], offs2)
        load_weight_scales(2, w3_scales)
        load_table(0, slice(0, T))

        halves = [slice(0, HALF), slice(HALF, S)]

        def gather_words(contexts, u, a, dst):
            picks = lists[u][:, contexts.start // 16 : contexts.stop // 16]
            nc.vector.tensor_copy(dst, table[a][:].bitcast(U32).indirect(picks))

        def cast_w1(a, raw, places, copy):
            dst = w1_bf[a][:].rearrange("p (t m j) -> p m t j", t=4, j=4)
            copy(dst[:, places], raw[:].rearrange("p j (m t) -> p m t j", t=4)[:, places])

        def quantize_w1(a):
            nc.vector.quantize_mx(out=w1_codes[a][:].bitcast(FP8X4), scales=w1_sc[a][:], in_=w1_bf[a][:])

        def reorder_pass(dst, src, dtype, line):
            nc.gpsimd.tensor_copy(
                dst.bitcast(dtype).rearrange("p (t m i) -> p m t i", t=4, i=line),
                src.bitcast(dtype).rearrange("p (m i t) -> p m t i", t=4, i=line),
            )

        def first_product(s, acc, u, a, x_words, start, stop):
            x_first = s * HALF
            for t in range(4):
                if u == 0:
                    lhs = w1_codes[a][:, t * P : (t + 1) * P].bitcast(FP8X4)
                    lhs_sc = w1_sc[a][:, t * P : (t + 1) * P]
                elif u == 1:
                    lhs = w2_codes[a][:, t * P : (t + 1) * P].bitcast(FP8X4)
                    lhs_sc = w_sc[1, a][SHIFT:P, t * 32 : (t + 1) * 32].bitcast(U8)
                else:
                    lhs = w3_codes[a][:, t * 64 : (t + 1) * 64].bitcast(U8).bitcast(FP4X4)
                    lhs_sc = w_sc[2, a][:, t * 32 : (t + 1) * 32].bitcast(U8)
                nc.tensor.matmul_mx(
                    out=acc[t][:],
                    lhsT=lhs,
                    lhsT_scale=lhs_sc,
                    rhs=x_words.bitcast(FP8X4),
                    rhs_scale=planes[u][plane_row[u] : P, a, :].bitcast(U8)[:, x_first : x_first + HALF],
                    start=start,
                    stop=stop,
                )

        def squash(acc, th, bias):
            for v in range(2):
                for t in range(4):
                    nc.scalar.activation(
                        th[v][:, t, :],
                        acc[t][:, v * SUB : (v + 1) * SUB],
                        ACT.Tanh,
                        bias=bias[:, t : t + 1],
                    )

        def vector_gain(dst, src):
            gains = gain_cols[:].unsqueeze(1).unsqueeze(3).to_broadcast([P, src.shape[2] // 2, 4, 2])
            nc.vector.tensor_tensor(
                dst.rearrange("p (m i t) -> p m t i", i=2, t=4),
                src.rearrange("p t (m i) -> p m t i", i=2),
                gains,
                ALU.mult,
            )

        def quantize_h(s, cols, src):
            nc.vector.quantize_mx(out=h_codes[s][:, cols].bitcast(FP8X4), scales=h_sc[s][:, cols], in_=src)

        def cast_wo(dst, src, copy):
            copy(dst.rearrange("p (m i t) -> p m t i", i=2, t=4), src.rearrange("p t (m i) -> p m t i", i=2))

        def gpsimd_cast(dst, src):
            nc.gpsimd.tensor_scalar(dst, src, 1.0, 0.0, ALU.mult, ALU.add)

        def quantize_wo(cols, src, codes=None):
            if codes is None:
                codes = held("wo_codes%d" % cols.start, [P, cols.stop - cols.start], U32)
            nc.vector.quantize_mx(out=codes[:].bitcast(FP8X4), scales=wo_sc[:, cols], in_=src)
            for first in range(cols.start, cols.stop, P):
                wo_codes[first // P] = codes[:, first - cols.start : first - cols.start + P]

        def logits(n, parts, banks, on_vector):
            staged = held("staged%d" % n, [P, len(parts), HALF], F32)
            for e, (i, s) in enumerate(parts):
                y = bank(banks[e], "y")
                cols = slice(i * P, (i + 1) * P)
                nc.tensor.matmul_mx(
                    out=y[:],
                    lhsT=wo_codes[i].bitcast(FP8X4),
                    lhsT_scale=wo_sc[:, cols],
                    rhs=h_codes[s].bitcast(FP8X4),
                    rhs_scale=h_sc[s][:],
                    start=True,
                    stop=True,
                )
                if on_vector[e]:
                    nc.vector.tensor_scalar(staged[:, e, :], y[:], consts[:, i : i + 1], None, ALU.add)
                else:
                    nc.scalar.activation(staged[:, e, :], y[:], ACT.Identity, bias=consts[:, i : i + 1])
            (i0, s0), (i1, s1) = parts[0], parts[-1]
            dst = out[i0 * P : (i1 + 1) * P, s0 * HALF : (s1 + 1) * HALF]
            nc.sync.dma_start(
                dst.rearrange("(e p) n -> p e n", p=P), staged[:].rearrange("p (e s) n -> p e (s n)", s=s1 - s0 + 1)
            )

        for u in (0, 2, 1):
            nc.vector.tensor_copy(picked_scales[u][:], table_scales[:].bitcast(U8).indirect(lists[u][:]))
        move_planes(0)
        nc.sync.dma_start(w3_raw[:], w3_words.rearrange("a p b -> p a b").bitcast(I32))
        nc.sync.dma_start(w2_raw[:], w2_words.rearrange("a p c i -> p a (c i)").bitcast(I32))
        load_weight_scales(1, w2_scales)
        load_table(1, slice(0, 1536))
        move_planes(2)
        load_table(1, slice(1536, 3072))
        move_planes(1)
        load_table(1, slice(3072, T))
        nc.sync.dma_start(bh_cols[:], bh.rearrange("(p t) -> p t", t=4))
        nc.sync.dma_start(gain_cols[:], gain.rearrange("(p t) -> p t", t=4))
        load_w1(w1_raw1, 1, slice(0, H))
        for c in range(3):
            load_wo(wo_raw[c], wo_cols[c])
        nc.scalar.activation(rows[0:96, :], w1_raw0[0:96, 0, 0:P], ACT.Tanh, scale=0.0)
        cast_w1(0, w1_raw0, slice(0, P), nc.scalar.copy)
        quantize_w1(0)

        turned = bank(BANKS - 1, "turned")
        nc.tensor.transpose(turned[:, 0:P], rows[:], ident[:])
        consts = held("consts", [P, OUT_TILES], F32)
        nc.scalar.copy(consts[:], turned[:, BO_ROW:P])

        acc0 = [bank(b, "acc") for b in range(4)]
        acc1 = [bank(b, "acc") for b in range(4, BANKS)]
        words0 = held("words0", [P, S], U32)
        for half in halves:
            gather_words(half, 0, 0, words0[:, half])
        for a in range(PASSES):
            reorder_pass(w_sc[2, a][:], w_sc_raw[2][:, a, :], U8, 16)
        for a in range(PASSES):
            reorder_pass(w3_codes[a][:], w3_raw[:, a, :], U16, 8)
            reorder_pass(w2_codes[a][:], w2_raw[:, a, :], I32, 4)
            reorder_pass(w_sc[1, a][:], w_sc_raw[1][:, a, :], U8, 16)
        words12 = held("words12", [P, 2, S], U32)
        first_words = [words0[:], words12[:, 0, :], words12[:, 1, :]]
        early = [(u, s) for u in (0, 2, 1) for s in range(2)]
        for u, s in early[2:]:
            gather_words(halves[s], u, 0, first_words[u][:, halves[s]])
        for u, s in early:
            first_product(s, (acc0, acc1)[s], u, 0, first_words[u][:, halves[s]], u == 0, False)

        second_words = held("second_words", [P, 4, HALF], U32)
        for u in (2, 1, 0):
            gather_words(halves[0], u, 1, second_words[:, u, :])
        gather_words(halves[1], 2, 1, second_words[:, 3, :])
        cast_w1(1, w1_raw1, slice(0, P // 2), nc.scalar.copy)
        cast_w1(1, w1_raw1, slice(P // 2, P), gpsimd_cast)
        quantize_w1(1)
        last_words = held("last_words", [P, 2, HALF], U32, "w1_bf1")
        for e, u in enumerate((1, 0)):
            gather_words(halves[1], u, 1, last_words[:, e, :])
        for u in (2, 1):
            first_product(0, acc0, u, 1, second_words[:, u, :], False, False)
        first_product(1, acc1, 2, 1, second_words[:, 3, :], False, False)
        first_product(0, acc0, 0, 1, second_words[:, 0, :], False, True)
        for e, u in enumerate((1, 0)):
            first_product(1, acc1, u, 1, last_words[:, e, :], False, u == 0)

        wo0_bf = held("wo0_bf", [P, 1024], BF16)
        cast_wo(wo0_bf[:], wo_raw[0][:, :, 0:256], nc.scalar.copy)
        wo1_bf = held("wo1_bf", [P, 2048], BF16)
        for e, src in enumerate((wo_raw[0][:, :, 256:512], wo_raw[1][:])):
            gpsimd_cast(wo1_bf[:, 1024 * e : 1024 * (e + 1)].rearrange("p (m t) -> p m t", t=4), src.rearrange("p t m -> p m t"))
        th0 = [held("th0_%d" % v, [P, 4, SUB], F32, tag) for v, tag in enumerate(("wo_raw0", "th0_1"))]
        th1 = held("th1", [P, 4, HALF], F32)
        squash(acc0, th0, bh_cols)
        for t in range(4):
            nc.scalar.activation(th1[:, t, :], acc1[t][:], ACT.Tanh, bias=bh_cols[:, t : t + 1])

        late = over_table("late", [P, 640], U32, 0)
        h_codes[0] = late[:, 0:HALF]
        h0_bf = [over_table("h0_bf%d" % v, [P, 4 * SUB], BF16, 4096 + 2048 * v) for v in range(2)]
        for v in range(2):
            vector_gain(h0_bf[v][:], th0[v][:])
        nc.vector.quantize_mx(out=late[:, 512:640].bitcast(FP8X4), scales=wo_sc[:, 0:P], in_=wo0_bf[:, 0:512])
        wo_codes[0] = late[:, 512:640]
        for v in range(2):
            quantize_h(0, slice(v * SUB, (v + 1) * SUB), h0_bf[v][:])

        quantize_wo(slice(P, 256), wo0_bf[:, 512:1024], over_table("wo_codes128", [P, P], U32, 6144))
        quantize_wo(slice(256, 768), wo1_bf[:], over_table("wo_codes256", [P, 512], U32, 6144 + 512))

        def second_half():
            vector_gain(h1_bf[:, 0, :], th1[:, :, 0:SUB])
            vector_gain(h1_bf[:, 1, :], th1[:, :, SUB:HALF])
            for v in range(2):
                quantize_h(1, slice(v * SUB, (v + 1) * SUB), h1_bf[:, v, :])


        stores = [[(i, 0)] for i in range(EARLY_TILES)]
        stores.extend([(i, 1)] for i in range(EARLY_TILES))
        for first, last in ((6, 7), (7, 9), (9, 12)):
            stores.append([(i, s) for i in range(first, last) for s in range(2)])
        done = 0
        for n, parts in enumerate(stores):
            turns = range(done, done + len(parts))
            logits(n, parts, [k % BANKS for k in turns], [k >= SCALAR_ONLY and k % 2 == 0 for k in turns])
            done = done + len(parts)
            if n == 0:
                second_half()
            if n == EARLY_TILES - 1:
                wo3_bf = held("wo3_bf", [P, 1024], BF16, "th1")
                wo4_bf = held("wo4_bf", [P, 2048], BF16, "h1_bf")
                cast_wo(wo3_bf[:], wo_raw[2][:, :, 0:256], nc.vector.tensor_copy)
                cast_wo(wo4_bf[:], wo_raw[2][:, :, 256:768], nc.vector.tensor_copy)
                quantize_wo(slice(768, 1024), wo3_bf[:])
                quantize_wo(slice(1024, 1536), wo4_bf[:])
